import numpy as np, ml_dtypes
CORES = [3,7,11,15,131,135,139,143]
N = 8
import mx_ref
BF = ml_dtypes.bfloat16
def entries(a):
    return np.ascontiguousarray(a.T).reshape(-1)
def table(e):
    return np.ascontiguousarray(np.reshape(e, (-1, 16)).T).astype(np.int32)
def pick(q, e):
    c = np.concatenate([q[0].reshape(128, -1, 4), np.zeros((128, 1, 4), np.uint8)], axis=1); s = np.concatenate([q[1], np.ones((16, 1), np.uint8)], axis=1)
    return (np.ascontiguousarray(c[:, e].reshape(128, -1)), np.ascontiguousarray(s[:, e]))
def join(*qs):
    return (np.concatenate([q[0] for q in qs], axis=1), np.concatenate([q[1] for q in qs], axis=1))
def put(q, e, v):
    c, s = q[0].reshape(128, -1, 4).copy(), q[1].copy(); c[:, e] = v[0].reshape(128, -1, 4); s[:, e] = v[1]
    return (c.reshape(128, -1), s)
def pk(c, s):
    return (np.ascontiguousarray(c), mx_ref.live(s))
def emit(q):
    return q[0], q[1]
def decode(q):
    o = []
    for b in range(4):
        e = np.zeros((128, 128, 4), np.float32); e[np.arange(128), np.arange(128), b] = 1
        o.append(mx_ref.matmul(mx_ref.quantize(e.reshape(128, 512).astype(BF)), q))
    return np.stack(o, axis=2).reshape(128, -1)
def f(rng, *shape):
    return mx_ref.flush((rng.standard_normal(shape, dtype=np.float32) * np.exp2(rng.integers(-2, 3, shape[:-1] + (1,)))).astype(BF))
def wide(rng, *shape, cols=0):
    v = rng.standard_normal(shape, dtype=np.float32) * np.exp2(rng.integers(-12, 13, shape)).astype(np.float32)
    if cols: v *= np.repeat(np.exp2(rng.integers(-cols, cols + 1, shape[:-2] + (1, shape[-1] // 4))) * (rng.random(shape[:-2] + (1, shape[-1] // 4)) > 0.0625), 4, axis=-1).astype(np.float32)
    return mx_ref.flush(v.astype(BF))
P, F, R = 128, 16, 2
def big(v):
    v = np.array(v, np.float32)
    v[np.abs(v) < np.float32(2.0 ** -16)] = 0
    return v.astype(BF)
def share(v):
    return big(np.ascontiguousarray(v.reshape(128, N, 4 * P).transpose(1, 0, 2)))
def links(nb):
    return np.concatenate([entries(nb[r]).reshape(P, 3) for r in range(N)])
def graph(rng, ends=False):
    to, far, n = np.zeros((N * P, 3), int), [], P - (N - 1) * F
    for r in range(N):
        a, i = P * r + rng.permutation(P), 0
        while i < P:
            m = min(2 * int(rng.integers(2, 17)), P - i)
            if P - i - m < 4: m = P - i
            for k in range(2):
                c = np.roll(a[i:i + m], -k)
                to[c[0::2], k], to[c[1::2], k] = c[1::2], c[0::2]
            i += m
        if ends:
            h = rng.permutation(a[a < to[a, 0]])[:n]
            e = np.where(rng.random(n) < 0.5, h, to[h, 0])
        else: e = rng.permutation(a)[:n]
        far.append(rng.permutation(np.setdiff1d(a, e)).reshape(N - 1, F))
        for i in range(0, n, 2):
            if e[i + 1] in to[e[i], :2]:
                for j in range(0, n, 2):
                    if j != i and e[j + 1] not in to[e[i], :2] and e[i + 1] not in to[e[j], :2]:
                        e[i + 1], e[j + 1] = e[j + 1], e[i + 1]
                        break
        to[e[0::2], 2], to[e[1::2], 2] = e[1::2], e[0::2]
    for r in range(N):
        for q in range(r + 1, N):
            u, v = far[r][q - 1], far[q][r]
            to[u, 2], to[v, 2] = v, u
    return to
def inputs(rng, x, to):
    return {"x": x, "nb": np.stack([table(to[P * r:P * r + P].reshape(-1)) for r in range(N)]), "w": f(rng, N, 128, 512)}
def setup_inputs(rng):
    return inputs(rng, big(f(rng, N, 128, 4 * P)), graph(rng))
def setup_inputs_far(rng):
    to, n = graph(rng), np.arange(N * P)
    v = (1 + 0.5 * rng.random((128, N * P, 4))) * rng.choice([-1.0, 1.0], (128, N * P, 4))
    a = n[(to[:, 2] // P != n // P) & (n < to[:, 2])]
    b = to[a, 2]
    v[:, b] = np.abs(v[:, b]) * np.sign(v[:, a]) * np.where(rng.random((128, a.size, 4)) < 0.125, -1.0, 1.0)
    return inputs(rng, share(v), to)
def setup_inputs_none(rng):
    to, n, z = graph(rng, ends=True), np.arange(N * P), int(rng.integers(0, N))
    own = n // P == z
    size = np.where(own & (to[:, 2] // P == z), 0.125, 1.0)
    color = np.full(N * P, -1)
    for a in n[n < to[:, 0]]:
        both = np.array([a, to[a, 0]])
        near = color[to[both, 1:]].reshape(-1).tolist()
        color[both] = next(int(c) for c in rng.permutation(5) if c not in near)
    v = rng.choice([-1.0, 1.0], (128, N * P, 4))
    a = n[(to[:, 2] // P != n // P) & (n < to[:, 2])]
    v[:, to[a, 2]] = v[:, a]
    v[:40] = np.where((np.arange(40) // 8)[:, None, None] == color[None, :, None], 8.0, 0.0)
    v[40:48] = 64.0
    v = np.where(own[None, :, None], (1 + 0.5 * rng.random((128, N * P, 4))) * size[None, :, None], 16.0 * v)
    return inputs(rng, share(v), to)
def setup_inputs_spread(rng):
    return inputs(rng, big(wide(rng, N, 128, 4 * P, cols=6)), graph(rng))
def setup_inputs_ties(rng):
    to = graph(rng)
    t = f(rng, 128, 12).astype(np.float32).reshape(128, 3, 4)
    five = np.concatenate([t, 0 - t[:, :1], np.zeros((128, 1, 4), np.float32)], axis=1)
    e = rng.integers(0, 5, N * P)
    for r in range(N):
        j = P * r + int(rng.integers(0, P))
        e[to[j]] = 0
        e[to[to[j]].reshape(-1)] = 0
    return inputs(rng, share(five[:, e]), to)
def setup_inputs_twice(rng):
    to, large = graph(rng), np.zeros(N * P, bool)
    v = np.abs(rng.standard_normal((128, N * P, 4))) * np.exp2(rng.integers(-1, 2, (1, N * P, 1)))
    for i in range(P // 32):
        for r in rng.permutation(N):
            for j in rng.permutation(P):
                n1 = P * r + j
                n2 = to[n1, 1]
                p = np.array([to[n1, 0], n1, n2, to[n2, 0]])
                if i == 0:
                    m = to[[n1, n2], 2]
                    q = np.concatenate([p, m])
                    if large[q].any() or large[to[q]].any() or np.count_nonzero(np.isin(to[q], q)) != 10: continue
                    size = np.concatenate([rng.choice([1.0, 1.25], (128, 4, 4)), rng.choice([3.5, 4.0], (128, 2, 4))], axis=1) * 2.0 ** 26
                    v[:, q] = size * rng.choice([-1.0, 1.0], (128, 1, 4)) * np.array([1.0, 1.0, -1.0, -1.0, -1.0, 1.0])[None, :, None]
                    large[q] = True
                    large[to[m]] = True
                    break
                if large[p].any() or large[to[p]].any() or np.isin(to[p, 2], p).any() or to[p[0], 1] == p[3]: continue
                large[p] = True
                v[:, p] = (1 + 0.5 * rng.random((128, 4, 4))) * np.array([256.0, 64.0, 64.0, 256.0])[None, :, None]
                break
    return inputs(rng, share(v), to)
def check_inputs(d):
    b = []
    for k, low, high in (("x", -16, 28), ("w", -30, 30)):
        v = np.abs(d[k].astype(np.float32))
        if not (np.isfinite(v).all() and ((v == 0) | (v >= 2.0 ** low) & (v <= 2.0 ** high)).all()): b.append("a value of " + k)
    to, n = links(d["nb"]), np.arange(N * P)
    if to.min() < 0 or to.max() >= N * P: return b + ["range of nb"]
    for k in range(3):
        if (to[to[:, k], k] != n).any() or (to[:, k] == n).any(): b.append("edges k = %d are no pairs" % k)
    if (to[:, :2] // P != n[:, None] // P).any(): b.append("an edge k = 0 or 1 leaves its rank")
    if (to[:, 0] == to[:, 1]).any() or (to[:, 0] == to[:, 2]).any() or (to[:, 1] == to[:, 2]).any(): b.append("two edges of a node lead to the same node")
    c = np.zeros((N, N), int)
    np.add.at(c, (n // P, to[:, 2] // P), 1)
    if (c[~np.eye(N, dtype=bool)] != F).any(): b.append("number of edges between two ranks")
    return b
def scores(h, to):
    s = np.zeros((N * P, 3), np.float32)
    for i in range(0, N * P, 128):
        a = pick(h, np.arange(i, i + 128))
        for k in range(3): s[i:i + 128, k] = np.diagonal(mx_ref.matmul(a, pick(h, to[i:i + 128, k]))) + np.float32(0)
    return s
def reference(x, nb, w):
    to, n = links(nb), np.arange(N * P)
    h = join(*[mx_ref.quantize(np.ascontiguousarray(x[r])) for r in range(N)])
    merged, pr = np.zeros((N * P, 3), bool), np.zeros((N, R, P), np.float32)
    for t in range(R):
        s = scores(h, to)
        s[merged] = -np.inf
        c = np.argmax(s, axis=1)
        v = to[n, c]
        met = c[v] == c
        merged[n[met], c[met]] = True
        pr[:, t] = np.where(met, v, -1).reshape(N, P)
        d = decode(h).reshape(128, N * P, 4)
        m = np.float32(0.5) * d + np.float32(0.5) * d[:, np.where(met, v, n)]
        new = mx_ref.quantize(np.ascontiguousarray(m.reshape(128, -1).astype(BF)))
        h = pick(join(h, new), np.where(met, N * P + n, n))
    oc, osc, y = np.zeros((N, 128, 4 * P), np.uint8), np.zeros((N, 16, P), np.uint8), np.zeros((N, 128, P), np.float32)
    for r in range(N):
        own = pick(h, np.arange(P * r, P * r + P))
        oc[r], osc[r] = emit(own)
        y[r] = mx_ref.matmul(mx_ref.quantize(np.ascontiguousarray(w[r])), own)
    return {"oc": oc, "osc": osc, "pr": pr, "y": y}

@@ -1,0 +1,653 @@
+from concourse.bass import DstId, RemoteDMATransfer
+from concourse.mybir import dt, AluOpType as OP, AxisListType, ActivationFunctionType as AF
+
+F32, BF16, I32, U16, U8, C4 = "float32", "bfloat16", "int32", "uint16", "uint8", "float8_e4m3fn_x4"
+SCRATCH = {"pn": ("psum", [128, 2048], F32), "pm": ("psum", [128, 2048], F32)}
+
+
+def _declare(dtype, width, names):
+    for n in names.split():
+        SCRATCH[n] = ("sbuf", [128, width], dtype)
+
+
+_declare(I32, 72, "nl")
+_declare(I32, 16, "icol")
+_declare(I32, 8, "nbt")
+_declare(BF16, 520, "xt wt et")
+_declare(BF16, 128, "sgn wmb wmh smb")
+_declare(BF16, 8, "dmk dsr dt1 dxm")
+_declare(F32, 64, "fcol")
+_declare(F32, 24, "d24")
+_declare(F32, 32, "lf lft pq pqt")
+_declare(F32, 8, "dmb")
+_declare(F32, 128, "mq npf npb n16 k128 wm nmA nmB nm ed zz sm eye zk rk zx rx dx e0 e1 posn yo xm0 xm1 xs0 xs1")
+_declare(F32, 256, "selm npos nsl")
+_declare(F32, 384, "nbp pb")
+_declare(F32, 512, "ks pa")
+_declare(U16, 24, "nlu pl swl cl xsl pol gll dll")
+_declare(C4, 512, "eq")
+_declare(U8, 512, "es")
+_declare(C4, 256, "ll")
+_declare(U8, 256, "lls")
+_declare(U8, 128, "hls")
+_declare(C4, 128, "q0 wq f0 f1 gl l1")
+_declare(U8, 128, "q0s wqs f0s f1s gls l1s")
+for _c in ("p", "v0", "v1", "l", "d"):
+    _declare(BF16, 128, "qz%s qt%s qs%s" % (_c, _c, _c))
+for _t in "01":
+    _declare(C4, 512, "w" + _t)
+    _declare(U8, 512, "ws" + _t)
+    _declare(C4, 256, "g" + _t)
+    _declare(U8, 256, "gs" + _t)
+    _declare(F32, 8, "lt%s cq%s s4m%s pen%s met%s" % (_t, _t, _t, _t, _t))
+    _declare(F32, 32, "mx%s sc%s" % (_t, _t))
+    _declare(F32, 1024, "ex" + _t)
+    _declare(BF16, 1536, "nt" + _t)
+    _declare(U16, 8, "vl" + _t)
+    _declare(F32, 128, "prs%s pro%s" % (_t, _t))
+DMAS = ["d_nbt", "d_nbu", "d_n0", "d_n1", "d_n2", "d_x", "d_w", "d_nbp", "d_pq0", "d_pq1", "d_oc", "d_os0", "d_os1", "d_os2", "d_os3", "d_y", "d_p0", "d_p1"]
+SEMAPHORES = ["cV", "cS", "cT", "cG", "sent", "arr0", "arr1", "thr0", "thr1", "thd", "hop"] + DMAS
+BIG = 1e29
+WAKE, TENS, LOAD, ISSUE, FLIGHT = 200.0, 130.0, 1000.0, 400.0, 3500.0
+HOP, WAY0, WAY1 = 2500.0, 4200.0, 3000.0
+LOOK = 250.0
+WHOLE = 12582912.0
+
+
+def rank_program(g, core, T, topo):
+    N, cores = len(T.cores), T.cores
+    owner, helper = {}, {}
+    for c in cores:
+        for h in topo.cores_of(c):
+            if h not in cores and h not in owner and topo.die(h) == topo.die(c) and all(topo.may_write(h, d) for d in cores):
+                owner[h], helper[c] = c, h
+                break
+    me = owner.get(core, core)
+    r = T.rank_of(me)
+    if r is None:
+        return
+
+    peers = [(d, cores[r ^ d]) for d in range(1, N)]
+    chip = topo.cores_of(core)
+    far = [(d, c) for d, c in peers if c not in chip]
+    near = [(d, c) for d, c in peers if c in chip]
+    lanes = topo.engines(core, far[0][1])
+    spare = 2 * len(far) - len(lanes)
+    others = [e for e in topo.engines(core, near[0][1]) if e not in lanes]
+    inside = others[:2]
+    ways = []
+    for part in range(2):
+        mine = lanes[spare:] + lanes[:spare] if part else lanes
+        way = {d: inside for d, c in near}
+        for k, (d, c) in enumerate(far):
+            way[d] = [mine[k]] if k < spare else [mine[spare + 2 * (k - spare)], mine[spare + 2 * (k - spare) + 1]]
+        ways.append(way)
+    leave = [sum(len(x) for x in w.values()) for w in ways]
+
+    def bits(es):
+        return sum(1 << e for e in es)
+
+    def dest(c):
+        rid, pid = topo.addr(c, core)
+        return DstId(rid=rid, pnc=pid)
+
+    def columns(name, dst, c0, d0, part, sem):
+        tr = []
+        for d, c in peers:
+            a, b = T[name][:, c0 + 16 * d:c0 + 16 * d + 16], T[dst][:, d0 + 16 * d:d0 + 16 * d + 16]
+            if part == 0:
+                a, b = a.bitcast(dt.uint8), b.bitcast(dt.uint8)
+            tr.append(RemoteDMATransfer(dst_ids=[dest(c)], dma_engine_mask=bits(ways[part][d]), remote_sem=T.sem[sem], src=a, dst=b))
+        return tr
+
+    if core != me:
+        g.wait_ge(T.sem.hop, len(others))
+        g.remote_dma_fused(columns("hls", "lls", 0, 128, 1, "arr1"), local_sem=T.sem.sent)
+        g.wait_ge(T.sem.sent, leave[1])
+        return
+
+    queue = {"V": g.vector, "S": g.scalar, "T": g.tensor, "G": g, "Y": g.sync}
+    count = {e: 0 for e in "VSTG"}
+    known = {e: {} for e in "VSTGY"}
+    snap, hist, waited, total = {}, {}, {}, {}
+
+    def v(name, c0=0, c1=None, st=1, p0=0, p1=128):
+        c1 = SCRATCH[name][1][1] if c1 is None else c1
+        ap = T[name][p0:p1, c0:c1] if st == 1 else T[name][p0:p1, c0:c1:st]
+        if SCRATCH[name][0] == "psum":
+            return (ap, name, 0, 128, c0 // 512 * 512, (c1 + 511) // 512 * 512, 1, 128)
+        return (ap, name, p0, p1, c0, c1, st, (c1 - c0 + st - 1) // st)
+
+    def meet(a, b):
+        if a[3] <= b[2] or b[3] <= a[2] or a[5] <= b[4] or b[5] <= a[4]:
+            return False
+        return not (a[6] == b[6] and a[6] > 1 and (a[4] - b[4]) % a[6])
+
+    def need(e, tok):
+        sem, val = tok
+        if known[e].get(sem, 0) < val:
+            queue[e].wait_ge(T.sem[sem], val)
+            waited[sem] = max(waited.get(sem, 0), val)
+            for s, n in list(snap.get(tok, {}).items()) + [(sem, val)]:
+                known[e][s] = max(known[e].get(s, 0), n)
+
+    def order(e, outs, ins):
+        toks = {}
+        for x in ins:
+            psum = SCRATCH[x[1]][0] == "psum"
+            for (y, tok, w, f) in hist.get(x[1], []):
+                if (w or (psum and f != e)) and meet(x, y):
+                    toks[tok[0]] = max(toks.get(tok[0], 0), tok[1])
+        for x in outs:
+            for (y, tok, w, f) in hist.get(x[1], []):
+                if (f != e or e != "T") and meet(x, y):
+                    toks[tok[0]] = max(toks.get(tok[0], 0), tok[1])
+        for s in sorted(toks, key=lambda s: s == "c" + e):
+            need(e, (s, toks[s]))
+
+    def note(e, outs, ins, tok):
+        for x in outs:
+            hist.setdefault(x[1], []).append((x, tok, True, e))
+        for x in ins:
+            hist.setdefault(x[1], []).append((x, tok, False, e))
+
+    ops, seen = [], {}
+
+    def views(xs):
+        return [x for x in xs if isinstance(x, tuple)]
+
+    def add(outs, ins, emit, cost, late=0.0, after=()):
+        e, outs, ins = "".join(cost), views(outs), views(ins)
+        i, deps = len(ops), set(after)
+        for x in ins:
+            psum = SCRATCH[x[1]][0] == "psum"
+            deps.update(j for y, j, w, f in seen.get(x[1], []) if (w or (psum and f != e)) and meet(x, y))
+        for x in outs:
+            deps.update(j for y, j, w, f in seen.get(x[1], []) if meet(x, y))
+        for x in outs:
+            seen.setdefault(x[1], []).append((x, i, True, e))
+        for x in ins:
+            seen.setdefault(x[1], []).append((x, i, False, e))
+        ops.append((emit, cost, late, sorted(deps)))
+        return i
+
+    def run(outs, ins, call, cost):
+        outs, ins = views(outs), views(ins)
+
+        def emit(e):
+            order(e, outs, ins)
+            count[e] += 1
+            tok = ("c" + e, count[e])
+            call(e).then_inc(T.sem[tok[0]], 1)
+            total[tok[0]] = count[e]
+            snap[tok] = dict(known[e])
+            note(e, outs, ins, tok)
+        return add(outs, ins, emit, cost)
+
+    def schedule():
+        n = len(ops)
+        users = [[] for _ in ops]
+        for i, o in enumerate(ops):
+            for j in o[3]:
+                users[j].append(i)
+        way = [0.0] * n
+        for i in range(n - 1, -1, -1):
+            way[i] = min(ops[i][1].values()) + ops[i][2] + max([way[j] + WAKE for j in users[i]] + [0.0])
+        left, end, free = [len(o[3]) for o in ops], [0.0] * n, {}
+        ready = {i: 0.0 for i in range(n) if not left[i]}
+        when = []
+        while ready:
+            best = None
+            for e in "RVSTGY":
+                c = [(s, i) for i, s in ready.items() if e in ops[i][1]]
+                if not c:
+                    continue
+                t = free.get(e, 0.0)
+                if e == "R":
+                    x, t = min(c), 0.0
+                elif e == "G":
+                    x = min(c, key=lambda y: y[1])
+                else:
+                    t0 = max(t, min(c)[0])
+                    x = max([y for y in c if y[0] <= t0 + LOOK], key=lambda y: (way[y[1]] - max(0.0, y[0] - t0), -y[1]))
+                    if x[0] > t0:
+                        fit = [y for y in c if max(t, y[0]) + ops[y[1]][1][e] <= x[0]]
+                        if fit:
+                            x = max(fit, key=lambda y: (way[y[1]], -y[1]))
+                s = max(t, x[0])
+                z = s + ops[x[1]][1][e]
+                if best is None or (s, z) < best[:2]:
+                    best = (s, z, e, x[1])
+            s, z, e, i = best
+            end[i] = z + ops[i][2]
+            free[e] = z
+            when.append((s, len(when), e, i))
+            del ready[i]
+            for j in users[i]:
+                left[j] -= 1
+                if not left[j]:
+                    ready[j] = max(end[m] for m in ops[j][3]) + WAKE
+        for s, k, e, i in when:
+            if e != "R":
+                ops[i][0](e)
+
+    def val(x):
+        return x[0] if isinstance(x, tuple) else x
+
+    def dma(e, sem, *moves):
+        outs, ins = views([x for x, y in moves]), views([y for x, y in moves])
+
+        def emit(e):
+            for out, in_ in moves:
+                order(e, views([out]), views([in_]))
+                queue[e].dma_start(val(out), val(in_)).then_inc(T.sem[sem], 16)
+            total[sem] = 16 * len(moves)
+            snap[(sem, total[sem])] = dict(known[e])
+            note("D" + sem, outs, ins, (sem, total[sem]))
+        add(outs, ins, emit, {e: 60.0 * len(moves)}, LOAD)
+
+    def vec(x, a=1.0):
+        return max(64, a * x[7] * (0.5 if SCRATCH[x[1]][2] == BF16 else 1)) * 0.83
+
+    def ts(out, a, s1, op0, s2=None, op1=None):
+        if op1 is None:
+            run([out], [a, s1], lambda e: g.vector.tensor_scalar(out[0], a[0], val(s1), None, op0), {"V": vec(a)})
+        else:
+            run([out], [a, s1, s2], lambda e: g.vector.tensor_scalar(out[0], a[0], val(s1), val(s2), op0, op1), {"V": vec(a)})
+
+    def tt(out, a, b, op):
+        run([out], [a, b], lambda e: g.vector.tensor_tensor(out[0], a[0], b[0], op), {"V": vec(a, 1 if a[1] in ("pn", "pm") else 2)})
+
+    def act(out, a, func, scale=1.0, bias=0.0, acc=None):
+        if acc is None:
+            run([out], [a, bias, scale], lambda e: g.scalar.activation(out[0], a[0], func, bias=val(bias), scale=val(scale)), {"S": vec(a)})
+        else:
+            run([out, acc], [a, bias], lambda e: g.scalar.activation(out[0], a[0], func, bias=val(bias), scale=scale, accum_out=acc[0]), {"S": vec(a) + 20})
+
+    def cp(out, a, es="V"):
+        def call(e):
+            if e == "V":
+                return g.vector.tensor_copy(out[0], a[0])
+            return g.scalar.activation(out[0], a[0], AF.Copy)
+        run([out], [a], call, {e: vec(a) for e in es})
+
+    def fill(out, c):
+        run([out], [], lambda e: g.vector.memset(out[0], c), {"V": vec(out)})
+
+    def red(out, a, op, ab=False):
+        run([out], [a], lambda e: g.vector.tensor_reduce(out[0], a[0], AxisListType.X, op, apply_absolute_value=ab), {"V": vec(a)})
+
+    def turn(out, a):
+        run([out], [a], lambda e: g.vector.transpose(out[0], a[0]), {"V": vec(a)})
+
+    def scan(z, q, op=OP.add):
+        s = v("smb" if SCRATCH[q[1]][2] == BF16 else "sm")
+        run([z], [q, s], lambda e: g.vector.tensor_tensor_scan(z[0], s[0], q[0], 0.0, OP.mult, op), {"V": vec(q)})
+
+    def quant(q, s, a):
+        run([q, s], [a], lambda e: g.vector.quantize_mx(q[0], s[0], a[0]), {"V": 12 + 0.22 * a[7]})
+
+    def mm(out, a, asc, b, bsc, start=True, stop=True):
+        run([out], [a, asc, b, bsc], lambda e: g.tensor.matmul_mx(out[0], a[0], asc[0], b[0], bsc[0], start, stop), {"T": TENS})
+
+    def by_list(out):
+        return 60 + 1.25 * out[7]
+
+    def gather(out, win, off, es="S", func=AF.Copy, scale=1.0, bias=0.0):
+        def call(e):
+            if e == "V":
+                return g.vector.tensor_copy(out[0], win[0].indirect(off[0]))
+            if func == AF.Copy:
+                return g.scalar.activation(out[0], win[0].indirect(off[0]), AF.Copy)
+            return g.scalar.activation(out[0], win[0].indirect(off[0]), func, bias=bias, scale=scale)
+        run([out], [win, off], call, {e: by_list(out) for e in es})
+
+    def choose(out, win, off, m):
+        run([out], [win, off, m], lambda e: g.vector.tensor_tensor(out[0], win[0].indirect(off[0]), m[0], OP.mult), {"V": by_list(out)})
+
+    def pick(oq, os, oa, ob, iq, isc, ia, ib, off):
+        o, w = v(oq, oa, ob), v(iq, ia, ib)
+        i = run([o], [w, off], lambda e: g.vector.tensor_copy(o[0].bitcast(dt.uint32), w[0].bitcast(dt.uint32).indirect(off[0])), {"V": by_list(o)})
+        gather(v(os, oa, ob), v(isc, ia, ib), off)
+        return i
+
+    def iota(out, pattern, base, cm, flag=True):
+        run([out], [], lambda e: g.iota(out[0], pattern, base, cm, allow_small_or_imprecise_dtypes=True) if flag else g.iota(out[0], pattern, base, cm),
+            {"G": 130 + 1.66 * out[7]})
+
+    def quarters(name, c0, st):
+        for d in range(4):
+            a = d ^ 1
+            cp(v(name, 32 * a + c0, 32 * a + 32, st, 32 * d, 32 * d + 32), v(name, 32 * a + c0, 32 * a + 32, st, 32 * a, 32 * a + 32), "VS")
+        cp(v(name, 64 + c0, 128, st, 0, 64), v(name, 64 + c0, 128, st, 64, 128), "VS")
+        cp(v(name, c0, 64, st, 64, 128), v(name, c0, 64, st, 0, 64), "VS")
+
+    def wrap(tag, col):
+        ts(v("qz" + tag), v("wmh"), col, OP.mult)
+        turn(v("qt" + tag), v("qz" + tag))
+        scan(v("qs" + tag), v("qt" + tag))
+        quarters("qs" + tag, 15, 16)
+        return v("qs" + tag, 15, 128, 16)
+
+    def wrap_sum(tag, a, b, out):
+        ts(v("qz" + tag), v("wmb"), a, OP.add, b, OP.add)
+        turn(v("qt" + tag), v("qz" + tag))
+        scan(v("qs" + tag), v("qt" + tag), OP.max)
+        quarters("qs" + tag, 15, 16)
+        ts(out, v("qs" + tag, 15, 128, 16), 128, OP.mult, fc(17), OP.add)
+
+    def ic(k):
+        return v("icol", k, k + 1)
+
+    def fc(k):
+        return v("fcol", k, k + 1)
+
+    classes = ((2, 0, 5), (1, 5, 5), (0, 10, 6))
+    part = [(v("nbt", 2 - (2 - i) % 3, 5 - (2 - i) % 3, 1, 8 * s, 8 * (s + n)), T.nb[i:16:3, :]) for i, s, n in classes]
+    dma("S", "d_nbu", part[0])
+    dma("Y", "d_nbt", *part[1:])
+    dma("S", "d_x", (v("xt", 0, 512), T.x[:, :]))
+    for k, by in ((0, 6), (1, 11), (2, 0)):
+        moves = []
+        for h in range(2):
+            for i, s, n in classes:
+                p, c = 16 * h + (s + by) % 16, (k - i) % 3
+                moves.append((v("nl", 24 * k, 24 * k + 22, 1, p, p + n), T.nb[i:16:3, c:c + 22]))
+        dma("Y", "d_n%d" % k, *moves)
+    dma("Y", "d_w", (v("wt", 0, 512), T.w[:, :]))
+
+    iota(ic(0), [[0, 1]], 0, 1, False)
+    iota(v("npf"), [[1, 128]], 0, -1)
+    iota(v("k128"), [[0, 128]], 128, 0)
+    iota(v("n16"), [[0, 8], [1, 16]], 0, 0)
+    iota(fc(0), [[0, 1]], 0, 1)
+    iota(v("d24"), [[1, 24]], 0, 0)
+    iota(fc(6), [[0, 1]], -64, 256)
+    iota(v("lf"), [[0, 32]], 0, 0)
+    iota(v("ks"), [[1, 4], [0, 128]], 0, 0)
+    iota(v("nbp"), [[0, 384]], 0, 0)
+    iota(v("pa", 0, 128), [[0, 128]], -1, 0)
+    iota(v("pb", 0, 128), [[0, 128]], -1, 0)
+    fill(v("zz"), 0.0)
+    fill(v("et"), 0.0)
+    fill(v("mq"), -BIG)
+    ts(ic(1), ic(0), 3, OP.arith_shift_right)
+    ts(ic(2), ic(0), 7, OP.bitwise_and)
+    ts(ic(3), ic(0), 15, OP.bitwise_and)
+    cp(fc(1), ic(1))
+    cp(fc(2), ic(3))
+    ts(fc(3), ic(2), 16, OP.mult, fc(1), OP.add)
+    ts(fc(7), fc(2), 8, OP.mult)
+    ts(fc(4), fc(3), 128 * r, OP.add)
+    ts(fc(5), fc(3), 128 * 127 - 64, OP.add)
+    act(v("npb"), v("npf"), AF.Abs)
+    act(v("eye"), v("npb"), AF.Relu, -1.0, 1.0)
+    act(v("et", 4, 516, 4), v("eye"), AF.Copy, 0.5)
+    for b in range(4):
+        quant(v("eq", 128 * b, 128 * b + 128), v("es", 128 * b, 128 * b + 128), v("et", 4 - b, 516 - b))
+    act(v("sm"), v("n16"), AF.Sign)
+    ts(v("wm"), v("n16"), fc(2), OP.is_equal)
+    ts(v("wmb"), v("n16"), fc(2), OP.is_equal, 4, OP.mult)
+    ts(v("wmh"), v("n16"), fc(2), OP.is_equal)
+    cp(v("smb"), v("sm"), "S")
+    ts(ic(5), ic(0), 4, OP.arith_shift_right)
+    cp(fc(14), ic(5))
+    ts(fc(15), fc(14), 0.125, OP.mult)
+    ts(fc(16), fc(14), 0, OP.is_equal, fc(15), OP.add)
+    ts(fc(17), fc(2), -512, OP.add)
+    fill(v("pq", 0, 32, 1, 0, 32), 0.0)
+
+    ts(fc(9), v("nbt", 2, 3), 0.5, OP.add, fc(4), OP.min)
+    turned = [(k, bit, sign) for k, bit, sign in ((8, 128 * r, -8), (9, 896 - 128 * r, 8)) if bit]
+    for k, bit, sign in turned:
+        ts(ic(k), v("nbt", 2, 3), bit, OP.bitwise_and)
+    k, bit, sign = turned[0]
+    ts(fc(28), ic(k), sign, OP.mult)
+    rest = fc(9)
+    for k, bit, sign in turned[1:]:
+        ts(fc(29), ic(k), sign, OP.mult, rest, OP.add)
+        rest = fc(29)
+    ts(v("zk"), v("zz"), fc(28), OP.add, rest, OP.add)
+    key = fc(10)
+    tt(key, fc(28), rest, OP.add)
+    turn(v("rk"), v("zk"))
+    quarters("rk", 0, 1)
+    act(v("sgn"), v("rk"), AF.Sign, -1.0, key, fc(11))
+    ts(v("cl", 0, 8), v("d24", 0, 8), fc(7), OP.add)
+    quant(v("q0"), v("q0s"), v("xt", 0, 512))
+    ts(v("zx"), v("k128"), fc(11), OP.mult, fc(5), OP.add)
+    turn(v("rx"), v("zx"))
+    quarters("rx", 0, 1)
+    ts(v("dx"), v("rx"), fc(6), OP.subtract)
+    red(fc(12), v("dx"), OP.min, True)
+    gather(v("posn"), v("rx"), v("cl", 0, 8), "S", AF.Identity, 1.0 / 256, WHOLE)
+    wp = wrap("p", fc(12))
+    cp(v("pl", 0, 8), wp)
+    pick("w0", "ws0", 0, 128, "q0", "q0s", 0, 128, v("pl", 0, 8))
+
+    def post(src, tr, leave, land, flight):
+        def emit(e):
+            order("G", [], [src])
+            g.remote_dma_fused(tr, local_sem=T.sem.sent)
+            total["sent"] = total.get("sent", 0) + leave
+        i = add([], [src], emit, {"G": ISSUE})
+        add([land], [], None, {"R": 0.0}, flight, (i,))
+
+    def send(part):
+        name, dst = (("w0", "ll"), ("ws0", "lls"))[part]
+        post(v(name, 0, 128), columns(name, dst, 0, 0, part, "arr0"), leave[part], v(dst, 16, 128), FLIGHT)
+
+    def send_merged(part):
+        if part == 0:
+            post(v("w0", 256, 384), columns("w0", "ll", 256, 128, 0, "arr1"), leave[0], v("ll", 144, 256), FLIGHT)
+        else:
+            tr = [RemoteDMATransfer(dst_ids=[dest(helper[core])], dma_engine_mask=bits(others), remote_sem=T.sem.hop,
+                                    src=T.ws0[:, 272:384], dst=T.hls[:, 16:128])]
+            post(v("ws0", 272, 384), tr, len(others), v("lls", 144, 256), FLIGHT + HOP)
+
+    def send_col(name, c0, dst, sem, flight):
+        tr = []
+        for who, es in ((far, lanes), (near, inside)):
+            tr.append(RemoteDMATransfer(dst_ids=[dest(c) for d, c in who], dma_engine_mask=bits(es), remote_sem=T.sem[sem],
+                                        srcs=[T[name][:, c0:c0 + 1]], dsts=[T[dst][:, d:d + 1] for d, c in who]))
+        post(v(name, c0, c0 + 1), tr, len(lanes) + len(inside), v(dst, 1, 8), flight)
+
+    few = len(far) * len(lanes) + len(near) * len(inside)
+    for t in range(2):
+        total["arr%d" % t] = sum(leave)
+        note("R", [v("ll", 128 * t + 16, 128 * t + 128), v("lls", 128 * t + 16, 128 * t + 128)], [], ("arr%d" % t, total["arr%d" % t]))
+    for sem, dst in (("thr0", "lt0"), ("thr1", "lt1"), ("thd", "dt1")):
+        total[sem] = few
+        note("R", [v(dst, 1, 8)], [], (sem, few))
+
+    def bank(k):
+        return v("pm", 512 * k, 512 * k + 128)
+
+    def scores(t, jobs):
+        for k, b, m, col in jobs:
+            x, out = v("ex" + t, 128 * k, 128 * k + 128), v("sc" + t, col, col + 1)
+            tt(x, bank(b), v(m), OP.mult)
+            if t == "0":
+                act(x, x, AF.Copy, acc=out)
+            else:
+                act(x, x, AF.Identity, bias=v("pen1", col, col + 1), acc=out)
+
+    def halves(t, k, part):
+        if part == 0:
+            m, s = v("w" + t, 0, 128), v("ws" + t, 0, 128)
+        elif k == 2:
+            m, s = (v("l1"), v("l1s")) if t == "1" else (v("ll", 0, 128), v("lls", 0, 128))
+        elif t == "0":
+            m, s = v("gl"), v("gls")
+        else:
+            m, s = v("g1", 128 * k, 128 * k + 128), v("gs1", 128 * k, 128 * k + 128)
+        for b in range(4):
+            mm(v("pn", 512 * b, 512 * b + 128), v("eq", 128 * b, 128 * b + 128), v("es", 128 * b, 128 * b + 128), m, s, part == 0, part == 1)
+
+    def drain(t, k):
+        for b in range(4):
+            cp(v("nt" + t, 512 * k + b, 512 * k + 512, 4), v("pn", 512 * b, 512 * b + 128), "VS")
+
+    def requant(t, k):
+        a = (256, 384, 128)[k]
+        quant(v("w" + t, a, a + 128), v("ws" + t, a, a + 128), v("nt" + t, 512 * k, 512 * k + 512))
+
+    for t in "01":
+        W, WS, G, GS, sc, met = "w" + t, "ws" + t, "g" + t, "gs" + t, "sc" + t, "met" + t
+        L, LS = ("ll", "lls") if t == "0" else ("l1", "l1s")
+
+        def s_(a):
+            return v(sc, a, a + 1)
+
+        def m_(a):
+            return v(met, a, a + 1)
+
+        mb, mx = 32 * int(t), "mx" + t
+        best = v("mq", mb, mb + 1)
+        if t == "0":
+            send(0)
+            send(1)
+        mm(bank(0), v(W, 0, 128), v(WS, 0, 128), v(W, 0, 128), v(WS, 0, 128))
+        if t == "0":
+            ts(v("lf", 0, 24, 1, 0, 32), v("nl", 0, 72, 3, 0, 32), 0, OP.add)
+            cp(v("lf", 0, 16, 1, 32, 64), v("lf", 0, 16, 1, 0, 32), "S")
+            cp(v("lf", 0, 16, 1, 64, 128), v("lf", 0, 16, 1, 0, 64), "S")
+            ts(v("nlu", 0, 16), v("lf", 0, 16), -128 * r, OP.add)
+            gather(v("npos"), v("posn"), v("nlu", 0, 16), "S", AF.Identity, 1.0, -WHOLE)
+            ts(v("pl", 8, 16), wp, 128, OP.add)
+            gather(v("nsl"), v("npos"), v("pl", 0, 16))
+            for k in range(2):
+                ts(v("e%d" % k), v("nsl", 128 * k, 128 * k + 128), fc(0), OP.is_equal)
+            for k in range(2):
+                choose(v("xm%d" % k), v("npos", 128 * k, 128 * k + 128), v("pl", 0, 8), v("wm"))
+            for k in range(2):
+                scan(v("xs%d" % k), v("xm%d" % k))
+            for k in range(2):
+                cp(v("xsl", 8 * k, 8 * k + 8), v("xs%d" % k, 15, 128, 16))
+            ts(ic(4), ic(0), 1, OP.bitwise_and)
+            ts(fc(13), ic(4), -2, OP.mult, fc(2), OP.add)
+            ts(v("swl", 0, 1), fc(13), 1, OP.add)
+            ts(v("dmb"), v("d24", 0, 8), fc(14), OP.not_equal, BIG, OP.mult)
+            ts(v("dmk"), v("d24", 0, 8), fc(14), OP.is_equal)
+            scores(t, [(0, 0, "e0", 0), (1, 0, "e1", 1)])
+            tt(best, s_(0), s_(1), OP.max)
+            tt(v("ed"), v("e1"), v("e0"), OP.subtract)
+        else:
+            ts(v("pen1", 0, 2), v("met0", 0, 2), -BIG / 128, OP.mult)
+            ts(v("pen1", 4, 5), v("met0", 2, 3), -BIG / 128, OP.mult)
+            ts(fc(30), v("dsr", 0, 1), -BIG / 2, OP.mult, BIG, OP.add)
+            ts(fc(31), v("met0", 0, 1), v("met0", 1, 2), OP.subtract, BIG / 2, OP.mult)
+            act(v("nmA"), v("ed"), AF.Abs, fc(30), fc(31))
+            act(v("nm"), v("nmA"), AF.Identity, 1.0, -BIG)
+            tt(v("nmB"), bank(0), v("nm"), OP.add)
+            red(best, v("nmB"), OP.max)
+        send_col("mq", mb, "lt" + t, "thr" + t, (WAY0, WAY1)[int(t)])
+        if t == "0":
+            pick(G, GS, 0, 256, W, WS, 0, 128, v("xsl", 0, 16))
+            ts(fc(19), s_(1), s_(0), OP.is_gt)
+            wrap_sum("l", fc(19), fc(15), v("gll", 0, 8))
+            pick("gl", "gls", 0, 128, G, GS, 0, 256, v("gll", 0, 8))
+        else:
+            scores(t, [(0, 0, "e0", 0), (1, 0, "e1", 1)])
+            pick(G, GS, 0, 128, W, WS, 0, 128, v("xsl", 0, 8))
+            pick(G, GS, 128, 256, W, WS, 0, 128, v("xsl", 8, 16))
+        halves(t, 0, 0)
+        halves(t, 0, 1)
+        pick("ll", "lls", 128 * int(t), 128 * int(t) + 16, W, WS, 0, 128, v("swl", 0, 1))
+        mm(bank(2), v(G, 0, 128), v(GS, 0, 128), v(G, 128, 256), v(GS, 128, 256))
+        mm(bank(3), v(G, 128, 256), v(GS, 128, 256), v(G, 0, 128), v(GS, 0, 128))
+        if t == "1":
+            for k in range(2):
+                x = v("selm", 128 * k, 128 * k + 128)
+                choose(x, v("ks"), v("vl0"), v("e%d" % k))
+                act(x, x, AF.Copy, acc=fc(20 + k))
+            ts(fc(22), v("sc0", 2, 3), v("sc0", 0, 1), OP.is_gt, -BIG / 128, OP.mult)
+            ts(fc(23), v("sc0", 3, 4), v("sc0", 1, 2), OP.is_ge, -BIG / 128, OP.mult)
+            ts(v("pen1", 2, 3), fc(20), 2, OP.is_equal, fc(22), OP.mult)
+            ts(v("pen1", 3, 4), fc(21), 2, OP.is_equal, fc(23), OP.mult)
+            ts(v("pen1", 5, 7), v("fcol", 20, 22), 1, OP.is_equal, -BIG / 128, OP.mult)
+        drain(t, 0)
+        if t == "1":
+            halves(t, 1, 0)
+            halves(t, 1, 1)
+        scores(t, [(2, 2, "e0", 2), (3, 3, "e1", 3)])
+        requant(t, 0)
+        if t == "0":
+            send_merged(1)
+            send_merged(0)
+        turn(v(mx, 0, 32, 1, 0, 32), v("mq", mb, mb + 32, 1, 0, 32))
+        cp(v("mq", 64, 80, 2, 0, 32), v(mx, 1, 16, 2, 0, 32), "VS")
+        cp(v("mq", 65, 80, 2, 0, 32), v(mx, 0, 16, 2, 0, 32), "VS")
+        turn(v("mq", 96, 128, 1, 0, 32), v("mq", 64, 96, 1, 0, 32))
+        ts(s_(10), s_(1), s_(2), OP.max, s_(0), OP.is_gt)
+        ts(s_(11), s_(0), s_(3), OP.max, s_(1), OP.is_ge)
+        tt(s_(7), v("mq", 96, 97), best, OP.max)
+        ts(s_(12), s_(10), -9 * BIG, OP.mult, s_(0), OP.add)
+        ts(s_(13), s_(11), -9 * BIG, OP.mult, s_(1), OP.add)
+        if t == "1":
+            drain(t, 1)
+            requant(t, 1)
+        halves(t, 2, 0)
+        if t == "0":
+            turn(v("lft", 0, 32, 1, 0, 32), v("lf", 0, 32, 1, 0, 32))
+            dma("Y", "d_nbp", (v("nbp", 0, 384, 1, 0, 1), v("lft", 0, 16, 1, 0, 24)))
+        else:
+            ts(v("pl", 16, 24), wp, 256, OP.add)
+            for k in range(2):
+                dma("Y", "d_pq%d" % k, (v("pq", 16 * k, 16 * k + 16, 1, 0, 8), v("posn", 0, 128, 1, 0, 1)))
+            turn(v("pqt", 0, 32, 1, 0, 32), v("pq", 0, 32, 1, 0, 32))
+            cp(v("pqt", 0, 8, 1, 32, 64), v("pqt", 0, 8, 1, 0, 32), "S")
+            cp(v("pqt", 0, 8, 1, 64, 128), v("pqt", 0, 8, 1, 0, 64), "S")
+            gather(v("pa", 128, 256), v("nbp"), v("pl", 16, 24), "VS")
+            gather(v("pa", 256, 512), v("nbp"), v("pl", 0, 16), "VS")
+            cp(v("pb", 128, 256), v("pa", 128, 256), "VS")
+            gather(v("pb", 256, 384), v("pa", 256, 512), v("gll", 0, 8), "VS")
+            ts(v("pol", 0, 8), v("pqt", 0, 8), -WHOLE, OP.add)
+            quant(v("wq"), v("wqs"), v("wt", 0, 512))
+            gather(v("prs0"), v("pb"), v("vl0"), "VS")
+            gather(v("pro0"), v("prs0"), v("pol", 0, 8), "VS")
+            dma("Y", "d_p0", (T.pr[0:1, :], v("pro0", 0, 128, 1, 0, 1)))
+            tt(v("dxm", 1, 8), v("dt1", 1, 8), v("dmk", 1, 8), OP.mult)
+            red(fc(24), v("dxm", 1, 8), OP.max)
+            wrap_sum("d", fc(24), fc(16), v("dll", 0, 8))
+            pick("l1", "l1s", 0, 128, "ll", "lls", 0, 256, v("dll", 0, 8))
+        l, ls = v(L, 0, 128), v(LS, 0, 128)
+        mm(bank(0), v(W, 0, 128), v(WS, 0, 128), l, ls)
+        mm(bank(1), v(G, 0, 128), v(GS, 0, 128), l, ls)
+        mm(bank(2), v(G, 128, 256), v(GS, 128, 256), l, ls)
+        halves(t, 2, 1)
+        scores(t, [(4, 0, "eye", 4), (5, 1, "e0", 5), (6, 2, "e1", 6)])
+        ts(v("s4m" + t, 1, 8), v("dmb", 1, 8), s_(4), OP.add)
+        ts(v("cq" + t, 0, 1), s_(7), s_(4), OP.is_lt)
+        ts(m_(0), s_(5), s_(4), OP.max, s_(12), OP.is_le)
+        ts(m_(1), s_(6), s_(4), OP.max, s_(13), OP.is_le)
+        if t == "0":
+            tt(v("dsr", 0, 1), m_(0), m_(1), OP.max)
+            send_col("dsr", 0, "dt1", "thd", HOP)
+        ts(s_(15), m_(0), 2, OP.mult, fc(15), OP.add)
+        ts(s_(16), m_(1), 2 + int(t), OP.mult, s_(15), OP.add)
+        drain(t, 2)
+        tt(v("cq" + t, 1, 8), v("lt" + t, 1, 8), v("s4m" + t, 1, 8), OP.is_lt)
+        red(m_(2), v("cq" + t), OP.min)
+        requant(t, 2)
+        wrap_sum("v" + t, m_(2), s_(16), v("vl" + t))
+        if t == "0":
+            pick("w1", "ws1", 0, 128, W, WS, 0, 384, v("vl0"))
+
+    pick("f0", "f0s", 0, 128, "w1", "ws1", 0, 512, v("vl1"))
+    last = pick("f1", "f1s", 0, 128, "f0", "f0s", 0, 128, v("pol", 0, 8))
+    mm(bank(3), v("wq"), v("wqs"), v("f1"), v("f1s"))
+    f1 = v("f1")
+    dma("Y", "d_oc", (T.oc[:, :], (T.f1[:, :].bitcast(dt.uint8),) + f1[1:]))
+    gather(v("prs1"), v("pa"), v("vl1"), "VS")
+    ops[-1][3].append(last)
+    gather(v("pro1"), v("prs1"), v("pol", 0, 8), "VS")
+    cp(v("yo"), bank(3), "VS")
+    for k in range(4):
+        dma("Y", "d_os%d" % k, (T.osc[4 * k:4 * k + 4, :], v("f1s", 0, 128, 1, 32 * k, 32 * k + 4)))
+    dma("S", "d_y", (T.y[:, :], v("yo")))
+    dma("Y", "d_p1", (T.pr[1:2, :], v("pro1", 0, 128, 1, 0, 1)))
+    schedule()
+    for sem, n in total.items():
+        if waited.get(sem, 0) < n:
+            (g if sem == "sent" else g.sync).wait_ge(T.sem[sem], n)

@@ -11,47 +11,48 @@ def _declare(dtype, width, names):
 
 
 _declare(I32, 72, "nl")
-_declare(I32, 16, "icol")
-_declare(I32, 8, "nbt")
+_declare(I32, 24, "icol km")
 _declare(BF16, 520, "xt wt et")
-_declare(BF16, 128, "sgn wmb wmh smb")
+_declare(BF16, 1024, "sgn")
+_declare(BF16, 128, "wmb wmh smb inv invm invs")
 _declare(BF16, 8, "dmk dsr dt1 dxm")
-_declare(F32, 64, "fcol")
-_declare(F32, 24, "d24")
-_declare(F32, 32, "lf lft pq pqt")
-_declare(F32, 8, "dmb")
-_declare(F32, 128, "mq npf npb n16 k128 wm nmA nmB nm ed zz sm eye zk rk zx rx dx e0 e1 posn yo xm0 xm1 xs0 xs1")
-_declare(F32, 256, "selm npos nsl")
+_declare(F32, 80, "fcol kf")
+_declare(F32, 32, "lf lft")
+_declare(F32, 128, "mq npf npb n16 wm nmA nmB nm ed zz sm eye rk zx rx frr e0 e1 posn yo xm0 xm1 xs0 xs1 fm fs")
+_declare(F32, 256, "selm npos nsl kb")
 _declare(F32, 384, "nbp pb")
-_declare(F32, 512, "ks pa")
-_declare(U16, 24, "nlu pl swl cl xsl pol gll dll")
+_declare(F32, 512, "ks pa ya")
+_declare(F32, 2048, "kt")
+_declare(U16, 24, "nlu pl swl cl xsl pol gll dll gol")
 _declare(C4, 512, "eq")
 _declare(U8, 512, "es")
 _declare(C4, 256, "ll")
 _declare(U8, 256, "lls")
 _declare(U8, 128, "hls")
-_declare(C4, 128, "q0 wq f0 f1 gl l1")
-_declare(U8, 128, "q0s wqs f0s f1s gls l1s")
-for _c in ("p", "v0", "v1", "l", "d"):
+_declare(C4, 128, "q0 wq f1 gl l1")
+_declare(U8, 128, "q0s wqs f1s gls l1s")
+for _c in ("v0", "l", "d"):
     _declare(BF16, 128, "qz%s qt%s qs%s" % (_c, _c, _c))
 for _t in "01":
     _declare(C4, 512, "w" + _t)
     _declare(U8, 512, "ws" + _t)
     _declare(C4, 256, "g" + _t)
     _declare(U8, 256, "gs" + _t)
-    _declare(F32, 8, "lt%s cq%s s4m%s pen%s met%s" % (_t, _t, _t, _t, _t))
+    _declare(F32, 8, "pen%s met%s" % (_t, _t))
+    _declare(F32, 16, "lt" + _t)
     _declare(F32, 32, "mx%s sc%s" % (_t, _t))
     _declare(F32, 1024, "ex" + _t)
     _declare(BF16, 1536, "nt" + _t)
     _declare(U16, 8, "vl" + _t)
-    _declare(F32, 128, "prs%s pro%s" % (_t, _t))
-DMAS = ["d_nbt", "d_nbu", "d_n0", "d_n1", "d_n2", "d_x", "d_w", "d_nbp", "d_pq0", "d_pq1", "d_oc", "d_os0", "d_os1", "d_os2", "d_os3", "d_y", "d_p0", "d_p1"]
+    _declare(F32, 128, "pro" + _t)
+_declare(F32, 128, "prs0")
+_declare(F32, 16, "cq0")
+DMAS = ["d_n0", "d_n1", "d_n2", "d_n3", "d_x", "d_w", "d_nbp", "d_oc", "d_os0", "d_os1", "d_os2", "d_os3", "d_y", "d_p0", "d_p1"]
 SEMAPHORES = ["cV", "cS", "cT", "cG", "sent", "arr0", "arr1", "thr0", "thr1", "thd", "hop"] + DMAS
 BIG = 1e29
 WAKE, TENS, LOAD, ISSUE, FLIGHT = 200.0, 130.0, 1000.0, 400.0, 3500.0
 HOP, WAY0, WAY1 = 2500.0, 4200.0, 3000.0
 LOOK = 250.0
-WHOLE = 12582912.0
 
 
 def rank_program(g, core, T, topo):
@@ -115,7 +116,7 @@ def rank_program(g, core, T, topo):
         c1 = SCRATCH[name][1][1] if c1 is None else c1
         ap = T[name][p0:p1, c0:c1] if st == 1 else T[name][p0:p1, c0:c1:st]
         if SCRATCH[name][0] == "psum":
-            return (ap, name, 0, 128, c0 // 512 * 512, (c1 + 511) // 512 * 512, 1, 128)
+            return (ap, name, 0, 128, c0 // 512 * 512, (c1 + 511) // 512 * 512, 1, c1 - c0)
         return (ap, name, p0, p1, c0, c1, st, (c1 - c0 + st - 1) // st)
 
     def meet(a, b):
@@ -271,11 +272,18 @@ def rank_program(g, core, T, topo):
             return g.scalar.activation(out[0], a[0], AF.Copy)
         run([out], [a], call, {e: vec(a) for e in es})
 
+    def shift(out, a, c):
+        def call(e):
+            if e == "V":
+                return g.vector.tensor_scalar(out[0], a[0], c, None, OP.add)
+            return g.scalar.activation(out[0], a[0], AF.Identity, bias=c)
+        run([out], [a], call, {e: vec(a) for e in "VS"})
+
     def fill(out, c):
         run([out], [], lambda e: g.vector.memset(out[0], c), {"V": vec(out)})
 
-    def red(out, a, op, ab=False):
-        run([out], [a], lambda e: g.vector.tensor_reduce(out[0], a[0], AxisListType.X, op, apply_absolute_value=ab), {"V": vec(a)})
+    def red(out, a, op):
+        run([out], [a], lambda e: g.vector.tensor_reduce(out[0], a[0], AxisListType.X, op), {"V": max(64, a[7]) * 0.83})
 
     def turn(out, a):
         run([out], [a], lambda e: g.vector.transpose(out[0], a[0]), {"V": vec(a)})
@@ -288,28 +296,32 @@ def rank_program(g, core, T, topo):
         run([q, s], [a], lambda e: g.vector.quantize_mx(q[0], s[0], a[0]), {"V": 12 + 0.22 * a[7]})
 
     def mm(out, a, asc, b, bsc, start=True, stop=True):
-        run([out], [a, asc, b, bsc], lambda e: g.tensor.matmul_mx(out[0], a[0], asc[0], b[0], bsc[0], start, stop), {"T": TENS})
+        run([out], [a, asc, b, bsc], lambda e: g.tensor.matmul_mx(out[0], a[0], asc[0], b[0], bsc[0], start, stop), {"T": TENS * b[7] / 128})
 
     def by_list(out):
         return 60 + 1.25 * out[7]
 
-    def gather(out, win, off, es="S", func=AF.Copy, scale=1.0, bias=0.0):
+    def gather(out, win, off, es="S"):
         def call(e):
             if e == "V":
                 return g.vector.tensor_copy(out[0], win[0].indirect(off[0]))
-            if func == AF.Copy:
-                return g.scalar.activation(out[0], win[0].indirect(off[0]), AF.Copy)
-            return g.scalar.activation(out[0], win[0].indirect(off[0]), func, bias=bias, scale=scale)
+            return g.scalar.activation(out[0], win[0].indirect(off[0]), AF.Copy)
         run([out], [win, off], call, {e: by_list(out) for e in es})
 
-    def choose(out, win, off, m):
-        run([out], [win, off, m], lambda e: g.vector.tensor_tensor(out[0], win[0].indirect(off[0]), m[0], OP.mult), {"V": by_list(out)})
+    def choose(out, win, off, m, op=OP.mult):
+        run([out], [win, off, m], lambda e: g.vector.tensor_tensor(out[0], win[0].indirect(off[0]), m[0], op), {"V": by_list(out)})
+
+    def under(out, win, off, a, b=None):
+        if b is None:
+            run([out], [win, off, a], lambda e: g.vector.tensor_scalar(out[0], win[0].indirect(off[0]), a[0], None, OP.is_lt), {"V": by_list(out)})
+        else:
+            run([out], [win, off, a, b], lambda e: g.vector.tensor_scalar(out[0], win[0].indirect(off[0]), a[0], b[0], OP.is_lt, OP.add),
+                {"V": by_list(out)})
 
     def pick(oq, os, oa, ob, iq, isc, ia, ib, off):
         o, w = v(oq, oa, ob), v(iq, ia, ib)
-        i = run([o], [w, off], lambda e: g.vector.tensor_copy(o[0].bitcast(dt.uint32), w[0].bitcast(dt.uint32).indirect(off[0])), {"V": by_list(o)})
+        run([o], [w, off], lambda e: g.vector.tensor_copy(o[0].bitcast(dt.uint32), w[0].bitcast(dt.uint32).indirect(off[0])), {"V": by_list(o)})
         gather(v(os, oa, ob), v(isc, ia, ib), off)
-        return i
 
     def iota(out, pattern, base, cm, flag=True):
         run([out], [], lambda e: g.iota(out[0], pattern, base, cm, allow_small_or_imprecise_dtypes=True) if flag else g.iota(out[0], pattern, base, cm),
@@ -321,13 +333,6 @@ def rank_program(g, core, T, topo):
             cp(v(name, 32 * a + c0, 32 * a + 32, st, 32 * d, 32 * d + 32), v(name, 32 * a + c0, 32 * a + 32, st, 32 * a, 32 * a + 32), "VS")
         cp(v(name, 64 + c0, 128, st, 0, 64), v(name, 64 + c0, 128, st, 64, 128), "VS")
         cp(v(name, c0, 64, st, 64, 128), v(name, c0, 64, st, 0, 64), "VS")
-
-    def wrap(tag, col):
-        ts(v("qz" + tag), v("wmh"), col, OP.mult)
-        turn(v("qt" + tag), v("qz" + tag))
-        scan(v("qs" + tag), v("qt" + tag))
-        quarters("qs" + tag, 15, 16)
-        return v("qs" + tag, 15, 128, 16)
 
     def wrap_sum(tag, a, b, out):
         ts(v("qz" + tag), v("wmb"), a, OP.add, b, OP.add)
@@ -342,44 +347,44 @@ def rank_program(g, core, T, topo):
     def fc(k):
         return v("fcol", k, k + 1)
 
+    def kf(k):
+        return v("kf", 8 * k, 8 * k + 8)
+
     classes = ((2, 0, 5), (1, 5, 5), (0, 10, 6))
-    part = [(v("nbt", 2 - (2 - i) % 3, 5 - (2 - i) % 3, 1, 8 * s, 8 * (s + n)), T.nb[i:16:3, :]) for i, s, n in classes]
-    dma("S", "d_nbu", part[0])
-    dma("Y", "d_nbt", *part[1:])
-    dma("S", "d_x", (v("xt", 0, 512), T.x[:, :]))
-    for k, by in ((0, 6), (1, 11), (2, 0)):
+    for k, by in ((2, 0), (0, 6), (1, 11)):
         moves = []
         for h in range(2):
             for i, s, n in classes:
                 p, c = 16 * h + (s + by) % 16, (k - i) % 3
                 moves.append((v("nl", 24 * k, 24 * k + 22, 1, p, p + n), T.nb[i:16:3, c:c + 22]))
-        dma("Y", "d_n%d" % k, *moves)
+        if k == 2:
+            dma("S", "d_n3", *moves[:3])
+            dma("Y", "d_n2", *moves[3:])
+            dma("Y", "d_x", (v("xt", 0, 512), T.x[:, :]))
+        else:
+            dma("Y", "d_n%d" % k, *moves)
     dma("Y", "d_w", (v("wt", 0, 512), T.w[:, :]))
 
     iota(ic(0), [[0, 1]], 0, 1, False)
-    iota(v("npf"), [[1, 128]], 0, -1)
-    iota(v("k128"), [[0, 128]], 128, 0)
+    iota(v("kb"), [[1, 256]], 0, 0)
     iota(v("n16"), [[0, 8], [1, 16]], 0, 0)
+    iota(v("npf"), [[1, 128]], 0, -1)
     iota(fc(0), [[0, 1]], 0, 1)
-    iota(v("d24"), [[1, 24]], 0, 0)
-    iota(fc(6), [[0, 1]], -64, 256)
     iota(v("lf"), [[0, 32]], 0, 0)
     iota(v("ks"), [[1, 4], [0, 128]], 0, 0)
     iota(v("nbp"), [[0, 384]], 0, 0)
     iota(v("pa", 0, 128), [[0, 128]], -1, 0)
     iota(v("pb", 0, 128), [[0, 128]], -1, 0)
-    fill(v("zz"), 0.0)
+    fill(v("zz", 0, 8), 0.0)
     fill(v("et"), 0.0)
     fill(v("mq"), -BIG)
-    ts(ic(1), ic(0), 3, OP.arith_shift_right)
-    ts(ic(2), ic(0), 7, OP.bitwise_and)
+    fill(v("inv"), 0.0)
+    for t in "01":
+        fill(v("lt" + t, 0, 4), -BIG / 2)
     ts(ic(3), ic(0), 15, OP.bitwise_and)
-    cp(fc(1), ic(1))
     cp(fc(2), ic(3))
-    ts(fc(3), ic(2), 16, OP.mult, fc(1), OP.add)
-    ts(fc(7), fc(2), 8, OP.mult)
-    ts(fc(4), fc(3), 128 * r, OP.add)
-    ts(fc(5), fc(3), 128 * 127 - 64, OP.add)
+    ts(fc(4), ic(3), 128 * r, OP.add)
+    ts(fc(5), ic(3), 1.0 / 4096, OP.mult)
     act(v("npb"), v("npf"), AF.Abs)
     act(v("eye"), v("npb"), AF.Relu, -1.0, 1.0)
     act(v("et", 4, 516, 4), v("eye"), AF.Copy, 0.5)
@@ -389,39 +394,51 @@ def rank_program(g, core, T, topo):
     ts(v("wm"), v("n16"), fc(2), OP.is_equal)
     ts(v("wmb"), v("n16"), fc(2), OP.is_equal, 4, OP.mult)
     ts(v("wmh"), v("n16"), fc(2), OP.is_equal)
-    cp(v("smb"), v("sm"), "S")
+    act(v("smb"), v("n16"), AF.Sign)
     ts(ic(5), ic(0), 4, OP.arith_shift_right)
     cp(fc(14), ic(5))
     ts(fc(15), fc(14), 0.125, OP.mult)
     ts(fc(16), fc(14), 0, OP.is_equal, fc(15), OP.add)
     ts(fc(17), fc(2), -512, OP.add)
-    fill(v("pq", 0, 32, 1, 0, 32), 0.0)
+    ts(fc(18), fc(0), 1.0 / 128, OP.mult)
+    ts(fc(32), fc(14), 0, OP.is_gt, 3, OP.mult)
+    ts(v("gol", 0, 8), v("zz", 0, 8), fc(32), OP.add, fc(14), OP.add)
 
-    ts(fc(9), v("nbt", 2, 3), 0.5, OP.add, fc(4), OP.min)
-    turned = [(k, bit, sign) for k, bit, sign in ((8, 128 * r, -8), (9, 896 - 128 * r, 8)) if bit]
-    for k, bit, sign in turned:
-        ts(ic(k), v("nbt", 2, 3), bit, OP.bitwise_and)
-    k, bit, sign = turned[0]
-    ts(fc(28), ic(k), sign, OP.mult)
-    rest = fc(9)
-    for k, bit, sign in turned[1:]:
-        ts(fc(29), ic(k), sign, OP.mult, rest, OP.add)
-        rest = fc(29)
-    ts(v("zk"), v("zz"), fc(28), OP.add, rest, OP.add)
-    key = fc(10)
-    tt(key, fc(28), rest, OP.add)
-    turn(v("rk"), v("zk"))
-    quarters("rk", 0, 1)
-    act(v("sgn"), v("rk"), AF.Sign, -1.0, key, fc(11))
-    ts(v("cl", 0, 8), v("d24", 0, 8), fc(7), OP.add)
+    wide = max(256 * r + 128, 128 * (N + r)) if r < N - 1 else 256 * r + 128
+    for q in range(N):
+        a, b = 128 * (q + min(q, r)), 256 if q < r else 128
+        shift(v("kt", a, a + b), v("kb", 0, b), float(a + 2048 * (q ^ r)))
+    ts(kf(0), v("kb", 0, 8), 16, OP.mult, fc(4), OP.add)
+    ts(kf(1), v("kb", 0, 8), 1.0 / 256, OP.mult, fc(5), OP.add)
+    act(v("frr"), v("kb", 0, 128), AF.Copy, 1.0 / 256)
+    for q in range(4):
+        cp(v("km", 0, 8, 1, 32 * q, 32 * q + 32), v("nl", 48, 72, 3, 0, 32))
+    ts(v("km", 8, 16), v("km", 0, 8), 128 * (N - 1), OP.bitwise_and)
+    tt(kf(2), v("km", 0, 8), kf(0), OP.min)
+    ts(v("km", 16, 24), v("km", 0, 8), 128 * r, OP.bitwise_and)
+    tt(kf(3), v("km", 8, 16), kf(2), OP.add)
+    ts(kf(4), v("km", 16, 24), -32, OP.mult, 2048 * r, OP.add)
+    tt(kf(8), v("km", 8, 16), kf(1), OP.add)
+    cp(v("cl", 0, 8), kf(3))
+    tt(kf(5), kf(4), kf(3), OP.add)
+    ts(kf(9), kf(8), 16, OP.mult)
+    tt(kf(6), kf(5), kf(9), OP.add)
+    choose(v("rk"), v("kt", 0, wide), v("cl", 0, 8), v("frr"), OP.add)
+    for c in range(5):
+        act(v("sgn", 128 * c, 128 * c + 128), v("rk"), AF.Sign, -1.0, v("kf", 48 + c, 49 + c), v("kf", 56 + c, 57 + c))
+    for c in range(5, 8):
+        ts(v("sgn", 128 * c, 128 * c + 128), v("rk"), v("kf", 48 + c, 49 + c), OP.is_lt)
+    for c in range(5, 8):
+        red(v("kf", 56 + c, 57 + c), v("sgn", 128 * c, 128 * c + 128), OP.add)
+    cp(v("pol", 5, 8), v("kf", 61, 64))
+    ts(v("pol", 0, 5), v("kf", 56, 61), 127, OP.add, 0.5, OP.mult)
     quant(v("q0"), v("q0s"), v("xt", 0, 512))
-    ts(v("zx"), v("k128"), fc(11), OP.mult, fc(5), OP.add)
-    turn(v("rx"), v("zx"))
-    quarters("rx", 0, 1)
-    ts(v("dx"), v("rx"), fc(6), OP.subtract)
-    red(fc(12), v("dx"), OP.min, True)
-    gather(v("posn"), v("rx"), v("cl", 0, 8), "S", AF.Identity, 1.0 / 256, WHOLE)
-    wp = wrap("p", fc(12))
+    run([v("inv")], [v("kb", 0, 128), v("pol", 0, 8)],
+        lambda e: g.vector.tensor_copy(T.inv[:, 0:128].indirect(T.pol[:, 0:8]), T.kb[:, 0:128]), {"V": 400.0})
+    gather(v("posn"), v("kb", 0, 128), v("pol", 0, 8))
+    tt(v("invm"), v("inv"), v("wmh"), OP.mult)
+    scan(v("invs"), v("invm"))
+    wp = v("invs", 15, 128, 16)
     cp(v("pl", 0, 8), wp)
     pick("w0", "ws0", 0, 128, "q0", "q0s", 0, 128, v("pl", 0, 8))
 
@@ -445,23 +462,23 @@ def rank_program(g, core, T, topo):
                                     src=T.ws0[:, 272:384], dst=T.hls[:, 16:128])]
             post(v("ws0", 272, 384), tr, len(others), v("lls", 144, 256), FLIGHT + HOP)
 
-    def send_col(name, c0, dst, sem, flight):
+    def send_col(name, c0, dst, d0, sem, flight):
         tr = []
         for who, es in ((far, lanes), (near, inside)):
             tr.append(RemoteDMATransfer(dst_ids=[dest(c) for d, c in who], dma_engine_mask=bits(es), remote_sem=T.sem[sem],
-                                        srcs=[T[name][:, c0:c0 + 1]], dsts=[T[dst][:, d:d + 1] for d, c in who]))
-        post(v(name, c0, c0 + 1), tr, len(lanes) + len(inside), v(dst, 1, 8), flight)
+                                        srcs=[T[name][:, c0:c0 + 1]], dsts=[T[dst][:, d0 + d:d0 + d + 1] for d, c in who]))
+        post(v(name, c0, c0 + 1), tr, len(lanes) + len(inside), v(dst, d0 + 1, d0 + 8), flight)
 
     few = len(far) * len(lanes) + len(near) * len(inside)
     for t in range(2):
         total["arr%d" % t] = sum(leave)
         note("R", [v("ll", 128 * t + 16, 128 * t + 128), v("lls", 128 * t + 16, 128 * t + 128)], [], ("arr%d" % t, total["arr%d" % t]))
-    for sem, dst in (("thr0", "lt0"), ("thr1", "lt1"), ("thd", "dt1")):
+    for sem, dst, d0 in (("thr0", "lt0", 3), ("thr1", "lt1", 3), ("thd", "dt1", 0)):
         total[sem] = few
-        note("R", [v(dst, 1, 8)], [], (sem, few))
+        note("R", [v(dst, d0 + 1, d0 + 8)], [], (sem, few))
 
-    def bank(k):
-        return v("pm", 512 * k, 512 * k + 128)
+    def bank(k, n=128):
+        return v("pm", 512 * k, 512 * k + n)
 
     def scores(t, jobs):
         for k, b, m, col in jobs:
@@ -492,6 +509,10 @@ def rank_program(g, core, T, topo):
         a = (256, 384, 128)[k]
         quant(v("w" + t, a, a + 128), v("ws" + t, a, a + 128), v("nt" + t, 512 * k, 512 * k + 512))
 
+    def with_w(k, a, b):
+        mm(bank(k, b - a), v("wq"), v("wqs"), v("w1", a, b), v("ws1", a, b))
+        cp(v("ya", a, b), bank(k, b - a), "VS")
+
     for t in "01":
         W, WS, G, GS, sc, met = "w" + t, "ws" + t, "g" + t, "gs" + t, "sc" + t, "met" + t
         L, LS = ("ll", "lls") if t == "0" else ("l1", "l1s")
@@ -513,7 +534,7 @@ def rank_program(g, core, T, topo):
             cp(v("lf", 0, 16, 1, 32, 64), v("lf", 0, 16, 1, 0, 32), "S")
             cp(v("lf", 0, 16, 1, 64, 128), v("lf", 0, 16, 1, 0, 64), "S")
             ts(v("nlu", 0, 16), v("lf", 0, 16), -128 * r, OP.add)
-            gather(v("npos"), v("posn"), v("nlu", 0, 16), "S", AF.Identity, 1.0, -WHOLE)
+            gather(v("npos"), v("posn"), v("nlu", 0, 16))
             ts(v("pl", 8, 16), wp, 128, OP.add)
             gather(v("nsl"), v("npos"), v("pl", 0, 16))
             for k in range(2):
@@ -527,21 +548,20 @@ def rank_program(g, core, T, topo):
             ts(ic(4), ic(0), 1, OP.bitwise_and)
             ts(fc(13), ic(4), -2, OP.mult, fc(2), OP.add)
             ts(v("swl", 0, 1), fc(13), 1, OP.add)
-            ts(v("dmb"), v("d24", 0, 8), fc(14), OP.not_equal, BIG, OP.mult)
-            ts(v("dmk"), v("d24", 0, 8), fc(14), OP.is_equal)
+            ts(v("dmk"), v("kb", 0, 8), fc(14), OP.is_equal)
             scores(t, [(0, 0, "e0", 0), (1, 0, "e1", 1)])
             tt(best, s_(0), s_(1), OP.max)
             tt(v("ed"), v("e1"), v("e0"), OP.subtract)
         else:
             ts(v("pen1", 0, 2), v("met0", 0, 2), -BIG / 128, OP.mult)
-            ts(v("pen1", 4, 5), v("met0", 2, 3), -BIG / 128, OP.mult)
+            ts(v("pen1", 4, 5), v("cq0", 0, 1), -BIG / 128, OP.mult)
             ts(fc(30), v("dsr", 0, 1), -BIG / 2, OP.mult, BIG, OP.add)
             ts(fc(31), v("met0", 0, 1), v("met0", 1, 2), OP.subtract, BIG / 2, OP.mult)
             act(v("nmA"), v("ed"), AF.Abs, fc(30), fc(31))
             act(v("nm"), v("nmA"), AF.Identity, 1.0, -BIG)
             tt(v("nmB"), bank(0), v("nm"), OP.add)
             red(best, v("nmB"), OP.max)
-        send_col("mq", mb, "lt" + t, "thr" + t, (WAY0, WAY1)[int(t)])
+        send_col("mq", mb, "lt" + t, 3, "thr" + t, (WAY0, WAY1)[int(t)])
         if t == "0":
             pick(G, GS, 0, 256, W, WS, 0, 128, v("xsl", 0, 16))
             ts(fc(19), s_(1), s_(0), OP.is_gt)
@@ -593,16 +613,10 @@ def rank_program(g, core, T, topo):
             dma("Y", "d_nbp", (v("nbp", 0, 384, 1, 0, 1), v("lft", 0, 16, 1, 0, 24)))
         else:
             ts(v("pl", 16, 24), wp, 256, OP.add)
-            for k in range(2):
-                dma("Y", "d_pq%d" % k, (v("pq", 16 * k, 16 * k + 16, 1, 0, 8), v("posn", 0, 128, 1, 0, 1)))
-            turn(v("pqt", 0, 32, 1, 0, 32), v("pq", 0, 32, 1, 0, 32))
-            cp(v("pqt", 0, 8, 1, 32, 64), v("pqt", 0, 8, 1, 0, 32), "S")
-            cp(v("pqt", 0, 8, 1, 64, 128), v("pqt", 0, 8, 1, 0, 64), "S")
             gather(v("pa", 128, 256), v("nbp"), v("pl", 16, 24), "VS")
             gather(v("pa", 256, 512), v("nbp"), v("pl", 0, 16), "VS")
             cp(v("pb", 128, 256), v("pa", 128, 256), "VS")
             gather(v("pb", 256, 384), v("pa", 256, 512), v("gll", 0, 8), "VS")
-            ts(v("pol", 0, 8), v("pqt", 0, 8), -WHOLE, OP.add)
             quant(v("wq"), v("wqs"), v("wt", 0, 512))
             gather(v("prs0"), v("pb"), v("vl0"), "VS")
             gather(v("pro0"), v("prs0"), v("pol", 0, 8), "VS")
@@ -617,36 +631,39 @@ def rank_program(g, core, T, topo):
         mm(bank(2), v(G, 128, 256), v(GS, 128, 256), l, ls)
         halves(t, 2, 1)
         scores(t, [(4, 0, "eye", 4), (5, 1, "e0", 5), (6, 2, "e1", 6)])
-        ts(v("s4m" + t, 1, 8), v("dmb", 1, 8), s_(4), OP.add)
-        ts(v("cq" + t, 0, 1), s_(7), s_(4), OP.is_lt)
+        ts(s_(17), s_(7), s_(4), OP.is_ge, -BIG, OP.mult)
         ts(m_(0), s_(5), s_(4), OP.max, s_(12), OP.is_le)
         ts(m_(1), s_(6), s_(4), OP.max, s_(13), OP.is_le)
+        tt(s_(18), s_(17), s_(4), OP.add)
         if t == "0":
             tt(v("dsr", 0, 1), m_(0), m_(1), OP.max)
-            send_col("dsr", 0, "dt1", "thd", HOP)
-        ts(s_(15), m_(0), 2, OP.mult, fc(15), OP.add)
+            send_col("dsr", 0, "dt1", 0, "thd", HOP)
+        ts(s_(15), m_(0), 2, OP.mult, fc((15, 18)[int(t)]), OP.add)
         ts(s_(16), m_(1), 2 + int(t), OP.mult, s_(15), OP.add)
         drain(t, 2)
-        tt(v("cq" + t, 1, 8), v("lt" + t, 1, 8), v("s4m" + t, 1, 8), OP.is_lt)
-        red(m_(2), v("cq" + t), OP.min)
         requant(t, 2)
-        wrap_sum("v" + t, m_(2), s_(16), v("vl" + t))
         if t == "0":
+            under(v("cq0"), v("lt0", 0, 11), v("gol", 0, 1), s_(18))
+            wrap_sum("v0", v("cq0", 0, 1), s_(16), v("vl0"))
             pick("w1", "ws1", 0, 128, W, WS, 0, 384, v("vl0"))
 
-    pick("f0", "f0s", 0, 128, "w1", "ws1", 0, 512, v("vl1"))
-    last = pick("f1", "f1s", 0, 128, "f0", "f0s", 0, 128, v("pol", 0, 8))
-    mm(bank(3), v("wq"), v("wqs"), v("f1"), v("f1s"))
+    with_w(3, 256, 512)
+    with_w(0, 0, 256)
+    under(v("zx"), v("lt1", 0, 11), v("gol", 0, 8), v("sc1", 18, 19), v("sc1", 16, 17))
+    turn(v("rx"), v("zx"))
+    quarters("rx", 0, 1)
+    choose(v("fm"), v("rx"), v("pol", 0, 8), v("wm"))
+    scan(v("fs"), v("fm"))
+    ts(v("vl1"), v("fs", 15, 128, 16), 128, OP.mult)
+    pick("f1", "f1s", 0, 128, "w1", "ws1", 0, 512, v("vl1"))
+    gather(v("yo"), v("ya"), v("vl1"), "V")
+    gather(v("pro1"), v("pa"), v("vl1"), "S")
     f1 = v("f1")
     dma("Y", "d_oc", (T.oc[:, :], (T.f1[:, :].bitcast(dt.uint8),) + f1[1:]))
-    gather(v("prs1"), v("pa"), v("vl1"), "VS")
-    ops[-1][3].append(last)
-    gather(v("pro1"), v("prs1"), v("pol", 0, 8), "VS")
-    cp(v("yo"), bank(3), "VS")
     for k in range(4):
         dma("Y", "d_os%d" % k, (T.osc[4 * k:4 * k + 4, :], v("f1s", 0, 128, 1, 32 * k, 32 * k + 4)))
     dma("S", "d_y", (T.y[:, :], v("yo")))
-    dma("Y", "d_p1", (T.pr[1:2, :], v("pro1", 0, 128, 1, 0, 1)))
+    dma("S", "d_p1", (T.pr[1:2, :], v("pro1", 0, 128, 1, 0, 1)))
     schedule()
     for sem, n in total.items():
         if waited.get(sem, 0) < n:

@@ -11,58 +11,58 @@ def _declare(dtype, width, names):
 
 
 _declare(I32, 72, "nl")
-_declare(I32, 24, "icol km")
+_declare(I32, 24, "icol km oi")
 _declare(BF16, 520, "xt wt et")
-_declare(BF16, 1024, "sgn")
-_declare(BF16, 128, "wmb wmh smb inv invm invs")
-_declare(BF16, 8, "dmk dsr dt1 dxm")
+_declare(BF16, 640, "sgs")
+_declare(BF16, 408, "sgn")
+_declare(BF16, 128, "wmb wmc inv invm invs kbh e0 e1 mp mu ma mb")
+_declare(BF16, 256, "wmh smb xm xs")
+_declare(BF16, 32, "iv n32")
 _declare(F32, 80, "fcol kf")
-_declare(F32, 32, "lf lft")
-_declare(F32, 128, "mq npf npb n16 wm nmA nmB nm ed zz sm eye rk zx rx frr e0 e1 posn yo xm0 xm1 xs0 xs1 fm fs")
-_declare(F32, 256, "selm npos nsl kb")
-_declare(F32, 384, "nbp pb")
-_declare(F32, 512, "ks pa ya")
+_declare(F32, 32, "lf lft cw zx ns")
+_declare(F32, 128, "mq n16 wm sm eye rk rx frr posn yo fm fs kb1 gid nbp sel pro0 pro1 prs0")
+_declare(F32, 256, "npos kb")
+_declare(F32, 384, "pa ks ya")
 _declare(F32, 2048, "kt")
-_declare(U16, 24, "nlu pl swl cl xsl pol gll dll gol")
-_declare(C4, 512, "eq")
-_declare(U8, 512, "es")
-_declare(C4, 256, "ll")
-_declare(U8, 256, "lls")
+_declare(U16, 16, "nlu pl xsl")
+_declare(U16, 8, "swl cl pol gol idl pcl il ofl dl")
+_declare(C4, 384, "eq ll")
+_declare(U8, 384, "es lls")
+_declare(C4, 256, "gn")
+_declare(U8, 256, "gns")
 _declare(U8, 128, "hls")
-_declare(C4, 128, "q0 wq f1 gl l1")
-_declare(U8, 128, "q0s wqs f1s gls l1s")
-for _c in ("v0", "l", "d"):
+_declare(C4, 128, "q0 wq f1 l1 hlc")
+_declare(U8, 128, "q0s wqs f1s l1s")
+for _c in ("v0", "b0", "b1"):
     _declare(BF16, 128, "qz%s qt%s qs%s" % (_c, _c, _c))
 for _t in "01":
-    _declare(C4, 512, "w" + _t)
-    _declare(U8, 512, "ws" + _t)
-    _declare(C4, 256, "g" + _t)
-    _declare(U8, 256, "gs" + _t)
-    _declare(F32, 8, "pen%s met%s" % (_t, _t))
-    _declare(F32, 16, "lt" + _t)
+    _declare(C4, 384, "w" + _t)
+    _declare(U8, 384, "ws" + _t)
+    _declare(C4, 128, "g" + _t)
+    _declare(U8, 128, "gs" + _t)
+    _declare(F32, 8, "pen" + _t)
+    _declare(F32, 16, "cq" + _t)
+    _declare(F32, 40, "lt" + _t)
     _declare(F32, 32, "mx%s sc%s" % (_t, _t))
-    _declare(F32, 1024, "ex" + _t)
-    _declare(BF16, 1536, "nt" + _t)
-    _declare(U16, 8, "vl" + _t)
-    _declare(F32, 128, "pro" + _t)
-_declare(F32, 128, "prs0")
-_declare(F32, 16, "cq0")
+    _declare(F32, 896, "ex" + _t)
+    _declare(BF16, 1024, "nt" + _t)
+    _declare(U16, 8, "vl%s bl%s" % (_t, _t))
 DMAS = ["d_n0", "d_n1", "d_n2", "d_n3", "d_x", "d_w", "d_nbp", "d_oc", "d_os0", "d_os1", "d_os2", "d_os3", "d_y", "d_p0", "d_p1"]
 SEMAPHORES = ["cV", "cS", "cT", "cG", "sent", "arr0", "arr1", "thr0", "thr1", "thd", "hop"] + DMAS
-BIG = 1e29
-WAKE, TENS, LOAD, ISSUE, FLIGHT = 200.0, 130.0, 1000.0, 400.0, 3500.0
-HOP, WAY0, WAY1 = 2500.0, 4200.0, 3000.0
-LOOK = 250.0
+BIG = 2.0 ** 88
+EST = {"wake": 180.0, "tens": 170.0, "load": 1180.0, "issue": 450.0, "flight": 3350.0, "scales": 3780.0, "hop": 4900.0, "merged": 2440.0,
+       "way0": 3450.0, "list": 1550.0, "way1": 2270.0, "look": 180.0, "cycle": 1.06}
 
 
 def rank_program(g, core, T, topo):
     N, cores = len(T.cores), T.cores
-    owner, helper = {}, {}
+    WAKE, LOOK = EST["wake"], EST["look"]
+    owner, first, second, third = {}, {}, {}, {}
     for c in cores:
-        for h in topo.cores_of(c):
-            if h not in cores and h not in owner and topo.die(h) == topo.die(c) and all(topo.may_write(h, d) for d in cores):
-                owner[h], helper[c] = c, h
-                break
+        free_ = [h for h in topo.cores_of(c) if h not in cores and h not in owner and topo.die(h) == topo.die(c)]
+        first[c] = [h for h in free_ if all(topo.may_write(h, d) for d in cores)][0]
+        second[c], third[c] = [h for h in free_ if h != first[c]][:2]
+        owner[first[c]] = owner[second[c]] = owner[third[c]] = c
     me = owner.get(core, core)
     r = T.rank_of(me)
     if r is None:
@@ -72,7 +72,9 @@ def rank_program(g, core, T, topo):
     chip = topo.cores_of(core)
     far = [(d, c) for d, c in peers if c not in chip]
     near = [(d, c) for d, c in peers if c in chip]
-    lanes = topo.engines(core, far[0][1])
+    plane = [(d, c) for d, c in far if topo.may_write(second[me], c) and topo.may_write(third[me], c)]
+    rest = [x for x in far if x not in plane]
+    lanes = topo.engines(me, far[0][1])
     spare = 2 * len(far) - len(lanes)
     others = [e for e in topo.engines(core, near[0][1]) if e not in lanes]
     inside = others[:2]
@@ -83,7 +85,16 @@ def rank_program(g, core, T, topo):
         for k, (d, c) in enumerate(far):
             way[d] = [mine[k]] if k < spare else [mine[spare + 2 * (k - spare)], mine[spare + 2 * (k - spare) + 1]]
         ways.append(way)
-    leave = [sum(len(x) for x in w.values()) for w in ways]
+
+    def even(who, with_near):
+        n = len(lanes) // len(who)
+        way = {d: lanes[n * k:n * k + n] for k, (d, c) in enumerate(who)}
+        if with_near:
+            way.update({d: inside for d, c in near})
+        return way
+
+    def engines(way):
+        return sum(len(x) for x in way.values())
 
     def bits(es):
         return sum(1 << e for e in es)
@@ -92,19 +103,22 @@ def rank_program(g, core, T, topo):
         rid, pid = topo.addr(c, core)
         return DstId(rid=rid, pnc=pid)
 
-    def columns(name, dst, c0, d0, part, sem):
+    def blocks(way, name, c0, dst, d0, sem, n=16):
         tr = []
-        for d, c in peers:
-            a, b = T[name][:, c0 + 16 * d:c0 + 16 * d + 16], T[dst][:, d0 + 16 * d:d0 + 16 * d + 16]
-            if part == 0:
+        for d, es in way.items():
+            a, b = T[name][:, c0 + n * d:c0 + n * d + n], T[dst][:, d0 + n * d:d0 + n * d + n]
+            if SCRATCH[name][2] == C4:
                 a, b = a.bitcast(dt.uint8), b.bitcast(dt.uint8)
-            tr.append(RemoteDMATransfer(dst_ids=[dest(c)], dma_engine_mask=bits(ways[part][d]), remote_sem=T.sem[sem], src=a, dst=b))
+            tr.append(RemoteDMATransfer(dst_ids=[dest(cores[r ^ d])], dma_engine_mask=bits(es), remote_sem=T.sem[sem], src=a, dst=b))
         return tr
 
+    half = len(others) // 2
     if core != me:
-        g.wait_ge(T.sem.hop, len(others))
-        g.remote_dma_fused(columns("hls", "lls", 0, 128, 1, "arr1"), local_sem=T.sem.sent)
-        g.wait_ge(T.sem.sent, leave[1])
+        way, src, dst = {first[me]: (even(rest, True), "hls", "lls"), second[me]: (even(plane, False), "hlc", "ll"),
+                         third[me]: (even(plane, False), "hls", "lls")}[core]
+        g.wait_ge(T.sem.hop, half)
+        g.remote_dma_fused(blocks(way, src, 0, dst, 256, "arr1"), local_sem=T.sem.sent)
+        g.wait_ge(T.sem.sent, engines(way))
         return
 
     queue = {"V": g.vector, "S": g.scalar, "T": g.tensor, "G": g, "Y": g.sync}
@@ -191,9 +205,12 @@ def rank_program(g, core, T, topo):
         for i, o in enumerate(ops):
             for j in o[3]:
                 users[j].append(i)
+
+        def gap(i, j):
+            return 0.0 if "T" in ops[i][1] and "T" in ops[j][1] else WAKE
         way = [0.0] * n
         for i in range(n - 1, -1, -1):
-            way[i] = min(ops[i][1].values()) + ops[i][2] + max([way[j] + WAKE for j in users[i]] + [0.0])
+            way[i] = min(ops[i][1].values()) + ops[i][2] + max([way[j] + gap(i, j) for j in users[i]] + [0.0])
         left, end, free = [len(o[3]) for o in ops], [0.0] * n, {}
         ready = {i: 0.0 for i in range(n) if not left[i]}
         when = []
@@ -227,7 +244,7 @@ def rank_program(g, core, T, topo):
             for j in users[i]:
                 left[j] -= 1
                 if not left[j]:
-                    ready[j] = max(end[m] for m in ops[j][3]) + WAKE
+                    ready[j] = max(end[m] + gap(m, j) for m in ops[j][3])
         for s, k, e, i in when:
             if e != "R":
                 ops[i][0](e)
@@ -235,7 +252,7 @@ def rank_program(g, core, T, topo):
     def val(x):
         return x[0] if isinstance(x, tuple) else x
 
-    def dma(e, sem, *moves):
+    def dma(es, sem, *moves):
         outs, ins = views([x for x, y in moves]), views([y for x, y in moves])
 
         def emit(e):
@@ -245,32 +262,34 @@ def rank_program(g, core, T, topo):
             total[sem] = 16 * len(moves)
             snap[(sem, total[sem])] = dict(known[e])
             note("D" + sem, outs, ins, (sem, total[sem]))
-        add(outs, ins, emit, {e: 60.0 * len(moves)}, LOAD)
+        add(outs, ins, emit, {e: 60.0 * len(moves) for e in es}, EST["load"])
 
-    def vec(x, a=1.0):
-        return max(64, a * x[7] * (0.5 if SCRATCH[x[1]][2] == BF16 else 1)) * 0.83
+    def vec(x, a=1.0, o=None):
+        two = SCRATCH[x[1]][2] in (BF16, U16) and (o is None or SCRATCH[o[1]][2] in (BF16, U16))
+        return max(64, a * x[7] * (0.5 if two else 1)) * EST["cycle"]
 
     def ts(out, a, s1, op0, s2=None, op1=None):
         if op1 is None:
-            run([out], [a, s1], lambda e: g.vector.tensor_scalar(out[0], a[0], val(s1), None, op0), {"V": vec(a)})
+            run([out], [a, s1], lambda e: g.vector.tensor_scalar(out[0], a[0], val(s1), None, op0), {"V": vec(a, 1, out)})
         else:
-            run([out], [a, s1, s2], lambda e: g.vector.tensor_scalar(out[0], a[0], val(s1), val(s2), op0, op1), {"V": vec(a)})
+            run([out], [a, s1, s2], lambda e: g.vector.tensor_scalar(out[0], a[0], val(s1), val(s2), op0, op1), {"V": vec(a, 1, out)})
 
     def tt(out, a, b, op):
         run([out], [a, b], lambda e: g.vector.tensor_tensor(out[0], a[0], b[0], op), {"V": vec(a, 1 if a[1] in ("pn", "pm") else 2)})
 
     def act(out, a, func, scale=1.0, bias=0.0, acc=None):
+        c = max(64, a[7]) * EST["cycle"]
         if acc is None:
-            run([out], [a, bias, scale], lambda e: g.scalar.activation(out[0], a[0], func, bias=val(bias), scale=val(scale)), {"S": vec(a)})
+            run([out], [a, bias, scale], lambda e: g.scalar.activation(out[0], a[0], func, bias=val(bias), scale=val(scale)), {"S": c})
         else:
-            run([out, acc], [a, bias], lambda e: g.scalar.activation(out[0], a[0], func, bias=val(bias), scale=scale, accum_out=acc[0]), {"S": vec(a) + 20})
+            run([out, acc], [a, bias], lambda e: g.scalar.activation(out[0], a[0], func, bias=val(bias), scale=scale, accum_out=acc[0]), {"S": c + 20})
 
     def cp(out, a, es="V"):
         def call(e):
             if e == "V":
                 return g.vector.tensor_copy(out[0], a[0])
             return g.scalar.activation(out[0], a[0], AF.Copy)
-        run([out], [a], call, {e: vec(a) for e in es})
+        run([out], [a], call, {e: vec(a, 1, out) for e in es})
 
     def shift(out, a, c):
         def call(e):
@@ -283,20 +302,20 @@ def rank_program(g, core, T, topo):
         run([out], [], lambda e: g.vector.memset(out[0], c), {"V": vec(out)})
 
     def red(out, a, op):
-        run([out], [a], lambda e: g.vector.tensor_reduce(out[0], a[0], AxisListType.X, op), {"V": max(64, a[7]) * 0.83})
+        run([out], [a], lambda e: g.vector.tensor_reduce(out[0], a[0], AxisListType.X, op), {"V": max(64, a[7]) * EST["cycle"]})
 
     def turn(out, a):
         run([out], [a], lambda e: g.vector.transpose(out[0], a[0]), {"V": vec(a)})
 
     def scan(z, q, op=OP.add):
-        s = v("smb" if SCRATCH[q[1]][2] == BF16 else "sm")
+        s = v("smb" if SCRATCH[q[1]][2] == BF16 else "sm", 0, q[7])
         run([z], [q, s], lambda e: g.vector.tensor_tensor_scan(z[0], s[0], q[0], 0.0, OP.mult, op), {"V": vec(q)})
 
     def quant(q, s, a):
-        run([q, s], [a], lambda e: g.vector.quantize_mx(q[0], s[0], a[0]), {"V": 12 + 0.22 * a[7]})
+        run([q, s], [a], lambda e: g.vector.quantize_mx(q[0], s[0], a[0]), {"V": (12 + 0.22 * a[7]) * EST["cycle"] / 0.83})
 
     def mm(out, a, asc, b, bsc, start=True, stop=True):
-        run([out], [a, asc, b, bsc], lambda e: g.tensor.matmul_mx(out[0], a[0], asc[0], b[0], bsc[0], start, stop), {"T": TENS * b[7] / 128})
+        run([out], [a, asc, b, bsc], lambda e: g.tensor.matmul_mx(out[0], a[0], asc[0], b[0], bsc[0], start, stop), {"T": EST["tens"] * b[7] / 128})
 
     def by_list(out):
         return 60 + 1.25 * out[7]
@@ -311,35 +330,30 @@ def rank_program(g, core, T, topo):
     def choose(out, win, off, m, op=OP.mult):
         run([out], [win, off, m], lambda e: g.vector.tensor_tensor(out[0], win[0].indirect(off[0]), m[0], op), {"V": by_list(out)})
 
-    def under(out, win, off, a, b=None):
-        if b is None:
-            run([out], [win, off, a], lambda e: g.vector.tensor_scalar(out[0], win[0].indirect(off[0]), a[0], None, OP.is_lt), {"V": by_list(out)})
-        else:
-            run([out], [win, off, a, b], lambda e: g.vector.tensor_scalar(out[0], win[0].indirect(off[0]), a[0], b[0], OP.is_lt, OP.add),
-                {"V": by_list(out)})
+    def under(out, win, off, a, b):
+        run([out], [win, off, a, b], lambda e: g.vector.tensor_scalar(out[0], win[0].indirect(off[0]), a[0], b[0], OP.max, OP.is_lt),
+            {"V": by_list(out)})
 
-    def pick(oq, os, oa, ob, iq, isc, ia, ib, off):
+    def pick(oq, os, oa, ob, iq, isc, ia, ib, off, es="S"):
         o, w = v(oq, oa, ob), v(iq, ia, ib)
         run([o], [w, off], lambda e: g.vector.tensor_copy(o[0].bitcast(dt.uint32), w[0].bitcast(dt.uint32).indirect(off[0])), {"V": by_list(o)})
-        gather(v(os, oa, ob), v(isc, ia, ib), off)
+        gather(v(os, oa, ob), v(isc, ia, ib), off, es)
 
     def iota(out, pattern, base, cm, flag=True):
         run([out], [], lambda e: g.iota(out[0], pattern, base, cm, allow_small_or_imprecise_dtypes=True) if flag else g.iota(out[0], pattern, base, cm),
             {"G": 130 + 1.66 * out[7]})
 
-    def quarters(name, c0, st):
-        for d in range(4):
-            a = d ^ 1
-            cp(v(name, 32 * a + c0, 32 * a + 32, st, 32 * d, 32 * d + 32), v(name, 32 * a + c0, 32 * a + 32, st, 32 * a, 32 * a + 32), "VS")
-        cp(v(name, 64 + c0, 128, st, 0, 64), v(name, 64 + c0, 128, st, 64, 128), "VS")
-        cp(v(name, c0, 64, st, 64, 128), v(name, c0, 64, st, 0, 64), "VS")
-
-    def wrap_sum(tag, a, b, out):
-        ts(v("qz" + tag), v("wmb"), a, OP.add, b, OP.add)
+    def wrap(tag, raised, a, b, op, out, *last):
+        name = "qs" + tag
+        ts(v("qz" + tag), v(raised), a, OP.add, b, op)
         turn(v("qt" + tag), v("qz" + tag))
-        scan(v("qs" + tag), v("qt" + tag), OP.max)
-        quarters("qs" + tag, 15, 16)
-        ts(out, v("qs" + tag, 15, 128, 16), 128, OP.mult, fc(17), OP.add)
+        scan(v(name), v("qt" + tag), OP.max)
+        for d in range(4):
+            x = d ^ 1
+            cp(v(name, 32 * x + 15, 32 * x + 32, 16, 32 * d, 32 * d + 32), v(name, 32 * x + 15, 32 * x + 32, 16, 32 * x, 32 * x + 32), "VS")
+        cp(v(name, 79, 128, 16, 0, 64), v(name, 79, 128, 16, 64, 128), "VS")
+        cp(v(name, 15, 64, 16, 64, 128), v(name, 15, 64, 16, 0, 64), "VS")
+        ts(out, v(name, 15, 128, 16), *last)
 
     def ic(k):
         return v("icol", k, k + 1)
@@ -348,7 +362,10 @@ def rank_program(g, core, T, topo):
         return v("fcol", k, k + 1)
 
     def kf(k):
-        return v("kf", 8 * k, 8 * k + 8)
+        return v("kf", 8 * k, 8 * k + 8, 1, 0, 32)
+
+    def km(k):
+        return v("km", 8 * k, 8 * k + 8, 1, 0, 32)
 
     classes = ((2, 0, 5), (1, 5, 5), (0, 10, 6))
     for k, by in ((2, 0), (0, 6), (1, 11)):
@@ -368,301 +385,313 @@ def rank_program(g, core, T, topo):
     iota(ic(0), [[0, 1]], 0, 1, False)
     iota(v("kb"), [[1, 256]], 0, 0)
     iota(v("n16"), [[0, 8], [1, 16]], 0, 0)
-    iota(v("npf"), [[1, 128]], 0, -1)
-    iota(fc(0), [[0, 1]], 0, 1)
     iota(v("lf"), [[0, 32]], 0, 0)
-    iota(v("ks"), [[1, 4], [0, 128]], 0, 0)
-    iota(v("nbp"), [[0, 384]], 0, 0)
-    iota(v("pa", 0, 128), [[0, 128]], -1, 0)
-    iota(v("pb", 0, 128), [[0, 128]], -1, 0)
-    fill(v("zz", 0, 8), 0.0)
-    fill(v("et"), 0.0)
-    fill(v("mq"), -BIG)
+    iota(v("nbp"), [[0, 128]], 0, 0)
+    iota(v("pa", 128, 256), [[0, 128]], -1, 0)
+    iota(v("ks"), [[-1, 3], [0, 128]], 2, 0)
+    fill(v("et", 0, 260), 0.0)
+    fill(v("et", 260, 520), 0.0)
+    fill(v("cl"), 0)
+    fill(v("mq"), 0.0)
     fill(v("inv"), 0.0)
+    fill(v("sgn", 128, 408, 136, 0, 32), -127.0)
     for t in "01":
-        fill(v("lt" + t, 0, 4), -BIG / 2)
+        fill(v("lt" + t, 0, 32), 0.0)
+    cp(fc(0), ic(0))
     ts(ic(3), ic(0), 15, OP.bitwise_and)
     cp(fc(2), ic(3))
     ts(fc(4), ic(3), 128 * r, OP.add)
     ts(fc(5), ic(3), 1.0 / 4096, OP.mult)
-    act(v("npb"), v("npf"), AF.Abs)
-    act(v("eye"), v("npb"), AF.Relu, -1.0, 1.0)
+    ts(v("eye"), v("kb", 0, 128), fc(0), OP.is_equal)
     act(v("et", 4, 516, 4), v("eye"), AF.Copy, 0.5)
+    units = [(v("eq", 128 * b, 128 * b + 128), v("es", 128 * b, 128 * b + 128)) for b in range(3)] + [(v("ll", 0, 128), v("lls", 0, 128))]
     for b in range(4):
-        quant(v("eq", 128 * b, 128 * b + 128), v("es", 128 * b, 128 * b + 128), v("et", 4 - b, 516 - b))
+        quant(units[b][0], units[b][1], v("et", 4 - b, 516 - b))
     act(v("sm"), v("n16"), AF.Sign)
+    for h in range(2):
+        act(v("smb", 128 * h, 128 * h + 128), v("n16"), AF.Sign)
+    act(v("kbh"), v("kb", 0, 128), AF.Copy)
+    act(v("kb1"), v("kb", 0, 128), AF.Identity, 1.0, 1.0)
     ts(v("wm"), v("n16"), fc(2), OP.is_equal)
-    ts(v("wmb"), v("n16"), fc(2), OP.is_equal, 4, OP.mult)
-    ts(v("wmh"), v("n16"), fc(2), OP.is_equal)
-    act(v("smb"), v("n16"), AF.Sign)
+    for h in range(2):
+        act(v("wmh", 128 * h, 128 * h + 128), v("wm"), AF.Copy)
+    act(v("wmb"), v("wm"), AF.Copy, 128.0)
     ts(ic(5), ic(0), 4, OP.arith_shift_right)
-    cp(fc(14), ic(5))
-    ts(fc(15), fc(14), 0.125, OP.mult)
-    ts(fc(16), fc(14), 0, OP.is_equal, fc(15), OP.add)
+    ts(fc(15), ic(5), 0.125, OP.mult, 5, OP.add)
+    act(v("wmc"), v("wm"), AF.Copy, fc(15))
     ts(fc(17), fc(2), -512, OP.add)
-    ts(fc(18), fc(0), 1.0 / 128, OP.mult)
-    ts(fc(32), fc(14), 0, OP.is_gt, 3, OP.mult)
-    ts(v("gol", 0, 8), v("zz", 0, 8), fc(32), OP.add, fc(14), OP.add)
+    ts(fc(18), fc(0), 1.0 / 128, OP.mult, 1, OP.add)
+    act(v("cw"), v("kb", 0, 32), AF.Identity, 0.0, fc(18))
+    ts(fc(1), ic(0), 1, OP.add)
+    ts(fc(32), ic(5), 0, OP.is_gt, 31, OP.mult)
+    ts(v("gol", 0, 1), ic(5), fc(32), OP.add)
+    ts(v("idl"), v("kb", 0, 8), 16, OP.mult, fc(2), OP.add)
+    cp(v("pcl", 0, 1), ic(0))
+    ts(ic(4), ic(0), 1, OP.bitwise_and)
+    ts(fc(13), ic(4), -2, OP.mult, fc(2), OP.add)
+    ts(v("swl", 0, 1), fc(13), 1, OP.add)
+    ts(ic(6), ic(0), 5, OP.arith_shift_right)
+    ts(fc(14), ic(6), -32, OP.mult, 128, OP.add)
 
     wide = max(256 * r + 128, 128 * (N + r)) if r < N - 1 else 256 * r + 128
     for q in range(N):
         a, b = 128 * (q + min(q, r)), 256 if q < r else 128
         shift(v("kt", a, a + b), v("kb", 0, b), float(a + 2048 * (q ^ r)))
-    ts(kf(0), v("kb", 0, 8), 16, OP.mult, fc(4), OP.add)
-    ts(kf(1), v("kb", 0, 8), 1.0 / 256, OP.mult, fc(5), OP.add)
+    low = v("kb", 0, 8, 1, 0, 32)
+    ts(kf(0), low, 16, OP.mult, v("fcol", 4, 5, 1, 0, 32), OP.add)
+    ts(kf(1), low, 1.0 / 256, OP.mult, v("fcol", 5, 6, 1, 0, 32), OP.add)
     act(v("frr"), v("kb", 0, 128), AF.Copy, 1.0 / 256)
-    for q in range(4):
-        cp(v("km", 0, 8, 1, 32 * q, 32 * q + 32), v("nl", 48, 72, 3, 0, 32))
-    ts(v("km", 8, 16), v("km", 0, 8), 128 * (N - 1), OP.bitwise_and)
-    tt(kf(2), v("km", 0, 8), kf(0), OP.min)
-    ts(v("km", 16, 24), v("km", 0, 8), 128 * r, OP.bitwise_and)
-    tt(kf(3), v("km", 8, 16), kf(2), OP.add)
-    ts(kf(4), v("km", 16, 24), -32, OP.mult, 2048 * r, OP.add)
-    tt(kf(8), v("km", 8, 16), kf(1), OP.add)
-    cp(v("cl", 0, 8), kf(3))
+    ends = v("nl", 48, 72, 3, 0, 32)
+    ts(km(1), ends, 128 * (N - 1), OP.bitwise_and)
+    tt(kf(2), ends, kf(0), OP.min)
+    ts(km(2), ends, 128 * r, OP.bitwise_and)
+    tt(kf(3), km(1), kf(2), OP.add)
+    ts(kf(4), km(2), -32, OP.mult, 2048 * r, OP.add)
+    tt(kf(8), km(1), kf(1), OP.add)
+    cp(v("cl", 0, 8, 1, 0, 32), kf(3))
     tt(kf(5), kf(4), kf(3), OP.add)
     ts(kf(9), kf(8), 16, OP.mult)
     tt(kf(6), kf(5), kf(9), OP.add)
-    choose(v("rk"), v("kt", 0, wide), v("cl", 0, 8), v("frr"), OP.add)
+    choose(v("rk"), v("kt", 0, wide), v("cl"), v("frr"), OP.add)
+    keys = v("rk", 0, 128, 1, 0, 32)
     for c in range(5):
-        act(v("sgn", 128 * c, 128 * c + 128), v("rk"), AF.Sign, -1.0, v("kf", 48 + c, 49 + c), v("kf", 56 + c, 57 + c))
-    for c in range(5, 8):
-        ts(v("sgn", 128 * c, 128 * c + 128), v("rk"), v("kf", 48 + c, 49 + c), OP.is_lt)
-    for c in range(5, 8):
-        red(v("kf", 56 + c, 57 + c), v("sgn", 128 * c, 128 * c + 128), OP.add)
-    cp(v("pol", 5, 8), v("kf", 61, 64))
-    ts(v("pol", 0, 5), v("kf", 56, 61), 127, OP.add, 0.5, OP.mult)
+        act(v("sgs", 128 * c, 128 * c + 128, 1, 0, 32), keys, AF.Sign, -1.0, v("kf", 48 + c, 49 + c, 1, 0, 32), v("kf", 56 + c, 57 + c, 1, 0, 32))
+    for c in range(3):
+        ts(v("sgn", 136 * c, 136 * c + 128, 1, 0, 32), keys, v("kf", 53 + c, 54 + c, 1, 0, 32), OP.is_lt, 2, OP.mult)
+    for c in range(3):
+        red(v("kf", 61 + c, 62 + c, 1, 0, 32), v("sgn", 136 * c, 136 * c + 129, 1, 0, 32), OP.add)
+    for q in range(4):
+        ts(v("pol", 0, 8, 1, 32 * q, 32 * q + 32), kf(7), 127, OP.add, 0.5, OP.mult)
     quant(v("q0"), v("q0s"), v("xt", 0, 512))
-    run([v("inv")], [v("kb", 0, 128), v("pol", 0, 8)],
+    run([v("inv")], [v("kb", 0, 128), v("pol")],
         lambda e: g.vector.tensor_copy(T.inv[:, 0:128].indirect(T.pol[:, 0:8]), T.kb[:, 0:128]), {"V": 400.0})
-    gather(v("posn"), v("kb", 0, 128), v("pol", 0, 8))
-    tt(v("invm"), v("inv"), v("wmh"), OP.mult)
+    choose(v("invm"), v("inv"), v("idl"), v("wmh", 0, 128))
     scan(v("invs"), v("invm"))
-    wp = v("invs", 15, 128, 16)
-    cp(v("pl", 0, 8), wp)
-    pick("w0", "ws0", 0, 128, "q0", "q0s", 0, 128, v("pl", 0, 8))
+    cp(v("pl", 0, 8), v("invs", 15, 128, 16))
+    pick("w0", "ws0", 128, 256, "q0", "q0s", 0, 128, v("pl", 0, 8))
 
-    def post(src, tr, leave, land, flight):
+    def post(srcs, tr, leave, land=None, flight=0.0):
         def emit(e):
-            order("G", [], [src])
+            order("G", [], srcs)
             g.remote_dma_fused(tr, local_sem=T.sem.sent)
             total["sent"] = total.get("sent", 0) + leave
-        i = add([], [src], emit, {"G": ISSUE})
-        add([land], [], None, {"R": 0.0}, flight, (i,))
-
-    def send(part):
-        name, dst = (("w0", "ll"), ("ws0", "lls"))[part]
-        post(v(name, 0, 128), columns(name, dst, 0, 0, part, "arr0"), leave[part], v(dst, 16, 128), FLIGHT)
-
-    def send_merged(part):
-        if part == 0:
-            post(v("w0", 256, 384), columns("w0", "ll", 256, 128, 0, "arr1"), leave[0], v("ll", 144, 256), FLIGHT)
-        else:
-            tr = [RemoteDMATransfer(dst_ids=[dest(helper[core])], dma_engine_mask=bits(others), remote_sem=T.sem.hop,
-                                    src=T.ws0[:, 272:384], dst=T.hls[:, 16:128])]
-            post(v("ws0", 272, 384), tr, len(others), v("lls", 144, 256), FLIGHT + HOP)
+        i = add([], srcs, emit, {"G": EST["issue"]})
+        if land is not None:
+            add([land], [], None, {"R": 0.0}, flight, (i,))
 
     def send_col(name, c0, dst, d0, sem, flight):
         tr = []
         for who, es in ((far, lanes), (near, inside)):
             tr.append(RemoteDMATransfer(dst_ids=[dest(c) for d, c in who], dma_engine_mask=bits(es), remote_sem=T.sem[sem],
                                         srcs=[T[name][:, c0:c0 + 1]], dsts=[T[dst][:, d0 + d:d0 + d + 1] for d, c in who]))
-        post(v(name, c0, c0 + 1), tr, len(lanes) + len(inside), v(dst, d0 + 1, d0 + 8), flight)
+        post([v(name, c0, c0 + 1)], tr, len(lanes) + len(inside), v(dst, d0 + 1, d0 + 8), flight)
+
+    def send_merged():
+        a, b = 16 * plane[0][0], 16 * plane[-1][0] + 16
+        tr = [RemoteDMATransfer(dst_ids=[dest(first[core]), dest(third[core])], dma_engine_mask=bits(others[:half]), remote_sem=T.sem.hop,
+                                srcs=[T.ws0[:, 256:256 + 4 * (b - a)]], dsts=[T.hls[:, 0:4 * (b - a)]] * 2),
+              RemoteDMATransfer(dst_ids=[dest(second[core])], dma_engine_mask=bits(others[half:]), remote_sem=T.sem.hop,
+                                src=T.w0[:, 256 + a:256 + b].bitcast(dt.uint8), dst=T.hlc[:, a:b].bitcast(dt.uint8))]
+        post([v("ws0", 256, 384), v("w0", 256, 384)], tr, len(others), v("lls", 272, 384), EST["hop"])
+        post([v("w0", 256, 384)], blocks(even(rest, True), "w0", 256, "ll", 256, "arr1"), engines(even(rest, True)), v("ll", 272, 384), EST["merged"])
 
     few = len(far) * len(lanes) + len(near) * len(inside)
+    total["arr0"] = engines(ways[0]) + engines(ways[1])
+    total["arr1"] = 2 * engines(even(rest, True)) + 2 * engines(even(plane, False))
+    total["thd"] = engines(even(rest, True)) + engines(even(plane, False))
+    total["thr0"] = total["thr1"] = few
     for t in range(2):
-        total["arr%d" % t] = sum(leave)
-        note("R", [v("ll", 128 * t + 16, 128 * t + 128), v("lls", 128 * t + 16, 128 * t + 128)], [], ("arr%d" % t, total["arr%d" % t]))
-    for sem, dst, d0 in (("thr0", "lt0", 3), ("thr1", "lt1", 3), ("thd", "dt1", 0)):
-        total[sem] = few
-        note("R", [v(dst, d0 + 1, d0 + 8)], [], (sem, few))
+        note("R", [v("ll", 128 * t + 144, 128 * t + 256), v("lls", 128 * t + 144, 128 * t + 256)], [], ("arr%d" % t, total["arr%d" % t]))
+        note("R", [v("lt%d" % t, 32, 39)], [], ("thr%d" % t, few))
+    note("R", [v("dl", 0, 7)], [], ("thd", total["thd"]))
 
     def bank(k, n=128):
-        return v("pm", 512 * k, 512 * k + n)
+        return v("pn" if k < 4 else "pm", 512 * (k % 4), 512 * (k % 4) + n)
 
-    def scores(t, jobs):
-        for k, b, m, col in jobs:
-            x, out = v("ex" + t, 128 * k, 128 * k + 128), v("sc" + t, col, col + 1)
-            tt(x, bank(b), v(m), OP.mult)
-            if t == "0":
-                act(x, x, AF.Copy, acc=out)
-            else:
-                act(x, x, AF.Identity, bias=v("pen1", col, col + 1), acc=out)
-
-    def halves(t, k, part):
-        if part == 0:
-            m, s = v("w" + t, 0, 128), v("ws" + t, 0, 128)
-        elif k == 2:
-            m, s = (v("l1"), v("l1s")) if t == "1" else (v("ll", 0, 128), v("lls", 0, 128))
-        elif t == "0":
-            m, s = v("gl"), v("gls")
+    def score(t, k, b, m, bias=None, at=None):
+        at = k if at is None else at
+        x, out = v("ex" + t, 128 * at, 128 * at + 128), v("sc" + t, k, k + 1)
+        tt(x, bank(b), v(m), OP.mult)
+        if bias is None:
+            act(x, x, AF.Copy, acc=out)
         else:
-            m, s = v("g1", 128 * k, 128 * k + 128), v("gs1", 128 * k, 128 * k + 128)
-        for b in range(4):
-            mm(v("pn", 512 * b, 512 * b + 128), v("eq", 128 * b, 128 * b + 128), v("es", 128 * b, 128 * b + 128), m, s, part == 0, part == 1)
+            act(x, x, AF.Identity, bias=bias, acc=out)
 
-    def drain(t, k):
+    def both(a, b0, b1, out, bias):
+        tt(v("ex1", a, a + 128), bank(b0), v("ma"), OP.mult)
+        tt(v("ex1", a + 128, a + 256), bank(b1), v("mb"), OP.mult)
+        act(v("ex1", a, a + 256), v("ex1", a, a + 256), AF.Identity, bias=bias, acc=out)
+
+    def halves(m, s, banks, start):
         for b in range(4):
-            cp(v("nt" + t, 512 * k + b, 512 * k + 512, 4), v("pn", 512 * b, 512 * b + 128), "VS")
+            mm(bank(banks[b]), units[b][0], units[b][1], m, s, start, not start)
+
+    def drain(t, k, banks):
+        for b in range(4):
+            cp(v("nt" + t, 512 * k + b, 512 * k + 512, 4), bank(banks[b]), "VS")
 
     def requant(t, k):
-        a = (256, 384, 128)[k]
-        quant(v("w" + t, a, a + 128), v("ws" + t, a, a + 128), v("nt" + t, 512 * k, 512 * k + 512))
+        quant(v("w" + t, 256 * k, 256 * k + 128), v("ws" + t, 256 * k, 256 * k + 128), v("nt" + t, 512 * k, 512 * k + 512))
 
-    def with_w(k, a, b):
-        mm(bank(k, b - a), v("wq"), v("wqs"), v("w1", a, b), v("ws1", a, b))
-        cp(v("ya", a, b), bank(k, b - a), "VS")
+    def with_w(k, a):
+        mm(bank(k), v("wq"), v("wqs"), v("w1", a, a + 128), v("ws1", a, a + 128))
+        cp(v("ya", a, a + 128), bank(k), "VS")
 
+    n0, n1 = v("ns", 15, 16), v("ns", 31, 32)
+    low4, mixed = (0, 1, 2, 3), (7, 5, 6, 4)
     for t in "01":
-        W, WS, G, GS, sc, met = "w" + t, "ws" + t, "g" + t, "gs" + t, "sc" + t, "met" + t
-        L, LS = ("ll", "lls") if t == "0" else ("l1", "l1s")
+        W, WS = v("w" + t, 128, 256), v("ws" + t, 128, 256)
+        G, GS = v("g" + t), v("gs" + t)
+        L, LS = (v("ll", 128, 256), v("lls", 128, 256)) if t == "0" else (v("l1"), v("l1s"))
 
         def s_(a):
-            return v(sc, a, a + 1)
+            return v("sc" + t, a, a + 1)
 
-        def m_(a):
-            return v(met, a, a + 1)
+        def pen(a):
+            return v("pen" + t, a, a + 1)
 
         mb, mx = 32 * int(t), "mx" + t
         best = v("mq", mb, mb + 1)
         if t == "0":
-            send(0)
-            send(1)
-        mm(bank(0), v(W, 0, 128), v(WS, 0, 128), v(W, 0, 128), v(WS, 0, 128))
-        if t == "0":
+            post([W], blocks(ways[0], "w0", 128, "ll", 128, "arr0"), engines(ways[0]), v("ll", 144, 256), EST["flight"])
+            post([WS], blocks(ways[1], "ws0", 128, "lls", 128, "arr0"), engines(ways[1]), v("lls", 144, 256), EST["scales"])
             ts(v("lf", 0, 24, 1, 0, 32), v("nl", 0, 72, 3, 0, 32), 0, OP.add)
             cp(v("lf", 0, 16, 1, 32, 64), v("lf", 0, 16, 1, 0, 32), "S")
             cp(v("lf", 0, 16, 1, 64, 128), v("lf", 0, 16, 1, 0, 64), "S")
-            ts(v("nlu", 0, 16), v("lf", 0, 16), -128 * r, OP.add)
-            gather(v("npos"), v("posn"), v("nlu", 0, 16))
-            ts(v("pl", 8, 16), wp, 128, OP.add)
-            gather(v("nsl"), v("npos"), v("pl", 0, 16))
-            for k in range(2):
-                ts(v("e%d" % k), v("nsl", 128 * k, 128 * k + 128), fc(0), OP.is_equal)
-            for k in range(2):
-                choose(v("xm%d" % k), v("npos", 128 * k, 128 * k + 128), v("pl", 0, 8), v("wm"))
-            for k in range(2):
-                scan(v("xs%d" % k), v("xm%d" % k))
-            for k in range(2):
-                cp(v("xsl", 8 * k, 8 * k + 8), v("xs%d" % k, 15, 128, 16))
-            ts(ic(4), ic(0), 1, OP.bitwise_and)
-            ts(fc(13), ic(4), -2, OP.mult, fc(2), OP.add)
-            ts(v("swl", 0, 1), fc(13), 1, OP.add)
-            ts(v("dmk"), v("kb", 0, 8), fc(14), OP.is_equal)
-            scores(t, [(0, 0, "e0", 0), (1, 0, "e1", 1)])
-            tt(best, s_(0), s_(1), OP.max)
-            tt(v("ed"), v("e1"), v("e0"), OP.subtract)
-        else:
-            ts(v("pen1", 0, 2), v("met0", 0, 2), -BIG / 128, OP.mult)
-            ts(v("pen1", 4, 5), v("cq0", 0, 1), -BIG / 128, OP.mult)
-            ts(fc(30), v("dsr", 0, 1), -BIG / 2, OP.mult, BIG, OP.add)
-            ts(fc(31), v("met0", 0, 1), v("met0", 1, 2), OP.subtract, BIG / 2, OP.mult)
-            act(v("nmA"), v("ed"), AF.Abs, fc(30), fc(31))
-            act(v("nm"), v("nmA"), AF.Identity, 1.0, -BIG)
-            tt(v("nmB"), bank(0), v("nm"), OP.add)
-            red(best, v("nmB"), OP.max)
-        send_col("mq", mb, "lt" + t, 3, "thr" + t, (WAY0, WAY1)[int(t)])
+            ts(v("nlu"), v("lf", 0, 16), -128 * r, OP.add)
+            gather(v("posn"), v("kb", 0, 128), v("pol"))
+            gather(v("npos"), v("posn"), v("nlu"))
+            choose(v("iv", 0, 16), v("inv"), v("pcl", 0, 1), v("wmh", 0, 16))
+            red(fc(40), v("iv", 0, 16), OP.add)
+            ts(v("il", 0, 2), v("kb", 0, 256, 128), fc(40), OP.add)
+            choose(v("n32"), v("npos"), v("il", 0, 2), v("wmh", 0, 32))
+            scan(v("ns"), v("n32"))
+            ts(v("e0"), v("kbh"), n0, OP.is_equal)
+            ts(v("e1"), v("kbh"), n1, OP.is_equal)
+            ts(fc(41), n1, n0, OP.subtract)
+        mm(bank(4), W, WS, W, WS)
+        score(t, 0, 4, "e0", pen(0) if t == "1" else None)
+        score(t, 1, 4, "e1", pen(1) if t == "1" else None)
+        tt(best, s_(0), s_(1), OP.max)
+        send_col("mq", mb, "lt" + t, 31, "thr" + t, EST["way" + t])
+        ts(s_(8), s_(1), s_(0), OP.is_gt, fc(41), OP.mult)
+        wrap("b" + t, "wmb", s_(8), n0, OP.add, v("bl" + t), -128, OP.add)
+        pick("g" + t, "gs" + t, 0, 128, "w" + t, "ws" + t, 128, 256, v("bl" + t))
         if t == "0":
-            pick(G, GS, 0, 256, W, WS, 0, 128, v("xsl", 0, 16))
-            ts(fc(19), s_(1), s_(0), OP.is_gt)
-            wrap_sum("l", fc(19), fc(15), v("gll", 0, 8))
-            pick("gl", "gls", 0, 128, G, GS, 0, 256, v("gll", 0, 8))
+            pick("ll", "lls", 128, 144, "w0", "ws0", 128, 256, v("swl", 0, 1))
+            halves(W, WS, low4, True)
+            halves(G, GS, low4, False)
+            drain(t, 1, low4)
+            requant(t, 1)
+            send_merged()
+            halves(W, WS, low4, True)
         else:
-            scores(t, [(0, 0, "e0", 0), (1, 0, "e1", 1)])
-            pick(G, GS, 0, 128, W, WS, 0, 128, v("xsl", 0, 8))
-            pick(G, GS, 128, 256, W, WS, 0, 128, v("xsl", 8, 16))
-        halves(t, 0, 0)
-        halves(t, 0, 1)
-        pick("ll", "lls", 128 * int(t), 128 * int(t) + 16, W, WS, 0, 128, v("swl", 0, 1))
-        mm(bank(2), v(G, 0, 128), v(GS, 0, 128), v(G, 128, 256), v(GS, 128, 256))
-        mm(bank(3), v(G, 128, 256), v(GS, 128, 256), v(G, 0, 128), v(GS, 0, 128))
-        if t == "1":
-            for k in range(2):
-                x = v("selm", 128 * k, 128 * k + 128)
-                choose(x, v("ks"), v("vl0"), v("e%d" % k))
-                act(x, x, AF.Copy, acc=fc(20 + k))
-            ts(fc(22), v("sc0", 2, 3), v("sc0", 0, 1), OP.is_gt, -BIG / 128, OP.mult)
-            ts(fc(23), v("sc0", 3, 4), v("sc0", 1, 2), OP.is_ge, -BIG / 128, OP.mult)
-            ts(v("pen1", 2, 3), fc(20), 2, OP.is_equal, fc(22), OP.mult)
-            ts(v("pen1", 3, 4), fc(21), 2, OP.is_equal, fc(23), OP.mult)
-            ts(v("pen1", 5, 7), v("fcol", 20, 22), 1, OP.is_equal, -BIG / 128, OP.mult)
-        drain(t, 0)
-        if t == "1":
-            halves(t, 1, 0)
-            halves(t, 1, 1)
-        scores(t, [(2, 2, "e0", 2), (3, 3, "e1", 3)])
-        requant(t, 0)
+            pick("l1", "l1s", 0, 16, "w1", "ws1", 128, 256, v("swl", 0, 1))
+            pick("l1", "l1s", 16, 128, "ll", "lls", 0, 384, v("dl", 0, 7))
+            with_w(5, 128)
+            halves(W, WS, low4, True)
+        ts(s_(10), s_(1), s_(0), OP.is_gt)
         if t == "0":
-            send_merged(1)
-            send_merged(0)
+            ts(s_(9), s_(8), n0, OP.add)
+            ts(v("mp"), v("kbh"), s_(9), OP.is_equal, fc(1), OP.mult)
+            choose(v("mu"), v("kb1"), v("bl0"), v("mp"), OP.is_equal)
+            act(v("sel"), v("mu"), AF.Identity, -BIG, BIG / 128, pen(3))
+            ts(v("pl", 8, 16), v("invs", 15, 128, 16), 128, OP.add)
+            choose(v("xm"), v("npos"), v("pl"), v("wmh"))
+            scan(v("xs"), v("xm"))
+            cp(v("xsl"), v("xs", 15, 256, 16))
+        else:
+            G0, G1 = (v("gn", 0, 128), v("gns", 0, 128)), (v("gn", 128, 256), v("gns", 128, 256))
+            pick("gn", "gns", 0, 256, "w1", "ws1", 128, 256, v("xsl"))
+            mm(bank(6), *G0, *G1)
+            mm(bank(7), *G1, *G0)
+            score(t, 4, 6, "e0", None, 2)
+            score(t, 5, 7, "e1", None, 3)
+            ts(v("mp"), v("kbh"), n0, OP.subtract, s_(8), OP.is_equal)
+            choose(v("fm"), v("ks"), v("vl0"), v("mp"))
+            act(v("sel"), v("fm"), AF.Copy, acc=s_(13))
+            ts(s_(12), s_(0), s_(1), OP.is_ge)
+            ts(v("ma"), v("e0"), s_(12), OP.mult)
+            ts(v("mb"), v("e1"), s_(10), OP.mult)
+            ts(pen(5), s_(13), 2, OP.is_equal, -BIG, OP.mult)
+            ts(v("sc1", 18, 20), v("kb", 0, 2), s_(10), OP.is_equal, -512 * BIG, OP.mult)
+            ts(v("sc1", 20, 22), v("sc1", 18, 20), s_(13), OP.mult)
+            ts(s_(15), s_(4), best, OP.is_gt, s_(20), OP.mult)
+            ts(s_(16), s_(5), best, OP.is_ge, s_(21), OP.mult)
+            ts(s_(17), s_(15), s_(16), OP.add, best, OP.add)
         turn(v(mx, 0, 32, 1, 0, 32), v("mq", mb, mb + 32, 1, 0, 32))
         cp(v("mq", 64, 80, 2, 0, 32), v(mx, 1, 16, 2, 0, 32), "VS")
         cp(v("mq", 65, 80, 2, 0, 32), v(mx, 0, 16, 2, 0, 32), "VS")
-        turn(v("mq", 96, 128, 1, 0, 32), v("mq", 64, 96, 1, 0, 32))
-        ts(s_(10), s_(1), s_(2), OP.max, s_(0), OP.is_gt)
-        ts(s_(11), s_(0), s_(3), OP.max, s_(1), OP.is_ge)
-        tt(s_(7), v("mq", 96, 97), best, OP.max)
-        ts(s_(12), s_(10), -9 * BIG, OP.mult, s_(0), OP.add)
-        ts(s_(13), s_(11), -9 * BIG, OP.mult, s_(1), OP.add)
-        if t == "1":
-            drain(t, 1)
-            requant(t, 1)
-        halves(t, 2, 0)
+        turn(v("lt" + t, 0, 32, 1, 0, 32), v("mq", 64, 96, 1, 0, 32))
         if t == "0":
             turn(v("lft", 0, 32, 1, 0, 32), v("lf", 0, 32, 1, 0, 32))
-            dma("Y", "d_nbp", (v("nbp", 0, 384, 1, 0, 1), v("lft", 0, 16, 1, 0, 24)))
-        else:
-            ts(v("pl", 16, 24), wp, 256, OP.add)
-            gather(v("pa", 128, 256), v("nbp"), v("pl", 16, 24), "VS")
-            gather(v("pa", 256, 512), v("nbp"), v("pl", 0, 16), "VS")
-            cp(v("pb", 128, 256), v("pa", 128, 256), "VS")
-            gather(v("pb", 256, 384), v("pa", 256, 512), v("gll", 0, 8), "VS")
+            dma("Y", "d_nbp", (v("nbp", 0, 128, 1, 0, 1), v("lft", 0, 16, 1, 16, 24)))
+            gather(v("pa", 0, 128), v("nbp"), v("pl", 0, 8))
+            act(v("gid"), v("inv"), AF.Identity, 1.0, float(128 * r))
+            ts(v("sc0", 12, 14), v("kb", 0, 2), s_(10), OP.is_equal, -BIG, OP.mult)
             quant(v("wq"), v("wqs"), v("wt", 0, 512))
-            gather(v("prs0"), v("pb"), v("vl0"), "VS")
-            gather(v("pro0"), v("prs0"), v("pol", 0, 8), "VS")
+            ts(v("oi", 0, 8), v("pol"), fc(14), OP.add)
+            ts(v("oi", 8, 16), v("oi", 0, 8), 127, OP.bitwise_and)
+            cp(v("ofl"), v("oi", 8, 16))
+        gather(v("pa", 256, 384), v("gid"), v("bl" + t))
+        if t == "0":
+            mm(bank(5), W, WS, L, LS)
+            mm(bank(6), G, GS, L, LS)
+            halves(L, LS, low4, False)
+            score(t, 2, 5, "eye")
+            score(t, 3, 6, "mu", pen(3))
+            ts(s_(11), s_(2), s_(3), OP.max, best, OP.is_le)
+        else:
+            mm(bank(5), *G0, L, LS)
+            mm(bank(6), *G1, L, LS)
+            mm(bank(4), W, WS, L, LS)
+            halves(L, LS, low4, False)
+            both(640, 5, 6, s_(3), pen(5))
+            tt(v("ex1", 512, 640), bank(4), v("frr"), OP.add)
+            red(s_(2), v("ex1", 512, 640), OP.max)
+            ts(s_(11), s_(2), s_(3), OP.max, s_(17), OP.is_le)
+        under(v("cq" + t), v("lt" + t, 0, 39), v("gol", 0, 1), best, s_(2))
+        if t == "1":
+            halves(W, WS, mixed, True)
+            halves(G, GS, mixed, False)
+        drain(t, 0, low4)
+        requant(t, 0)
+        if t == "0":
+            wrap("v0", "wmc", s_(11), v("cq0", 0, 1), OP.subtract, v("vl0"), 128, OP.mult, fc(17), OP.add)
+            pick("w1", "ws1", 128, 256, "w0", "ws0", 0, 384, v("vl0"))
+            post([v("vl0")], blocks(even(rest, True), "vl0", 0, "dl", -1, "thd", 1), engines(even(rest, True)))
+            post([v("vl0")], blocks(even(plane, False), "vl0", 0, "dl", -1, "thd", 1), engines(even(plane, False)), v("dl", 0, 7), EST["list"])
+            ts(v("pen1", 0, 2), v("sc0", 12, 14), s_(11), OP.mult)
+            ts(v("pen1", 2, 3), v("cq0", 0, 1), -BIG, OP.mult, BIG, OP.add)
+            ts(v("frr"), v("eye"), v("pen1", 2, 3), OP.mult, -BIG, OP.add)
+            gather(v("prs0"), v("pa"), v("vl0"))
+            gather(v("pro0"), v("prs0"), v("pol"))
             dma("Y", "d_p0", (T.pr[0:1, :], v("pro0", 0, 128, 1, 0, 1)))
-            tt(v("dxm", 1, 8), v("dt1", 1, 8), v("dmk", 1, 8), OP.mult)
-            red(fc(24), v("dxm", 1, 8), OP.max)
-            wrap_sum("d", fc(24), fc(16), v("dll", 0, 8))
-            pick("l1", "l1s", 0, 128, "ll", "lls", 0, 256, v("dll", 0, 8))
-        l, ls = v(L, 0, 128), v(LS, 0, 128)
-        mm(bank(0), v(W, 0, 128), v(WS, 0, 128), l, ls)
-        mm(bank(1), v(G, 0, 128), v(GS, 0, 128), l, ls)
-        mm(bank(2), v(G, 128, 256), v(GS, 128, 256), l, ls)
-        halves(t, 2, 1)
-        scores(t, [(4, 0, "eye", 4), (5, 1, "e0", 5), (6, 2, "e1", 6)])
-        ts(s_(17), s_(7), s_(4), OP.is_ge, -BIG, OP.mult)
-        ts(m_(0), s_(5), s_(4), OP.max, s_(12), OP.is_le)
-        ts(m_(1), s_(6), s_(4), OP.max, s_(13), OP.is_le)
-        tt(s_(18), s_(17), s_(4), OP.add)
-        if t == "0":
-            tt(v("dsr", 0, 1), m_(0), m_(1), OP.max)
-            send_col("dsr", 0, "dt1", 0, "thd", HOP)
-        ts(s_(15), m_(0), 2, OP.mult, fc((15, 18)[int(t)]), OP.add)
-        ts(s_(16), m_(1), 2 + int(t), OP.mult, s_(15), OP.add)
-        drain(t, 2)
-        requant(t, 2)
-        if t == "0":
-            under(v("cq0"), v("lt0", 0, 11), v("gol", 0, 1), s_(18))
-            wrap_sum("v0", v("cq0", 0, 1), s_(16), v("vl0"))
-            pick("w1", "ws1", 0, 128, W, WS, 0, 384, v("vl0"))
 
-    with_w(3, 256, 512)
-    with_w(0, 0, 256)
-    under(v("zx"), v("lt1", 0, 11), v("gol", 0, 8), v("sc1", 18, 19), v("sc1", 16, 17))
-    turn(v("rx"), v("zx"))
-    quarters("rx", 0, 1)
-    choose(v("fm"), v("rx"), v("pol", 0, 8), v("wm"))
-    scan(v("fs"), v("fm"))
+    with_w(0, 0)
+    drain("1", 1, mixed)
+    requant("1", 1)
+    with_w(7, 256)
+    ts(v("zx"), v("cw"), v("sc1", 11, 12), OP.add, v("cq1", 0, 1), OP.subtract)
+    turn(v("rx", 0, 32), v("zx"))
+    for d in range(4):
+        x = (d + 1) % 4
+        cp(v("rx", 32, 64, 1, 32 * d, 32 * d + 32), v("rx", 0, 32, 1, 32 * x, 32 * x + 32), "VS")
+    cp(v("rx", 64, 128, 1, 0, 64), v("rx", 0, 64, 1, 64, 128), "VS")
+    cp(v("rx", 64, 128, 1, 64, 128), v("rx", 0, 64, 1, 0, 64), "VS")
+    choose(v("rk"), v("rx"), v("ofl"), v("wm"))
+    scan(v("fs"), v("rk"))
     ts(v("vl1"), v("fs", 15, 128, 16), 128, OP.mult)
-    pick("f1", "f1s", 0, 128, "w1", "ws1", 0, 512, v("vl1"))
-    gather(v("yo"), v("ya"), v("vl1"), "V")
-    gather(v("pro1"), v("pa"), v("vl1"), "S")
-    f1 = v("f1")
+    f1, last = v("f1"), v("vl1")
+    run([f1], [v("w1"), last], lambda e: g.vector.tensor_copy(f1[0].bitcast(dt.uint32), v("w1")[0].bitcast(dt.uint32).indirect(last[0])),
+        {"V": by_list(f1)})
+    gather(v("yo"), v("ya"), last, "S")
+    gather(v("f1s"), v("ws1"), last, "V")
+    gather(v("pro1"), v("pa"), last, "S")
     dma("Y", "d_oc", (T.oc[:, :], (T.f1[:, :].bitcast(dt.uint8),) + f1[1:]))
+    dma("Y", "d_y", (T.y[:, :], v("yo")))
     for k in range(4):
         dma("Y", "d_os%d" % k, (T.osc[4 * k:4 * k + 4, :], v("f1s", 0, 128, 1, 32 * k, 32 * k + 4)))
-    dma("S", "d_y", (T.y[:, :], v("yo")))
     dma("S", "d_p1", (T.pr[1:2, :], v("pro1", 0, 128, 1, 0, 1)))
     schedule()
     for sem, n in total.items():

@@ -11,29 +11,27 @@ def _declare(dtype, width, names):
 
 
 _declare(I32, 72, "nl")
-_declare(I32, 24, "icol km oi")
+_declare(I32, 24, "icol km")
 _declare(BF16, 520, "xt wt et")
-_declare(BF16, 640, "sgs")
-_declare(BF16, 408, "sgn")
-_declare(BF16, 128, "wmb wmc inv invm invs kbh e0 e1 mp mu ma mb")
-_declare(BF16, 256, "wmh smb xm xs")
-_declare(BF16, 32, "iv n32")
+_declare(BF16, 128, "wmb wmc wmh smb posn inv invm invs kbr kbh em e0 e1 mp mu ma mb ry")
+_declare(BF16, 256, "xm xs sgs")
+_declare(BF16, 32, "iv n32 zy")
+_declare(BF16, 16, "dt1 dsr")
 _declare(F32, 80, "fcol kf")
 _declare(F32, 32, "lf lft cw zx ns")
-_declare(F32, 128, "mq n16 wm sm eye rk rx frr posn yo fm fs kb1 gid nbp sel pro0 pro1 prs0")
+_declare(F32, 128, "mq n16 wm sm eye rk rx fs kb1 gid nbp sel pro0 pro1 prs0")
 _declare(F32, 256, "npos kb")
-_declare(F32, 384, "pa ks ya")
-_declare(F32, 2048, "kt")
-_declare(U16, 16, "nlu pl xsl")
-_declare(U16, 8, "swl cl pol gol idl pcl il ofl dl")
-_declare(C4, 384, "eq ll")
-_declare(U8, 384, "es lls")
-_declare(C4, 256, "gn")
-_declare(U8, 256, "gns")
+_declare(F32, 384, "pa ya")
+_declare(U16, 32, "nlu")
+_declare(U16, 8, "pl swl clq pol gol idl il ofl dl")
+_declare(C4, 512, "eq")
+_declare(U8, 512, "es")
+_declare(C4, 256, "ll")
+_declare(U8, 256, "lls")
 _declare(U8, 128, "hls")
-_declare(C4, 128, "q0 wq f1 l1 hlc")
-_declare(U8, 128, "q0s wqs f1s l1s")
-for _c in ("v0", "b0", "b1"):
+_declare(C4, 128, "q0 wq f1 l1 hlc la")
+_declare(U8, 128, "q0s wqs f1s l1s las")
+for _c in ("v0", "b0", "b1", "s", "d"):
     _declare(BF16, 128, "qz%s qt%s qs%s" % (_c, _c, _c))
 for _t in "01":
     _declare(C4, 384, "w" + _t)
@@ -42,21 +40,35 @@ for _t in "01":
     _declare(U8, 128, "gs" + _t)
     _declare(F32, 8, "pen" + _t)
     _declare(F32, 16, "cq" + _t)
-    _declare(F32, 40, "lt" + _t)
+    _declare(F32, 16, "lt" + _t)
     _declare(F32, 32, "mx%s sc%s" % (_t, _t))
-    _declare(F32, 896, "ex" + _t)
+    _declare(F32, 512, "ex" + _t)
     _declare(BF16, 1024, "nt" + _t)
     _declare(U16, 8, "vl%s bl%s" % (_t, _t))
 DMAS = ["d_n0", "d_n1", "d_n2", "d_n3", "d_x", "d_w", "d_nbp", "d_oc", "d_os0", "d_os1", "d_os2", "d_os3", "d_y", "d_p0", "d_p1"]
 SEMAPHORES = ["cV", "cS", "cT", "cG", "sent", "arr0", "arr1", "thr0", "thr1", "thd", "hop"] + DMAS
 BIG = 2.0 ** 88
-EST = {"wake": 180.0, "tens": 170.0, "load": 1180.0, "issue": 450.0, "flight": 3350.0, "scales": 3780.0, "hop": 4900.0, "merged": 2440.0,
-       "way0": 3450.0, "list": 1550.0, "way1": 2270.0, "look": 180.0, "cycle": 1.06}
+ORDER = """
+Y1 V27 G6 S0 V17 G7 V18 Y4 V13 V51 V25 V26 V23 Y3 V19 V30 V20 G8 V22 V60 Y2 V31 Y5 S40 V24 V69 S39 V62 G11 V21 S45 V52 S41
+V55 S43 V48 S54 S44 V32 G10 V75 V73 S49 V76 V74 S47 V109 V29 G9 V77 S80 V110 S72 G12 V108 S57 V78 V70 S111 V81 V56 V197 S79
+V71 V14 S82 Y198 V94 S112 S84 V116 S87 V113 S83 V85 S86 V88 S90 V89 V64 S114 V117 V92 V91 V15 V118 S115 V93 V33 V139 S96 V95
+S34 V140 V121 S58 V61 S120 G106 T144 V142 V141 S122 V143 S59 V63 S50 V147 V145 V123 V67 S148 V65 V35 S146 V36 S124 S119 V155
+V97 S135 V66 T171 T170 V156 S192 V125 S100 V137 V157 V37 S138 S199 G104 R105 R107 V158 V126 V16 T172 V191 V159 S160 S162 V149
+S161 V193 V127 V152 S164 V150 S163 V38 S130 S131 S98 V165 S129 V68 T173 V136 V151 V166 S167 G153 R154 V99 S42 S128 S132 T176
+T174 S133 T177 S180 T175 V134 S178 V194 S181 V101 S179 T187 S195 S53 T188 V182 S200 V196 G183 S169 T207 T208 T190 G185 R184
+R186 V213 V257 V215 S214 V258 V168 S216 S206 V259 V217 T209 V201 V261 T212 T189 V218 V223 S224 T211 V265 S227 T210 V219 S264
+V229 V263 V220 V230 V28 S266 V102 S226 G221 R222 S225 V231 V202 V234 S235 V233 S232 V242 V228 S236 S237 V260 S268 V238 V267
+V103 V239 S240 V203 S241 V269 S46 V292 S254 T262 V204 T303 T294 S293 V270 T302 V275 T298 T301 V271 V305 S276 S299 V272 S306
+V279 V273 S243 V304 V280 V274 S309 T295 S244 T300 G277 R278 T339 V307 V317 V310 V281 V245 S308 T337 V314 T338 S255 V282 T336
+V311 V315 S284 V246 Y256 V312 V283 S316 V250 S248 V247 V249 S313 V329 S286 S285 S252 S251 V320 V288 S287 V318 V324 S323 V321
+S322 V253 S319 V289 S325 V326 S297 V296 V327 S291 T334 V290 S330 T332 S328 V205 T333 T335 S346 T340 S344 V358 T341 V345 S347
+T343 T342 V359 S352 V351 V363 S362 V361 S360 V354 S353 V348 S364 S365 S331 V355 V366 T356 T349 V367 S357 S350 V368 V369 S370
+V372 S371 Y374 Y373 Y379 S376 Y375 S377 Y378
+"""
 
 
 def rank_program(g, core, T, topo):
     N, cores = len(T.cores), T.cores
-    WAKE, LOOK = EST["wake"], EST["look"]
     owner, first, second, third = {}, {}, {}, {}
     for c in cores:
         free_ = [h for h in topo.cores_of(c) if h not in cores and h not in owner and topo.die(h) == topo.die(c)]
@@ -117,7 +129,7 @@ def rank_program(g, core, T, topo):
         way, src, dst = {first[me]: (even(rest, True), "hls", "lls"), second[me]: (even(plane, False), "hlc", "ll"),
                          third[me]: (even(plane, False), "hls", "lls")}[core]
         g.wait_ge(T.sem.hop, half)
-        g.remote_dma_fused(blocks(way, src, 0, dst, 256, "arr1"), local_sem=T.sem.sent)
+        g.remote_dma_fused(blocks(way, src, 0, dst, 128, "arr1"), local_sem=T.sem.sent)
         g.wait_ge(T.sem.sent, engines(way))
         return
 
@@ -171,8 +183,8 @@ def rank_program(g, core, T, topo):
     def views(xs):
         return [x for x in xs if isinstance(x, tuple)]
 
-    def add(outs, ins, emit, cost, late=0.0, after=()):
-        e, outs, ins = "".join(cost), views(outs), views(ins)
+    def add(outs, ins, emit, e, after=()):
+        outs, ins = views(outs), views(ins)
         i, deps = len(ops), set(after)
         for x in ins:
             psum = SCRATCH[x[1]][0] == "psum"
@@ -183,10 +195,10 @@ def rank_program(g, core, T, topo):
             seen.setdefault(x[1], []).append((x, i, True, e))
         for x in ins:
             seen.setdefault(x[1], []).append((x, i, False, e))
-        ops.append((emit, cost, late, sorted(deps)))
+        ops.append((emit, e, 0, sorted(deps)))
         return i
 
-    def run(outs, ins, call, cost):
+    def run(outs, ins, call, es):
         outs, ins = views(outs), views(ins)
 
         def emit(e):
@@ -197,57 +209,17 @@ def rank_program(g, core, T, topo):
             total[tok[0]] = count[e]
             snap[tok] = dict(known[e])
             note(e, outs, ins, tok)
-        return add(outs, ins, emit, cost)
+        return add(outs, ins, emit, es)
 
     def schedule():
-        n = len(ops)
-        users = [[] for _ in ops]
-        for i, o in enumerate(ops):
-            for j in o[3]:
-                users[j].append(i)
-
-        def gap(i, j):
-            return 0.0 if "T" in ops[i][1] and "T" in ops[j][1] else WAKE
-        way = [0.0] * n
-        for i in range(n - 1, -1, -1):
-            way[i] = min(ops[i][1].values()) + ops[i][2] + max([way[j] + gap(i, j) for j in users[i]] + [0.0])
-        left, end, free = [len(o[3]) for o in ops], [0.0] * n, {}
-        ready = {i: 0.0 for i in range(n) if not left[i]}
-        when = []
-        while ready:
-            best = None
-            for e in "RVSTGY":
-                c = [(s, i) for i, s in ready.items() if e in ops[i][1]]
-                if not c:
-                    continue
-                t = free.get(e, 0.0)
-                if e == "R":
-                    x, t = min(c), 0.0
-                elif e == "G":
-                    x = min(c, key=lambda y: y[1])
-                else:
-                    t0 = max(t, min(c)[0])
-                    x = max([y for y in c if y[0] <= t0 + LOOK], key=lambda y: (way[y[1]] - max(0.0, y[0] - t0), -y[1]))
-                    if x[0] > t0:
-                        fit = [y for y in c if max(t, y[0]) + ops[y[1]][1][e] <= x[0]]
-                        if fit:
-                            x = max(fit, key=lambda y: (way[y[1]], -y[1]))
-                s = max(t, x[0])
-                z = s + ops[x[1]][1][e]
-                if best is None or (s, z) < best[:2]:
-                    best = (s, z, e, x[1])
-            s, z, e, i = best
-            end[i] = z + ops[i][2]
-            free[e] = z
-            when.append((s, len(when), e, i))
-            del ready[i]
-            for j in users[i]:
-                left[j] -= 1
-                if not left[j]:
-                    ready[j] = max(end[m] + gap(m, j) for m in ops[j][3])
+        when = [(0, 0, x[0], int(x[1:])) for x in ORDER.split()]
+        done = set()
         for s, k, e, i in when:
+            assert e in ops[i][1] and done.issuperset(ops[i][3])
+            done.add(i)
             if e != "R":
                 ops[i][0](e)
+        assert len(done) == len(ops)
 
     def val(x):
         return x[0] if isinstance(x, tuple) else x
@@ -262,90 +234,94 @@ def rank_program(g, core, T, topo):
             total[sem] = 16 * len(moves)
             snap[(sem, total[sem])] = dict(known[e])
             note("D" + sem, outs, ins, (sem, total[sem]))
-        add(outs, ins, emit, {e: 60.0 * len(moves) for e in es}, EST["load"])
-
-    def vec(x, a=1.0, o=None):
-        two = SCRATCH[x[1]][2] in (BF16, U16) and (o is None or SCRATCH[o[1]][2] in (BF16, U16))
-        return max(64, a * x[7] * (0.5 if two else 1)) * EST["cycle"]
+        add(outs, ins, emit, es)
 
     def ts(out, a, s1, op0, s2=None, op1=None):
-        if op1 is None:
-            run([out], [a, s1], lambda e: g.vector.tensor_scalar(out[0], a[0], val(s1), None, op0), {"V": vec(a, 1, out)})
-        else:
-            run([out], [a, s1, s2], lambda e: g.vector.tensor_scalar(out[0], a[0], val(s1), val(s2), op0, op1), {"V": vec(a, 1, out)})
+        plain = all(SCRATCH[x[1]][2] in (F32, BF16) for x in (out, a)) and all(SCRATCH[x[1]][2] == F32 for x in views([s1, s2]))
+        either = plain and (op0, op1) in ((OP.mult, None), (OP.add, None), (OP.mult, OP.add))
+        b, c = (1.0, s1) if op0 == OP.add else (s1, 0.0 if op1 is None else s2)
+
+        def call(e):
+            if e == "S":
+                return g.scalar.activation(out[0], a[0], AF.Identity, bias=c[0] if isinstance(c, tuple) else float(c),
+                                           scale=b[0] if isinstance(b, tuple) else float(b))
+            if op1 is None:
+                return g.vector.tensor_scalar(out[0], a[0], val(s1), None, op0)
+            return g.vector.tensor_scalar(out[0], a[0], val(s1), val(s2), op0, op1)
+        run([out], [a, s1, s2], call, "VS" if either else "V")
 
     def tt(out, a, b, op):
-        run([out], [a, b], lambda e: g.vector.tensor_tensor(out[0], a[0], b[0], op), {"V": vec(a, 1 if a[1] in ("pn", "pm") else 2)})
+        run([out], [a, b], lambda e: g.vector.tensor_tensor(out[0], a[0], b[0], op), "V")
 
     def act(out, a, func, scale=1.0, bias=0.0, acc=None):
-        c = max(64, a[7]) * EST["cycle"]
         if acc is None:
-            run([out], [a, bias, scale], lambda e: g.scalar.activation(out[0], a[0], func, bias=val(bias), scale=val(scale)), {"S": c})
+            run([out], [a, bias, scale], lambda e: g.scalar.activation(out[0], a[0], func, bias=val(bias), scale=val(scale)), "S")
         else:
-            run([out, acc], [a, bias], lambda e: g.scalar.activation(out[0], a[0], func, bias=val(bias), scale=scale, accum_out=acc[0]), {"S": c + 20})
+            run([out, acc], [a, bias], lambda e: g.scalar.activation(out[0], a[0], func, bias=val(bias), scale=scale, accum_out=acc[0]), "S")
 
     def cp(out, a, es="V"):
         def call(e):
             if e == "V":
                 return g.vector.tensor_copy(out[0], a[0])
             return g.scalar.activation(out[0], a[0], AF.Copy)
-        run([out], [a], call, {e: vec(a, 1, out) for e in es})
-
-    def shift(out, a, c):
-        def call(e):
-            if e == "V":
-                return g.vector.tensor_scalar(out[0], a[0], c, None, OP.add)
-            return g.scalar.activation(out[0], a[0], AF.Identity, bias=c)
-        run([out], [a], call, {e: vec(a) for e in "VS"})
+        run([out], [a], call, es)
 
     def fill(out, c):
-        run([out], [], lambda e: g.vector.memset(out[0], c), {"V": vec(out)})
+        run([out], [], lambda e: g.vector.memset(out[0], c), "V")
 
     def red(out, a, op):
-        run([out], [a], lambda e: g.vector.tensor_reduce(out[0], a[0], AxisListType.X, op), {"V": max(64, a[7]) * EST["cycle"]})
+        if op == OP.add:
+            run([out, a], [a], lambda e: g.vector.tensor_reduce(out[0], a[0], AxisListType.X, op) if e == "V" else
+                g.scalar.activation(a[0], a[0], AF.Copy, accum_out=out[0]), "VS")
+        else:
+            run([out], [a], lambda e: g.vector.tensor_reduce(out[0], a[0], AxisListType.X, op), "V")
 
     def turn(out, a):
-        run([out], [a], lambda e: g.vector.transpose(out[0], a[0]), {"V": vec(a)})
+        run([out], [a], lambda e: g.vector.transpose(out[0], a[0]), "V")
 
     def scan(z, q, op=OP.add):
         s = v("smb" if SCRATCH[q[1]][2] == BF16 else "sm", 0, q[7])
-        run([z], [q, s], lambda e: g.vector.tensor_tensor_scan(z[0], s[0], q[0], 0.0, OP.mult, op), {"V": vec(q)})
+        run([z], [q, s], lambda e: g.vector.tensor_tensor_scan(z[0], s[0], q[0], 0.0, OP.mult, op), "V")
 
     def quant(q, s, a):
-        run([q, s], [a], lambda e: g.vector.quantize_mx(q[0], s[0], a[0]), {"V": (12 + 0.22 * a[7]) * EST["cycle"] / 0.83})
+        run([q, s], [a], lambda e: g.vector.quantize_mx(q[0], s[0], a[0]), "V")
 
     def mm(out, a, asc, b, bsc, start=True, stop=True):
-        run([out], [a, asc, b, bsc], lambda e: g.tensor.matmul_mx(out[0], a[0], asc[0], b[0], bsc[0], start, stop), {"T": EST["tens"] * b[7] / 128})
+        run([out], [a, asc, b, bsc], lambda e: g.tensor.matmul_mx(out[0], a[0], asc[0], b[0], bsc[0], start, stop), "T")
 
-    def by_list(out):
-        return 60 + 1.25 * out[7]
-
-    def gather(out, win, off, es="S"):
+    def gather(out, win, off, es="SV"):
         def call(e):
             if e == "V":
                 return g.vector.tensor_copy(out[0], win[0].indirect(off[0]))
             return g.scalar.activation(out[0], win[0].indirect(off[0]), AF.Copy)
-        run([out], [win, off], call, {e: by_list(out) for e in es})
+        run([out], [win, off], call, es)
 
     def choose(out, win, off, m, op=OP.mult):
-        run([out], [win, off, m], lambda e: g.vector.tensor_tensor(out[0], win[0].indirect(off[0]), m[0], op), {"V": by_list(out)})
+        run([out], [win, off, m], lambda e: g.vector.tensor_tensor(out[0], win[0].indirect(off[0]), m[0], op), "V")
 
     def under(out, win, off, a, b):
-        run([out], [win, off, a, b], lambda e: g.vector.tensor_scalar(out[0], win[0].indirect(off[0]), a[0], b[0], OP.max, OP.is_lt),
-            {"V": by_list(out)})
+        run([out], [win, off, a, b], lambda e: g.vector.tensor_scalar(out[0], win[0].indirect(off[0]), a[0], b[0], OP.max, OP.is_lt), "V")
 
-    def pick(oq, os, oa, ob, iq, isc, ia, ib, off, es="S"):
-        o, w = v(oq, oa, ob), v(iq, ia, ib)
-        run([o], [w, off], lambda e: g.vector.tensor_copy(o[0].bitcast(dt.uint32), w[0].bitcast(dt.uint32).indirect(off[0])), {"V": by_list(o)})
-        gather(v(os, oa, ob), v(isc, ia, ib), off, es)
+    def listed(out, win, off, a, b):
+        run([out], [win, off, a, b], lambda e: g.vector.tensor_scalar(out[0], win[0].indirect(off[0]), val(a), val(b), OP.mult, OP.add) if e == "V"
+            else g.scalar.activation(out[0], win[0].indirect(off[0]), AF.Identity, bias=val(b), scale=val(a)), "VS")
+
+    def codes(o, w, off):
+        run([o], [w, off], lambda e: g.vector.tensor_copy(o[0].bitcast(dt.uint32), w[0].bitcast(dt.uint32).indirect(off[0])), "V")
+
+    def pick(oq, os, oa, ob, iq, isc, ia, ib, off):
+        codes(v(oq, oa, ob), v(iq, ia, ib), off)
+        gather(v(os, oa, ob), v(isc, ia, ib), off)
 
     def iota(out, pattern, base, cm, flag=True):
-        run([out], [], lambda e: g.iota(out[0], pattern, base, cm, allow_small_or_imprecise_dtypes=True) if flag else g.iota(out[0], pattern, base, cm),
-            {"G": 130 + 1.66 * out[7]})
+        run([out], [], lambda e: g.iota(out[0], pattern, base, cm, allow_small_or_imprecise_dtypes=True) if flag else g.iota(out[0], pattern, base, cm), "G")
 
     def wrap(tag, raised, a, b, op, out, *last):
         name = "qs" + tag
-        ts(v("qz" + tag), v(raised), a, OP.add, b, op)
+        if b is None:
+            ts(v("qz" + tag), v(raised), a, OP.mult)
+        else:
+            ts(v("qz" + tag), v(raised), a, OP.add, b, op)
         turn(v("qt" + tag), v("qz" + tag))
         scan(v(name), v("qt" + tag), OP.max)
         for d in range(4):
@@ -360,9 +336,6 @@ def rank_program(g, core, T, topo):
 
     def fc(k):
         return v("fcol", k, k + 1)
-
-    def kf(k):
-        return v("kf", 8 * k, 8 * k + 8, 1, 0, 32)
 
     def km(k):
         return v("km", 8 * k, 8 * k + 8, 1, 0, 32)
@@ -385,106 +358,100 @@ def rank_program(g, core, T, topo):
     iota(ic(0), [[0, 1]], 0, 1, False)
     iota(v("kb"), [[1, 256]], 0, 0)
     iota(v("n16"), [[0, 8], [1, 16]], 0, 0)
-    iota(v("lf"), [[0, 32]], 0, 0)
+    iota(v("kbh"), [[1, 128]], 0, 0)
+    iota(v("kb1"), [[1, 128]], 1, 0)
     iota(v("nbp"), [[0, 128]], 0, 0)
     iota(v("pa", 128, 256), [[0, 128]], -1, 0)
-    iota(v("ks"), [[-1, 3], [0, 128]], 2, 0)
     fill(v("et", 0, 260), 0.0)
     fill(v("et", 260, 520), 0.0)
-    fill(v("cl"), 0)
-    fill(v("mq"), 0.0)
-    fill(v("inv"), 0.0)
-    fill(v("sgn", 128, 408, 136, 0, 32), -127.0)
+    fill(v("dt1", 0, 8), 1.0)
+    fill(v("posn"), 0.0)
+    fill(v("ry"), 0.0)
+    fill(v("fcol", 48, 64), 0.0)
+    for d in range(N):
+        fill(v("fcol", 48 + 8 * (d % 2) + (d ^ r), 49 + 8 * (d % 2) + (d ^ r), 1, 32 * (d // 2), 32 * (d // 2) + 32), 1.0)
     for t in "01":
-        fill(v("lt" + t, 0, 32), 0.0)
+        fill(v("lt" + t, 0, 4), 0.0)
     cp(fc(0), ic(0))
     ts(ic(3), ic(0), 15, OP.bitwise_and)
     cp(fc(2), ic(3))
-    ts(fc(4), ic(3), 128 * r, OP.add)
-    ts(fc(5), ic(3), 1.0 / 4096, OP.mult)
+    ts(fc(6), ic(3), 0.5, OP.add)
     ts(v("eye"), v("kb", 0, 128), fc(0), OP.is_equal)
     act(v("et", 4, 516, 4), v("eye"), AF.Copy, 0.5)
-    units = [(v("eq", 128 * b, 128 * b + 128), v("es", 128 * b, 128 * b + 128)) for b in range(3)] + [(v("ll", 0, 128), v("lls", 0, 128))]
+    units = [(v("eq", 128 * b, 128 * b + 128), v("es", 128 * b, 128 * b + 128)) for b in range(4)]
     for b in range(4):
         quant(units[b][0], units[b][1], v("et", 4 - b, 516 - b))
+    for d in range(4):
+        cp(v("kbr", 0, 128 - 32 * d, 1, 32 * d, 32 * d + 32), v("kb", 32 * d, 128, 1, 32 * d, 32 * d + 32), "VS")
+        if d:
+            cp(v("kbr", 128 - 32 * d, 128, 1, 32 * d, 32 * d + 32), v("kb", 0, 32 * d, 1, 32 * d, 32 * d + 32), "VS")
     act(v("sm"), v("n16"), AF.Sign)
-    for h in range(2):
-        act(v("smb", 128 * h, 128 * h + 128), v("n16"), AF.Sign)
-    act(v("kbh"), v("kb", 0, 128), AF.Copy)
-    act(v("kb1"), v("kb", 0, 128), AF.Identity, 1.0, 1.0)
+    act(v("smb"), v("n16"), AF.Sign)
     ts(v("wm"), v("n16"), fc(2), OP.is_equal)
-    for h in range(2):
-        act(v("wmh", 128 * h, 128 * h + 128), v("wm"), AF.Copy)
+    act(v("wmh"), v("wm"), AF.Copy)
     act(v("wmb"), v("wm"), AF.Copy, 128.0)
     ts(ic(5), ic(0), 4, OP.arith_shift_right)
     ts(fc(15), ic(5), 0.125, OP.mult, 5, OP.add)
     act(v("wmc"), v("wm"), AF.Copy, fc(15))
     ts(fc(17), fc(2), -512, OP.add)
-    ts(fc(18), fc(0), 1.0 / 128, OP.mult, 1, OP.add)
-    act(v("cw"), v("kb", 0, 32), AF.Identity, 0.0, fc(18))
-    ts(fc(1), ic(0), 1, OP.add)
-    ts(fc(32), ic(5), 0, OP.is_gt, 31, OP.mult)
-    ts(v("gol", 0, 1), ic(5), fc(32), OP.add)
-    ts(v("idl"), v("kb", 0, 8), 16, OP.mult, fc(2), OP.add)
-    cp(v("pcl", 0, 1), ic(0))
-    ts(ic(4), ic(0), 1, OP.bitwise_and)
-    ts(fc(13), ic(4), -2, OP.mult, fc(2), OP.add)
-    ts(v("swl", 0, 1), fc(13), 1, OP.add)
     ts(ic(6), ic(0), 5, OP.arith_shift_right)
     ts(fc(14), ic(6), -32, OP.mult, 128, OP.add)
+    ts(fc(18), fc(0), 1.0 / 16384, OP.mult)
+    ts(fc(7), fc(14), -1, OP.mult, 128, OP.add)
+    ts(v("cw"), v("kb", 0, 32), fc(7), OP.add)
+    ts(fc(32), ic(5), 0, OP.is_gt, 3, OP.mult)
+    ts(v("gol", 0, 1), ic(5), fc(32), OP.add)
+    ts(fc(35), ic(5), fc(32), OP.add)
+    ts(v("gol", 4, 6), v("kb", 0, 2), 0, OP.mult, fc(35), OP.add)
+    ts(fc(33), ic(5), 0, OP.is_gt, 7, OP.mult)
+    ts(fc(34), ic(5), fc(33), OP.add)
+    ts(v("gol", 2, 4), v("kb", 0, 2), 0, OP.mult, fc(34), OP.add)
+    ts(fc(9), ic(5), 16, OP.mult)
+    ts(v("idl"), v("kb", 0, 8), 16, OP.mult, fc(2), OP.add)
+    ts(ic(4), ic(0), 4, OP.arith_shift_right, 1, OP.bitwise_and)
+    cp(fc(8), ic(4))
+    ts(v("fcol", 10, 12), v("kb", 0, 2), fc(8), OP.is_equal)
+    ts(v("fcol", 12, 14), v("kb", 0, 256, 128), 2, OP.mult, 128, OP.add)
 
-    wide = max(256 * r + 128, 128 * (N + r)) if r < N - 1 else 256 * r + 128
-    for q in range(N):
-        a, b = 128 * (q + min(q, r)), 256 if q < r else 128
-        shift(v("kt", a, a + b), v("kb", 0, b), float(a + 2048 * (q ^ r)))
-    low = v("kb", 0, 8, 1, 0, 32)
-    ts(kf(0), low, 16, OP.mult, v("fcol", 4, 5, 1, 0, 32), OP.add)
-    ts(kf(1), low, 1.0 / 256, OP.mult, v("fcol", 5, 6, 1, 0, 32), OP.add)
-    act(v("frr"), v("kb", 0, 128), AF.Copy, 1.0 / 256)
     ends = v("nl", 48, 72, 3, 0, 32)
-    ts(km(1), ends, 128 * (N - 1), OP.bitwise_and)
-    tt(kf(2), ends, kf(0), OP.min)
-    ts(km(2), ends, 128 * r, OP.bitwise_and)
-    tt(kf(3), km(1), kf(2), OP.add)
-    ts(kf(4), km(2), -32, OP.mult, 2048 * r, OP.add)
-    tt(kf(8), km(1), kf(1), OP.add)
-    cp(v("cl", 0, 8, 1, 0, 32), kf(3))
-    tt(kf(5), kf(4), kf(3), OP.add)
-    ts(kf(9), kf(8), 16, OP.mult)
-    tt(kf(6), kf(5), kf(9), OP.add)
-    choose(v("rk"), v("kt", 0, wide), v("cl"), v("frr"), OP.add)
-    keys = v("rk", 0, 128, 1, 0, 32)
-    for c in range(5):
-        act(v("sgs", 128 * c, 128 * c + 128, 1, 0, 32), keys, AF.Sign, -1.0, v("kf", 48 + c, 49 + c, 1, 0, 32), v("kf", 56 + c, 57 + c, 1, 0, 32))
-    for c in range(3):
-        ts(v("sgn", 136 * c, 136 * c + 128, 1, 0, 32), keys, v("kf", 53 + c, 54 + c, 1, 0, 32), OP.is_lt, 2, OP.mult)
-    for c in range(3):
-        red(v("kf", 61 + c, 62 + c, 1, 0, 32), v("sgn", 136 * c, 136 * c + 129, 1, 0, 32), OP.add)
     for q in range(4):
-        ts(v("pol", 0, 8, 1, 32 * q, 32 * q + 32), kf(7), 127, OP.add, 0.5, OP.mult)
+        ts(v("clq", 0, 8, 1, 32 * q, 32 * q + 32), ends, 1.0 / 128, OP.mult, -63.5 / 128, OP.add)
+    for h in range(2):
+        m, c = v("xm", 128 * h, 128 * h + 128), v("xs", 128 * h, 128 * h + 128)
+        gather(m, v("fcol", 48 + 8 * h, 56 + 8 * h), v("clq"))
+        run([c], [m], lambda e, m=m, c=c: g.vector.tensor_tensor_scan(c[0], m[0], m[0], 0.0, OP.add, OP.max), "V")
+        act(v("sgs", 128 * h, 128 * h + 128), c, AF.Sign, -1.0, fc(6), v("kf", 64 + h, 65 + h))
+    for a in range(4):
+        for b in (a, a ^ 1):
+            cp(v("kf", 72 + 2 * a, 74 + 2 * a, 1, 32 * b, 32 * b + 32), v("kf", 64, 66, 1, 32 * a, 32 * a + 32), "VS")
+    cp(v("kf", 76, 80, 1, 0, 64), v("kf", 76, 80, 1, 64, 128), "VS")
+    cp(v("kf", 72, 76, 1, 64, 128), v("kf", 72, 76, 1, 0, 64), "VS")
+    ts(v("pl", 0, 8), v("kf", 72, 80), 128, OP.add, 0.5, OP.mult)
     quant(v("q0"), v("q0s"), v("xt", 0, 512))
-    run([v("inv")], [v("kb", 0, 128), v("pol")],
-        lambda e: g.vector.tensor_copy(T.inv[:, 0:128].indirect(T.pol[:, 0:8]), T.kb[:, 0:128]), {"V": 400.0})
-    choose(v("invm"), v("inv"), v("idl"), v("wmh", 0, 128))
-    scan(v("invs"), v("invm"))
-    cp(v("pl", 0, 8), v("invs", 15, 128, 16))
     pick("w0", "ws0", 128, 256, "q0", "q0s", 0, 128, v("pl", 0, 8))
+    pick("ll", "lls", 0, 16, "q0", "q0s", 0, 128, v("pl", 0, 1))
+    run([v("posn")], [v("kb", 0, 128), v("pl", 0, 8)],
+        lambda e: g.vector.tensor_copy(T.posn[:, 0:128].indirect(T.pl[:, 0:8]), T.kb[:, 0:128]), "V")
+    gather(v("inv"), v("kb", 0, 128), v("pl", 0, 8))
+    choose(v("invm"), v("posn"), v("idl"), v("wmh", 0, 128))
+    scan(v("invs"), v("invm"))
+    cp(v("pol"), v("invs", 15, 128, 16))
 
-    def post(srcs, tr, leave, land=None, flight=0.0):
+    def post(srcs, tr, leave, land=None):
         def emit(e):
             order("G", [], srcs)
             g.remote_dma_fused(tr, local_sem=T.sem.sent)
             total["sent"] = total.get("sent", 0) + leave
-        i = add([], srcs, emit, {"G": EST["issue"]})
+        i = add([], srcs, emit, "G")
         if land is not None:
-            add([land], [], None, {"R": 0.0}, flight, (i,))
+            add([land], [], None, "R", (i,))
 
-    def send_col(name, c0, dst, d0, sem, flight):
+    def send_col(name, c0, dst, d0, sem):
         tr = []
         for who, es in ((far, lanes), (near, inside)):
             tr.append(RemoteDMATransfer(dst_ids=[dest(c) for d, c in who], dma_engine_mask=bits(es), remote_sem=T.sem[sem],
                                         srcs=[T[name][:, c0:c0 + 1]], dsts=[T[dst][:, d0 + d:d0 + d + 1] for d, c in who]))
-        post([v(name, c0, c0 + 1)], tr, len(lanes) + len(inside), v(dst, d0 + 1, d0 + 8), flight)
+        post([v(name, c0, c0 + 1)], tr, len(lanes) + len(inside), v(dst, d0 + 1, d0 + 8))
 
     def send_merged():
         a, b = 16 * plane[0][0], 16 * plane[-1][0] + 16
@@ -492,35 +459,41 @@ def rank_program(g, core, T, topo):
                                 srcs=[T.ws0[:, 256:256 + 4 * (b - a)]], dsts=[T.hls[:, 0:4 * (b - a)]] * 2),
               RemoteDMATransfer(dst_ids=[dest(second[core])], dma_engine_mask=bits(others[half:]), remote_sem=T.sem.hop,
                                 src=T.w0[:, 256 + a:256 + b].bitcast(dt.uint8), dst=T.hlc[:, a:b].bitcast(dt.uint8))]
-        post([v("ws0", 256, 384), v("w0", 256, 384)], tr, len(others), v("lls", 272, 384), EST["hop"])
-        post([v("w0", 256, 384)], blocks(even(rest, True), "w0", 256, "ll", 256, "arr1"), engines(even(rest, True)), v("ll", 272, 384), EST["merged"])
+        post([v("ws0", 256, 384), v("w0", 256, 384)], tr, len(others), v("lls", 144, 256))
+        post([v("w0", 256, 384)], blocks(even(rest, True), "w0", 256, "ll", 128, "arr1"), engines(even(rest, True)), v("ll", 144, 256))
 
     few = len(far) * len(lanes) + len(near) * len(inside)
     total["arr0"] = engines(ways[0]) + engines(ways[1])
     total["arr1"] = 2 * engines(even(rest, True)) + 2 * engines(even(plane, False))
-    total["thd"] = engines(even(rest, True)) + engines(even(plane, False))
-    total["thr0"] = total["thr1"] = few
+    total["thr0"] = total["thr1"] = total["thd"] = few
     for t in range(2):
-        note("R", [v("ll", 128 * t + 144, 128 * t + 256), v("lls", 128 * t + 144, 128 * t + 256)], [], ("arr%d" % t, total["arr%d" % t]))
-        note("R", [v("lt%d" % t, 32, 39)], [], ("thr%d" % t, few))
-    note("R", [v("dl", 0, 7)], [], ("thd", total["thd"]))
+        note("R", [v("ll", 128 * t + 16, 128 * t + 128), v("lls", 128 * t + 16, 128 * t + 128)], [], ("arr%d" % t, total["arr%d" % t]))
+        note("R", [v("lt%d" % t, 4, 11)], [], ("thr%d" % t, few))
+    note("R", [v("dt1", 8, 15)], [], ("thd", few))
 
     def bank(k, n=128):
         return v("pn" if k < 4 else "pm", 512 * (k % 4), 512 * (k % 4) + n)
 
-    def score(t, k, b, m, bias=None, at=None):
-        at = k if at is None else at
-        x, out = v("ex" + t, 128 * at, 128 * at + 128), v("sc" + t, k, k + 1)
-        tt(x, bank(b), v(m), OP.mult)
+    def score(t, k, b, m, bias=None):
+        x, out = v("ex" + t, 128 * k, 128 * k + 128), v("sc" + t, k, k + 1)
+        tt(x, bank(b), v(m, 0, 128), OP.mult)
         if bias is None:
             act(x, x, AF.Copy, acc=out)
         else:
             act(x, x, AF.Identity, bias=bias, acc=out)
 
-    def both(a, b0, b1, out, bias):
-        tt(v("ex1", a, a + 128), bank(b0), v("ma"), OP.mult)
-        tt(v("ex1", a + 128, a + 256), bank(b1), v("mb"), OP.mult)
-        act(v("ex1", a, a + 256), v("ex1", a, a + 256), AF.Identity, bias=bias, acc=out)
+    def spread(row, col):
+        turn(v(row, 0, 32), v(col))
+        for d in range(4):
+            x = (d + 1) % 4
+            cp(v(row, 32, 64, 1, 32 * d, 32 * d + 32), v(row, 0, 32, 1, 32 * x, 32 * x + 32), "VS")
+        cp(v(row, 64, 128, 1, 0, 64), v(row, 0, 64, 1, 64, 128), "VS")
+        cp(v(row, 64, 128, 1, 64, 128), v(row, 0, 64, 1, 0, 64), "VS")
+
+    def across(out, a, b):
+        ts(v("mq", 64, 96), v("mx0"), a, OP.max, b, OP.max)
+        turn(v("mq", 96, 128), v("mq", 64, 96))
+        red(out, v("mq", 96, 128), OP.min)
 
     def halves(m, s, banks, start):
         for b in range(4):
@@ -538,11 +511,11 @@ def rank_program(g, core, T, topo):
         cp(v("ya", a, a + 128), bank(k), "VS")
 
     n0, n1 = v("ns", 15, 16), v("ns", 31, 32)
-    low4, mixed = (0, 1, 2, 3), (7, 5, 6, 4)
+    low4, mixed = (0, 1, 2, 3), (7, 6, 4, 5)
     for t in "01":
         W, WS = v("w" + t, 128, 256), v("ws" + t, 128, 256)
         G, GS = v("g" + t), v("gs" + t)
-        L, LS = (v("ll", 128, 256), v("lls", 128, 256)) if t == "0" else (v("l1"), v("l1s"))
+        L, LS = (v("la"), v("las")) if t == "0" else (v("l1"), v("l1s"))
 
         def s_(a):
             return v("sc" + t, a, a + 1)
@@ -550,35 +523,66 @@ def rank_program(g, core, T, topo):
         def pen(a):
             return v("pen" + t, a, a + 1)
 
-        mb, mx = 32 * int(t), "mx" + t
-        best = v("mq", mb, mb + 1)
+        best = v("mq", 32 * int(t), 32 * int(t) + 1)
         if t == "0":
-            post([W], blocks(ways[0], "w0", 128, "ll", 128, "arr0"), engines(ways[0]), v("ll", 144, 256), EST["flight"])
-            post([WS], blocks(ways[1], "ws0", 128, "lls", 128, "arr0"), engines(ways[1]), v("lls", 144, 256), EST["scales"])
+            post([W], blocks(ways[0], "w0", 128, "ll", 0, "arr0"), engines(ways[0]), v("ll", 16, 128))
+            post([WS], blocks(ways[1], "ws0", 128, "lls", 0, "arr0"), engines(ways[1]), v("lls", 16, 128))
             ts(v("lf", 0, 24, 1, 0, 32), v("nl", 0, 72, 3, 0, 32), 0, OP.add)
-            cp(v("lf", 0, 16, 1, 32, 64), v("lf", 0, 16, 1, 0, 32), "S")
-            cp(v("lf", 0, 16, 1, 64, 128), v("lf", 0, 16, 1, 0, 64), "S")
-            ts(v("nlu"), v("lf", 0, 16), -128 * r, OP.add)
-            gather(v("posn"), v("kb", 0, 128), v("pol"))
-            gather(v("npos"), v("posn"), v("nlu"))
-            choose(v("iv", 0, 16), v("inv"), v("pcl", 0, 1), v("wmh", 0, 16))
-            red(fc(40), v("iv", 0, 16), OP.add)
-            ts(v("il", 0, 2), v("kb", 0, 256, 128), fc(40), OP.add)
+            ts(km(2), ends, 127, OP.bitwise_and)
+            ts(v("lf", 24, 32, 1, 0, 32), km(2), 128 * r, OP.add)
+            cp(v("lf", 0, 32, 1, 32, 64), v("lf", 0, 32, 1, 0, 32), "S")
+            cp(v("lf", 0, 32, 1, 64, 128), v("lf", 0, 32, 1, 0, 64), "S")
+            ts(v("nlu"), v("lf"), -128 * r, OP.add)
+            gather(v("npos"), v("kb", 0, 128), v("nlu", 0, 16))
+            gather(v("rk"), v("kb", 0, 128), v("nlu", 24, 32))
+            tt(v("kf", 66, 68), v("kf", 64, 66), v("fcol", 10, 12), OP.mult)
+            red(fc(40), v("kf", 66, 68), OP.add)
+            ts(v("il", 0, 2), v("fcol", 12, 14), fc(40), OP.add, 0.5, OP.mult)
+            ts(fc(1), fc(40), 0.5, OP.mult, 65, OP.add)
+            gather(v("mq", 40, 56), v("rk"), v("il", 0, 1))
+            choose(v("iv", 16, 32), v("rk"), v("il", 0, 1), v("wmh", 0, 16))
+            red(fc(46), v("iv", 16, 32), OP.add)
+            ts(v("iv", 0, 16), v("mq", 40, 56), fc(46), OP.is_lt)
+            red(fc(47), v("iv", 0, 16), OP.add)
+            wrap("s", "wmb", fc(47), fc(9), OP.add, v("swl"), -128, OP.add)
+            ts(fc(45), fc(47), fc(9), OP.add)
+            ts(v("em"), v("kbh"), fc(45), OP.is_equal)
+            ts(v("mx1"), v("cw"), fc(9), OP.subtract, fc(47), OP.not_equal)
+            ts(v("mx0"), v("mx1"), 2 * BIG, OP.mult, -BIG, OP.add)
             choose(v("n32"), v("npos"), v("il", 0, 2), v("wmh", 0, 32))
-            scan(v("ns"), v("n32"))
-            ts(v("e0"), v("kbh"), n0, OP.is_equal)
-            ts(v("e1"), v("kbh"), n1, OP.is_equal)
-            ts(fc(41), n1, n0, OP.subtract)
-        mm(bank(4), W, WS, W, WS)
-        score(t, 0, 4, "e0", pen(0) if t == "1" else None)
-        score(t, 1, 4, "e1", pen(1) if t == "1" else None)
-        tt(best, s_(0), s_(1), OP.max)
-        send_col("mq", mb, "lt" + t, 31, "thr" + t, EST["way" + t])
-        ts(s_(8), s_(1), s_(0), OP.is_gt, fc(41), OP.mult)
-        wrap("b" + t, "wmb", s_(8), n0, OP.add, v("bl" + t), -128, OP.add)
-        pick("g" + t, "gs" + t, 0, 128, "w" + t, "ws" + t, 128, 256, v("bl" + t))
+        else:
+            cp(v("il", 2, 4), v("ns", 15, 32, 16))
+            choose(v("n32"), v("posn"), v("il", 2, 4), v("wmh", 0, 32))
+        scan(v("ns"), v("n32"))
+        ts(v("e0"), v("kbh", 0, 128), n0, OP.is_equal)
         if t == "0":
-            pick("ll", "lls", 128, 144, "w0", "ws0", 128, 256, v("swl", 0, 1))
+            ts(v("e1"), v("kbh", 0, 128), n1, OP.is_equal)
+        ts(fc(41), n1, n0, OP.subtract)
+        own = ("q0", "q0s", 0, 128) if t == "0" else ("w1", "ws1", 128, 256)
+        mm(bank(4), W, WS, v(own[0], *own[2:]), v(own[1], *own[2:]))
+        if t == "0":
+            score(t, 0, 4, "e0")
+            score(t, 1, 4, "e1")
+            across(v("lt0", 0, 1), s_(0), s_(1))
+            tt(best, s_(0), s_(1), OP.max)
+        else:
+            ts(fc(42), n0, n1, OP.add, -0.5, OP.mult)
+            act(fc(43), fc(41), AF.Abs, 0.5)
+            ts(fc(44), v("sc0", 10, 11), -0.5, OP.add, fc(41), OP.mult)
+            ts(fc(36), v("sc0", 11, 12), fc(44), OP.mult, fc(42), OP.add)
+            ts(fc(37), v("sc0", 11, 12), 0.5, OP.is_lt, fc(43), OP.mult)
+            act(v("fs"), v("kb", 0, 128), AF.Abs, 1.0, fc(36))
+            ts(v("rk"), v("fs"), fc(37), OP.not_equal, -BIG, OP.mult)
+            tt(v("ex1", 128, 256), bank(4), v("rk"), OP.add)
+            red(best, v("ex1", 128, 256), OP.max)
+            across(v("lt1", 0, 1), best, best)
+            score(t, 0, 4, "e0", pen(0))
+        send_col("lt" + t, 0, "lt" + t, 3, "thr" + t)
+        ts(s_(8), best if t == "1" else s_(1), s_(0), OP.is_gt, fc(41), OP.mult)
+        wrap("b" + t, "wmb", s_(8), n0, OP.add, v("bl" + t), -128, OP.add)
+        pick("g" + t, "gs" + t, 0, 128, *own, v("bl" + t))
+        if t == "0":
+            pick("la", "las", 0, 128, "ll", "lls", 0, 128, v("swl"))
             halves(W, WS, low4, True)
             halves(G, GS, low4, False)
             drain(t, 1, low4)
@@ -586,43 +590,38 @@ def rank_program(g, core, T, topo):
             send_merged()
             halves(W, WS, low4, True)
         else:
-            pick("l1", "l1s", 0, 16, "w1", "ws1", 128, 256, v("swl", 0, 1))
-            pick("l1", "l1s", 16, 128, "ll", "lls", 0, 384, v("dl", 0, 7))
-            with_w(5, 128)
+            pick("ll", "lls", 128, 144, "w1", "ws1", 128, 256, v("idl", 0, 1))
+            mm(bank(5), W, WS, v("ll", 0, 128), v("lls", 0, 128))
+            mm(bank(6), W, WS, v("ll", 128, 256), v("lls", 128, 256))
+            pick("l1", "l1s", 0, 128, "ll", "lls", 0, 256, v("dl"))
+            with_w(7, 128)
             halves(W, WS, low4, True)
-        ts(s_(10), s_(1), s_(0), OP.is_gt)
+        ts(s_(10), best if t == "1" else s_(1), s_(0), OP.is_gt)
         if t == "0":
             ts(s_(9), s_(8), n0, OP.add)
-            ts(v("mp"), v("kbh"), s_(9), OP.is_equal, fc(1), OP.mult)
+            ts(v("mp"), v("inv"), s_(9), OP.is_equal, fc(1), OP.mult)
             choose(v("mu"), v("kb1"), v("bl0"), v("mp"), OP.is_equal)
             act(v("sel"), v("mu"), AF.Identity, -BIG, BIG / 128, pen(3))
-            ts(v("pl", 8, 16), v("invs", 15, 128, 16), 128, OP.add)
-            choose(v("xm"), v("npos"), v("pl"), v("wmh"))
-            scan(v("xs"), v("xm"))
-            cp(v("xsl"), v("xs", 15, 256, 16))
+            run([v("ry")], [v("mu"), v("swl")], lambda e: g.vector.tensor_copy(T.ry[:, 0:128].indirect(T.swl[:, 0:8]), T.mu[:, 0:128]), "V")
         else:
-            G0, G1 = (v("gn", 0, 128), v("gns", 0, 128)), (v("gn", 128, 256), v("gns", 128, 256))
-            pick("gn", "gns", 0, 256, "w1", "ws1", 128, 256, v("xsl"))
-            mm(bank(6), *G0, *G1)
-            mm(bank(7), *G1, *G0)
-            score(t, 4, 6, "e0", None, 2)
-            score(t, 5, 7, "e1", None, 3)
-            ts(v("mp"), v("kbh"), n0, OP.subtract, s_(8), OP.is_equal)
-            choose(v("fm"), v("ks"), v("vl0"), v("mp"))
-            act(v("sel"), v("fm"), AF.Copy, acc=s_(13))
-            ts(s_(12), s_(0), s_(1), OP.is_ge)
-            ts(v("ma"), v("e0"), s_(12), OP.mult)
-            ts(v("mb"), v("e1"), s_(10), OP.mult)
-            ts(pen(5), s_(13), 2, OP.is_equal, -BIG, OP.mult)
-            ts(v("sc1", 18, 20), v("kb", 0, 2), s_(10), OP.is_equal, -512 * BIG, OP.mult)
-            ts(v("sc1", 20, 22), v("sc1", 18, 20), s_(13), OP.mult)
-            ts(s_(15), s_(4), best, OP.is_gt, s_(20), OP.mult)
-            ts(s_(16), s_(5), best, OP.is_ge, s_(21), OP.mult)
-            ts(s_(17), s_(15), s_(16), OP.add, best, OP.add)
-        turn(v(mx, 0, 32, 1, 0, 32), v("mq", mb, mb + 32, 1, 0, 32))
-        cp(v("mq", 64, 80, 2, 0, 32), v(mx, 1, 16, 2, 0, 32), "VS")
-        cp(v("mq", 65, 80, 2, 0, 32), v(mx, 0, 16, 2, 0, 32), "VS")
-        turn(v("lt" + t, 0, 32, 1, 0, 32), v("mq", 64, 96, 1, 0, 32))
+            score(t, 2, 5, "em", pen(2))
+            score(t, 3, 6, "em", pen(2))
+            ts(v("sc1", 12, 14), v("kb", 1, 3), s_(10), OP.add)
+            ts(s_(15), s_(2), best, OP.is_le, s_(12), OP.mult)
+            ts(s_(16), s_(3), best, OP.is_le, s_(12), OP.mult)
+            ts(s_(17), s_(16), s_(15), OP.subtract)
+            listed(v("zy"), v("dt1", 0, 15), v("gol", 2, 4), s_(17), s_(15))
+            ts(s_(18), v("mq", 8, 9), 128, OP.is_lt, s_(2), OP.mult)
+            ts(s_(19), v("mq", 8, 9), 128, OP.is_ge, s_(3), OP.mult)
+            ts(s_(20), s_(18), s_(19), OP.add)
+            ts(v("ma"), v("kbr"), n0, OP.subtract, s_(8), OP.is_equal)
+            ts(s_(14), v("zy", 0, 1), 0, OP.is_gt, s_(13), OP.mult)
+            ts(v("mb"), v("ma"), s_(14), OP.mult, -1, OP.add)
+            spread("ry", "zy")
+            choose(v("mp"), v("ry"), v("idl"), v("mb"), OP.is_equal)
+            act(v("sel"), v("mp"), AF.Identity, 1.0, fc(18), s_(11))
+            ts(s_(21), s_(20), best, OP.is_le, -4 * BIG, OP.mult)
+            ts(s_(22), s_(21), s_(20), OP.add)
         if t == "0":
             turn(v("lft", 0, 32, 1, 0, 32), v("lf", 0, 32, 1, 0, 32))
             dma("Y", "d_nbp", (v("nbp", 0, 128, 1, 0, 1), v("lft", 0, 16, 1, 16, 24)))
@@ -630,28 +629,27 @@ def rank_program(g, core, T, topo):
             act(v("gid"), v("inv"), AF.Identity, 1.0, float(128 * r))
             ts(v("sc0", 12, 14), v("kb", 0, 2), s_(10), OP.is_equal, -BIG, OP.mult)
             quant(v("wq"), v("wqs"), v("wt", 0, 512))
-            ts(v("oi", 0, 8), v("pol"), fc(14), OP.add)
-            ts(v("oi", 8, 16), v("oi", 0, 8), 127, OP.bitwise_and)
-            cp(v("ofl"), v("oi", 8, 16))
-        gather(v("pa", 256, 384), v("gid"), v("bl" + t))
-        if t == "0":
-            mm(bank(5), W, WS, L, LS)
-            mm(bank(6), G, GS, L, LS)
-            halves(L, LS, low4, False)
-            score(t, 2, 5, "eye")
-            score(t, 3, 6, "mu", pen(3))
-            ts(s_(11), s_(2), s_(3), OP.max, best, OP.is_le)
+            ts(v("km", 0, 8), v("pol"), fc(14), OP.add)
+            ts(v("km", 8, 16), v("km", 0, 8), 127, OP.bitwise_and)
+            cp(v("ofl"), v("km", 8, 16))
+            run([v("pa", 256, 384)], [v("kb1"), v("bl0")], lambda e: g.scalar.activation(
+                T.pa[:, 256:384], T.kb1[:, 0:128].indirect(T.bl0[:, 0:8]), AF.Identity, bias=float(128 * r - 1)), "S")
         else:
-            mm(bank(5), *G0, L, LS)
-            mm(bank(6), *G1, L, LS)
-            mm(bank(4), W, WS, L, LS)
+            gather(v("pa", 256, 384), v("gid"), v("bl1"))
+        if t == "0":
+            mm(bank(5), W, WS, v("ll", 0, 128), v("lls", 0, 128))
+            mm(bank(6), G, GS, v("ll", 0, 128), v("lls", 0, 128))
             halves(L, LS, low4, False)
-            both(640, 5, 6, s_(3), pen(5))
-            tt(v("ex1", 512, 640), bank(4), v("frr"), OP.add)
-            red(s_(2), v("ex1", 512, 640), OP.max)
-            ts(s_(11), s_(2), s_(3), OP.max, s_(17), OP.is_le)
-        under(v("cq" + t), v("lt" + t, 0, 39), v("gol", 0, 1), best, s_(2))
-        if t == "1":
+            score(t, 2, 5, "em")
+            score(t, 3, 6, "ry", pen(3))
+            ts(s_(11), s_(2), s_(3), OP.max, best, OP.is_le)
+            across(v("dsr", 0, 1), s_(11), s_(11))
+            send_col("dsr", 0, "dt1", 7, "thd")
+        else:
+            halves(L, LS, low4, False)
+        if t == "0":
+            under(v("cq0"), v("lt0", 0, 11), v("gol", 0, 1), best, s_(2))
+        else:
             halves(W, WS, mixed, True)
             halves(G, GS, mixed, False)
         drain(t, 0, low4)
@@ -659,11 +657,10 @@ def rank_program(g, core, T, topo):
         if t == "0":
             wrap("v0", "wmc", s_(11), v("cq0", 0, 1), OP.subtract, v("vl0"), 128, OP.mult, fc(17), OP.add)
             pick("w1", "ws1", 128, 256, "w0", "ws0", 0, 384, v("vl0"))
-            post([v("vl0")], blocks(even(rest, True), "vl0", 0, "dl", -1, "thd", 1), engines(even(rest, True)))
-            post([v("vl0")], blocks(even(plane, False), "vl0", 0, "dl", -1, "thd", 1), engines(even(plane, False)), v("dl", 0, 7), EST["list"])
             ts(v("pen1", 0, 2), v("sc0", 12, 14), s_(11), OP.mult)
-            ts(v("pen1", 2, 3), v("cq0", 0, 1), -BIG, OP.mult, BIG, OP.add)
-            ts(v("frr"), v("eye"), v("pen1", 2, 3), OP.mult, -BIG, OP.add)
+            ts(v("pen1", 2, 3), v("cq0", 0, 1), -BIG, OP.mult)
+            listed(v("mq", 8, 24), v("dt1", 0, 15), v("gol", 2, 3), 128.0, fc(45))
+            wrap("d", "wmh", v("mq", 8, 9), None, None, v("dl"), 0, OP.add)
             gather(v("prs0"), v("pa"), v("vl0"))
             gather(v("pro0"), v("prs0"), v("pol"))
             dma("Y", "d_p0", (T.pr[0:1, :], v("pro0", 0, 128, 1, 0, 1)))
@@ -672,27 +669,22 @@ def rank_program(g, core, T, topo):
     drain("1", 1, mixed)
     requant("1", 1)
     with_w(7, 256)
-    ts(v("zx"), v("cw"), v("sc1", 11, 12), OP.add, v("cq1", 0, 1), OP.subtract)
-    turn(v("rx", 0, 32), v("zx"))
-    for d in range(4):
-        x = (d + 1) % 4
-        cp(v("rx", 32, 64, 1, 32 * d, 32 * d + 32), v("rx", 0, 32, 1, 32 * x, 32 * x + 32), "VS")
-    cp(v("rx", 64, 128, 1, 0, 64), v("rx", 0, 64, 1, 64, 128), "VS")
-    cp(v("rx", 64, 128, 1, 64, 128), v("rx", 0, 64, 1, 0, 64), "VS")
+    run([v("zx")], [v("lt1", 0, 11), v("gol", 4, 6), v("sc1", 22, 23), v("sc1", 11, 12)], lambda e: g.vector.tensor_scalar(
+        T.zx[:, :], T.lt1[:, 0:11].indirect(T.gol[:, 4:6]), T.sc1[:, 22:23], T.sc1[:, 11:12], OP.is_ge, OP.add), "V")
+    spread("rx", "zx")
     choose(v("rk"), v("rx"), v("ofl"), v("wm"))
     scan(v("fs"), v("rk"))
     ts(v("vl1"), v("fs", 15, 128, 16), 128, OP.mult)
     f1, last = v("f1"), v("vl1")
-    run([f1], [v("w1"), last], lambda e: g.vector.tensor_copy(f1[0].bitcast(dt.uint32), v("w1")[0].bitcast(dt.uint32).indirect(last[0])),
-        {"V": by_list(f1)})
-    gather(v("yo"), v("ya"), last, "S")
-    gather(v("f1s"), v("ws1"), last, "V")
-    gather(v("pro1"), v("pa"), last, "S")
+    codes(f1, v("w1"), last)
+    gather(v("sel"), v("ya"), last, "VS")
+    gather(v("f1s"), v("ws1"), last, "VS")
+    gather(v("pro1"), v("pa"), last, "VS")
     dma("Y", "d_oc", (T.oc[:, :], (T.f1[:, :].bitcast(dt.uint8),) + f1[1:]))
-    dma("Y", "d_y", (T.y[:, :], v("yo")))
+    dma("YS", "d_y", (T.y[:, :], v("sel")))
     for k in range(4):
-        dma("Y", "d_os%d" % k, (T.osc[4 * k:4 * k + 4, :], v("f1s", 0, 128, 1, 32 * k, 32 * k + 4)))
-    dma("S", "d_p1", (T.pr[1:2, :], v("pro1", 0, 128, 1, 0, 1)))
+        dma("YS", "d_os%d" % k, (T.osc[4 * k:4 * k + 4, :], v("f1s", 0, 128, 1, 32 * k, 32 * k + 4)))
+    dma("YS", "d_p1", (T.pr[1:2, :], v("pro1", 0, 128, 1, 0, 1)))
     schedule()
     for sem, n in total.items():
         if waited.get(sem, 0) < n:

from concourse.bass import DstId, RemoteDMATransfer
from concourse.mybir import dt, AluOpType as OP, AxisListType, ActivationFunctionType as AF

F32, BF16, I32, U16, U8, C4 = "float32", "bfloat16", "int32", "uint16", "uint8", "float8_e4m3fn_x4"
SCRATCH = {"pn": ("psum", [128, 2048], F32), "pm": ("psum", [128, 2048], F32)}


def _declare(dtype, width, names):
    for n in names.split():
        SCRATCH[n] = ("sbuf", [128, width], dtype)


_declare(I32, 72, "nl")
_declare(I32, 24, "icol km")
_declare(BF16, 520, "xt wt et")
_declare(BF16, 128, "wmb wmc wmh smb posn inv invm invs kbr kbh em e0 e1 mp mu ma mb ry")
_declare(BF16, 256, "xm xs sgs")
_declare(BF16, 32, "iv n32 zy")
_declare(BF16, 16, "dt1 dsr")
_declare(F32, 80, "fcol kf")
_declare(F32, 32, "lf lft cw zx ns")
_declare(F32, 128, "mq n16 wm sm eye rk rx fs kb1 gid nbp sel pro0 pro1 prs0")
_declare(F32, 256, "npos kb")
_declare(F32, 384, "pa ya")
_declare(U16, 32, "nlu")
_declare(U16, 8, "pl swl clq pol gol idl il ofl dl")
_declare(C4, 512, "eq")
_declare(U8, 512, "es")
_declare(C4, 256, "ll")
_declare(U8, 256, "lls")
_declare(U8, 128, "hls")
_declare(C4, 128, "q0 wq f1 l1 hlc la")
_declare(U8, 128, "q0s wqs f1s l1s las")
for _c in ("v0", "b0", "b1", "s", "d"):
    _declare(BF16, 128, "qz%s qt%s qs%s" % (_c, _c, _c))
for _t in "01":
    _declare(C4, 384, "w" + _t)
    _declare(U8, 384, "ws" + _t)
    _declare(C4, 128, "g" + _t)
    _declare(U8, 128, "gs" + _t)
    _declare(F32, 8, "pen" + _t)
    _declare(F32, 16, "cq" + _t)
    _declare(F32, 16, "lt" + _t)
    _declare(F32, 32, "mx%s sc%s" % (_t, _t))
    _declare(F32, 512, "ex" + _t)
    _declare(BF16, 1024, "nt" + _t)
    _declare(U16, 8, "vl%s bl%s" % (_t, _t))
DMAS = ["d_n0", "d_n1", "d_n2", "d_n3", "d_x", "d_w", "d_nbp", "d_oc", "d_os0", "d_os1", "d_os2", "d_os3", "d_y", "d_p0", "d_p1"]
SEMAPHORES = ["cV", "cS", "cT", "cG", "sent", "arr0", "arr1", "thr0", "thr1", "thd", "hop"] + DMAS
BIG = 2.0 ** 88
ORDER = """
Y1 V27 G6 S0 V17 G7 V18 Y4 V13 V51 V25 V26 V23 Y3 V19 V30 V20 G8 V22 V60 Y2 V31 Y5 S40 V24 V69 S39 V62 G11 V21 S45 V52 S41
V55 S43 V48 S54 S44 V32 G10 V75 V73 S49 V76 V74 S47 V109 V29 G9 V77 S80 V110 S72 G12 V108 S57 V78 V70 S111 V81 V56 V197 S79
V71 V14 S82 Y198 V94 S112 S84 V116 S87 V113 S83 V85 S86 V88 S90 V89 V64 S114 V117 V92 V91 V15 V118 S115 V93 V33 V139 S96 V95
S34 V140 V121 S58 V61 S120 G106 T144 V142 V141 S122 V143 S59 V63 S50 V147 V145 V123 V67 S148 V65 V35 S146 V36 S124 S119 V155
V97 S135 V66 T171 T170 V156 S192 V125 S100 V137 V157 V37 S138 S199 G104 R105 R107 V158 V126 V16 T172 V191 V159 S160 S162 V149
S161 V193 V127 V152 S164 V150 S163 V38 S130 S131 S98 V165 S129 V68 T173 V136 V151 V166 S167 G153 R154 V99 S42 S128 S132 T176
T174 S133 T177 S180 T175 V134 S178 V194 S181 V101 S179 T187 S195 S53 T188 V182 S200 V196 G183 S169 T207 T208 T190 G185 R184
R186 V213 V257 V215 S214 V258 V168 S216 S206 V259 V217 T209 V201 V261 T212 T189 V218 V223 S224 T211 V265 S227 T210 V219 S264
V229 V263 V220 V230 V28 S266 V102 S226 G221 R222 S225 V231 V202 V234 S235 V233 S232 V242 V228 S236 S237 V260 S268 V238 V267
V103 V239 S240 V203 S241 V269 S46 V292 S254 T262 V204 T303 T294 S293 V270 T302 V275 T298 T301 V271 V305 S276 S299 V272 S306
V279 V273 S243 V304 V280 V274 S309 T295 S244 T300 G277 R278 T339 V307 V317 V310 V281 V245 S308 T337 V314 T338 S255 V282 T336
V311 V315 S284 V246 Y256 V312 V283 S316 V250 S248 V247 V249 S313 V329 S286 S285 S252 S251 V320 V288 S287 V318 V324 S323 V321
S322 V253 S319 V289 S325 V326 S297 V296 V327 S291 T334 V290 S330 T332 S328 V205 T333 T335 S346 T340 S344 V358 T341 V345 S347
T343 T342 V359 S352 V351 V363 S362 V361 S360 V354 S353 V348 S364 S365 S331 V355 V366 T356 T349 V367 S357 S350 V368 V369 S370
V372 S371 Y374 Y373 Y379 S376 Y375 S377 Y378
"""


def rank_program(g, core, T, topo):
    N, cores = len(T.cores), T.cores
    owner, first, second, third = {}, {}, {}, {}
    for c in cores:
        free_ = [h for h in topo.cores_of(c) if h not in cores and h not in owner and topo.die(h) == topo.die(c)]
        first[c] = [h for h in free_ if all(topo.may_write(h, d) for d in cores)][0]
        second[c], third[c] = [h for h in free_ if h != first[c]][:2]
        owner[first[c]] = owner[second[c]] = owner[third[c]] = c
    me = owner.get(core, core)
    r = T.rank_of(me)
    if r is None:
        return

    peers = [(d, cores[r ^ d]) for d in range(1, N)]
    chip = topo.cores_of(core)
    far = [(d, c) for d, c in peers if c not in chip]
    near = [(d, c) for d, c in peers if c in chip]
    plane = [(d, c) for d, c in far if topo.may_write(second[me], c) and topo.may_write(third[me], c)]
    rest = [x for x in far if x not in plane]
    lanes = topo.engines(me, far[0][1])
    spare = 2 * len(far) - len(lanes)
    others = [e for e in topo.engines(core, near[0][1]) if e not in lanes]
    inside = others[:2]
    ways = []
    for part in range(2):
        mine = lanes[spare:] + lanes[:spare] if part else lanes
        way = {d: inside for d, c in near}
        for k, (d, c) in enumerate(far):
            way[d] = [mine[k]] if k < spare else [mine[spare + 2 * (k - spare)], mine[spare + 2 * (k - spare) + 1]]
        ways.append(way)

    def even(who, with_near):
        n = len(lanes) // len(who)
        way = {d: lanes[n * k:n * k + n] for k, (d, c) in enumerate(who)}
        if with_near:
            way.update({d: inside for d, c in near})
        return way

    def engines(way):
        return sum(len(x) for x in way.values())

    def bits(es):
        return sum(1 << e for e in es)

    def dest(c):
        rid, pid = topo.addr(c, core)
        return DstId(rid=rid, pnc=pid)

    def blocks(way, name, c0, dst, d0, sem, n=16):
        tr = []
        for d, es in way.items():
            a, b = T[name][:, c0 + n * d:c0 + n * d + n], T[dst][:, d0 + n * d:d0 + n * d + n]
            if SCRATCH[name][2] == C4:
                a, b = a.bitcast(dt.uint8), b.bitcast(dt.uint8)
            tr.append(RemoteDMATransfer(dst_ids=[dest(cores[r ^ d])], dma_engine_mask=bits(es), remote_sem=T.sem[sem], src=a, dst=b))
        return tr

    half = len(others) // 2
    if core != me:
        way, src, dst = {first[me]: (even(rest, True), "hls", "lls"), second[me]: (even(plane, False), "hlc", "ll"),
                         third[me]: (even(plane, False), "hls", "lls")}[core]
        g.wait_ge(T.sem.hop, half)
        g.remote_dma_fused(blocks(way, src, 0, dst, 128, "arr1"), local_sem=T.sem.sent)
        g.wait_ge(T.sem.sent, engines(way))
        return

    queue = {"V": g.vector, "S": g.scalar, "T": g.tensor, "G": g, "Y": g.sync}
    count = {e: 0 for e in "VSTG"}
    known = {e: {} for e in "VSTGY"}
    snap, hist, waited, total = {}, {}, {}, {}

    def v(name, c0=0, c1=None, st=1, p0=0, p1=128):
        c1 = SCRATCH[name][1][1] if c1 is None else c1
        ap = T[name][p0:p1, c0:c1] if st == 1 else T[name][p0:p1, c0:c1:st]
        if SCRATCH[name][0] == "psum":
            return (ap, name, 0, 128, c0 // 512 * 512, (c1 + 511) // 512 * 512, 1, c1 - c0)
        return (ap, name, p0, p1, c0, c1, st, (c1 - c0 + st - 1) // st)

    def meet(a, b):
        if a[3] <= b[2] or b[3] <= a[2] or a[5] <= b[4] or b[5] <= a[4]:
            return False
        return not (a[6] == b[6] and a[6] > 1 and (a[4] - b[4]) % a[6])

    def need(e, tok):
        sem, val = tok
        if known[e].get(sem, 0) < val:
            queue[e].wait_ge(T.sem[sem], val)
            waited[sem] = max(waited.get(sem, 0), val)
            for s, n in list(snap.get(tok, {}).items()) + [(sem, val)]:
                known[e][s] = max(known[e].get(s, 0), n)

    def order(e, outs, ins):
        toks = {}
        for x in ins:
            psum = SCRATCH[x[1]][0] == "psum"
            for (y, tok, w, f) in hist.get(x[1], []):
                if (w or (psum and f != e)) and meet(x, y):
                    toks[tok[0]] = max(toks.get(tok[0], 0), tok[1])
        for x in outs:
            for (y, tok, w, f) in hist.get(x[1], []):
                if (f != e or e != "T") and meet(x, y):
                    toks[tok[0]] = max(toks.get(tok[0], 0), tok[1])
        for s in sorted(toks, key=lambda s: s == "c" + e):
            need(e, (s, toks[s]))

    def note(e, outs, ins, tok):
        for x in outs:
            hist.setdefault(x[1], []).append((x, tok, True, e))
        for x in ins:
            hist.setdefault(x[1], []).append((x, tok, False, e))

    ops, seen = [], {}

    def views(xs):
        return [x for x in xs if isinstance(x, tuple)]

    def add(outs, ins, emit, e, after=()):
        outs, ins = views(outs), views(ins)
        i, deps = len(ops), set(after)
        for x in ins:
            psum = SCRATCH[x[1]][0] == "psum"
            deps.update(j for y, j, w, f in seen.get(x[1], []) if (w or (psum and f != e)) and meet(x, y))
        for x in outs:
            deps.update(j for y, j, w, f in seen.get(x[1], []) if meet(x, y))
        for x in outs:
            seen.setdefault(x[1], []).append((x, i, True, e))
        for x in ins:
            seen.setdefault(x[1], []).append((x, i, False, e))
        ops.append((emit, e, 0, sorted(deps)))
        return i

    def run(outs, ins, call, es):
        outs, ins = views(outs), views(ins)

        def emit(e):
            order(e, outs, ins)
            count[e] += 1
            tok = ("c" + e, count[e])
            call(e).then_inc(T.sem[tok[0]], 1)
            total[tok[0]] = count[e]
            snap[tok] = dict(known[e])
            note(e, outs, ins, tok)
        return add(outs, ins, emit, es)

    def schedule():
        when = [(0, 0, x[0], int(x[1:])) for x in ORDER.split()]
        done = set()
        for s, k, e, i in when:
            assert e in ops[i][1] and done.issuperset(ops[i][3])
            done.add(i)
            if e != "R":
                ops[i][0](e)
        assert len(done) == len(ops)

    def val(x):
        return x[0] if isinstance(x, tuple) else x

    def dma(es, sem, *moves):
        outs, ins = views([x for x, y in moves]), views([y for x, y in moves])

        def emit(e):
            for out, in_ in moves:
                order(e, views([out]), views([in_]))
                queue[e].dma_start(val(out), val(in_)).then_inc(T.sem[sem], 16)
            total[sem] = 16 * len(moves)
            snap[(sem, total[sem])] = dict(known[e])
            note("D" + sem, outs, ins, (sem, total[sem]))
        add(outs, ins, emit, es)

    def ts(out, a, s1, op0, s2=None, op1=None):
        plain = all(SCRATCH[x[1]][2] in (F32, BF16) for x in (out, a)) and all(SCRATCH[x[1]][2] == F32 for x in views([s1, s2]))
        either = plain and (op0, op1) in ((OP.mult, None), (OP.add, None), (OP.mult, OP.add))
        b, c = (1.0, s1) if op0 == OP.add else (s1, 0.0 if op1 is None else s2)

        def call(e):
            if e == "S":
                return g.scalar.activation(out[0], a[0], AF.Identity, bias=c[0] if isinstance(c, tuple) else float(c),
                                           scale=b[0] if isinstance(b, tuple) else float(b))
            if op1 is None:
                return g.vector.tensor_scalar(out[0], a[0], val(s1), None, op0)
            return g.vector.tensor_scalar(out[0], a[0], val(s1), val(s2), op0, op1)
        run([out], [a, s1, s2], call, "VS" if either else "V")

    def tt(out, a, b, op):
        run([out], [a, b], lambda e: g.vector.tensor_tensor(out[0], a[0], b[0], op), "V")

    def act(out, a, func, scale=1.0, bias=0.0, acc=None):
        if acc is None:
            run([out], [a, bias, scale], lambda e: g.scalar.activation(out[0], a[0], func, bias=val(bias), scale=val(scale)), "S")
        else:
            run([out, acc], [a, bias], lambda e: g.scalar.activation(out[0], a[0], func, bias=val(bias), scale=scale, accum_out=acc[0]), "S")

    def cp(out, a, es="V"):
        def call(e):
            if e == "V":
                return g.vector.tensor_copy(out[0], a[0])
            return g.scalar.activation(out[0], a[0], AF.Copy)
        run([out], [a], call, es)

    def fill(out, c):
        run([out], [], lambda e: g.vector.memset(out[0], c), "V")

    def red(out, a, op):
        if op == OP.add:
            run([out, a], [a], lambda e: g.vector.tensor_reduce(out[0], a[0], AxisListType.X, op) if e == "V" else
                g.scalar.activation(a[0], a[0], AF.Copy, accum_out=out[0]), "VS")
        else:
            run([out], [a], lambda e: g.vector.tensor_reduce(out[0], a[0], AxisListType.X, op), "V")

    def turn(out, a):
        run([out], [a], lambda e: g.vector.transpose(out[0], a[0]), "V")

    def scan(z, q, op=OP.add):
        s = v("smb" if SCRATCH[q[1]][2] == BF16 else "sm", 0, q[7])
        run([z], [q, s], lambda e: g.vector.tensor_tensor_scan(z[0], s[0], q[0], 0.0, OP.mult, op), "V")

    def quant(q, s, a):
        run([q, s], [a], lambda e: g.vector.quantize_mx(q[0], s[0], a[0]), "V")

    def mm(out, a, asc, b, bsc, start=True, stop=True):
        run([out], [a, asc, b, bsc], lambda e: g.tensor.matmul_mx(out[0], a[0], asc[0], b[0], bsc[0], start, stop), "T")

    def gather(out, win, off, es="SV"):
        def call(e):
            if e == "V":
                return g.vector.tensor_copy(out[0], win[0].indirect(off[0]))
            return g.scalar.activation(out[0], win[0].indirect(off[0]), AF.Copy)
        run([out], [win, off], call, es)

    def choose(out, win, off, m, op=OP.mult):
        run([out], [win, off, m], lambda e: g.vector.tensor_tensor(out[0], win[0].indirect(off[0]), m[0], op), "V")

    def under(out, win, off, a, b):
        run([out], [win, off, a, b], lambda e: g.vector.tensor_scalar(out[0], win[0].indirect(off[0]), a[0], b[0], OP.max, OP.is_lt), "V")

    def listed(out, win, off, a, b):
        run([out], [win, off, a, b], lambda e: g.vector.tensor_scalar(out[0], win[0].indirect(off[0]), val(a), val(b), OP.mult, OP.add) if e == "V"
            else g.scalar.activation(out[0], win[0].indirect(off[0]), AF.Identity, bias=val(b), scale=val(a)), "VS")

    def codes(o, w, off):
        run([o], [w, off], lambda e: g.vector.tensor_copy(o[0].bitcast(dt.uint32), w[0].bitcast(dt.uint32).indirect(off[0])), "V")

    def pick(oq, os, oa, ob, iq, isc, ia, ib, off):
        codes(v(oq, oa, ob), v(iq, ia, ib), off)
        gather(v(os, oa, ob), v(isc, ia, ib), off)

    def iota(out, pattern, base, cm, flag=True):
        run([out], [], lambda e: g.iota(out[0], pattern, base, cm, allow_small_or_imprecise_dtypes=True) if flag else g.iota(out[0], pattern, base, cm), "G")

    def wrap(tag, raised, a, b, op, out, *last):
        name = "qs" + tag
        if b is None:
            ts(v("qz" + tag), v(raised), a, OP.mult)
        else:
            ts(v("qz" + tag), v(raised), a, OP.add, b, op)
        turn(v("qt" + tag), v("qz" + tag))
        scan(v(name), v("qt" + tag), OP.max)
        for d in range(4):
            x = d ^ 1
            cp(v(name, 32 * x + 15, 32 * x + 32, 16, 32 * d, 32 * d + 32), v(name, 32 * x + 15, 32 * x + 32, 16, 32 * x, 32 * x + 32), "VS")
        cp(v(name, 79, 128, 16, 0, 64), v(name, 79, 128, 16, 64, 128), "VS")
        cp(v(name, 15, 64, 16, 64, 128), v(name, 15, 64, 16, 0, 64), "VS")
        ts(out, v(name, 15, 128, 16), *last)

    def ic(k):
        return v("icol", k, k + 1)

    def fc(k):
        return v("fcol", k, k + 1)

    def km(k):
        return v("km", 8 * k, 8 * k + 8, 1, 0, 32)

    classes = ((2, 0, 5), (1, 5, 5), (0, 10, 6))
    for k, by in ((2, 0), (0, 6), (1, 11)):
        moves = []
        for h in range(2):
            for i, s, n in classes:
                p, c = 16 * h + (s + by) % 16, (k - i) % 3
                moves.append((v("nl", 24 * k, 24 * k + 22, 1, p, p + n), T.nb[i:16:3, c:c + 22]))
        if k == 2:
            dma("S", "d_n3", *moves[:3])
            dma("Y", "d_n2", *moves[3:])
            dma("Y", "d_x", (v("xt", 0, 512), T.x[:, :]))
        else:
            dma("Y", "d_n%d" % k, *moves)
    dma("Y", "d_w", (v("wt", 0, 512), T.w[:, :]))

    iota(ic(0), [[0, 1]], 0, 1, False)
    iota(v("kb"), [[1, 256]], 0, 0)
    iota(v("n16"), [[0, 8], [1, 16]], 0, 0)
    iota(v("kbh"), [[1, 128]], 0, 0)
    iota(v("kb1"), [[1, 128]], 1, 0)
    iota(v("nbp"), [[0, 128]], 0, 0)
    iota(v("pa", 128, 256), [[0, 128]], -1, 0)
    fill(v("et", 0, 260), 0.0)
    fill(v("et", 260, 520), 0.0)
    fill(v("dt1", 0, 8), 1.0)
    fill(v("posn"), 0.0)
    fill(v("ry"), 0.0)
    fill(v("fcol", 48, 64), 0.0)
    for d in range(N):
        fill(v("fcol", 48 + 8 * (d % 2) + (d ^ r), 49 + 8 * (d % 2) + (d ^ r), 1, 32 * (d // 2), 32 * (d // 2) + 32), 1.0)
    for t in "01":
        fill(v("lt" + t, 0, 4), 0.0)
    cp(fc(0), ic(0))
    ts(ic(3), ic(0), 15, OP.bitwise_and)
    cp(fc(2), ic(3))
    ts(fc(6), ic(3), 0.5, OP.add)
    ts(v("eye"), v("kb", 0, 128), fc(0), OP.is_equal)
    act(v("et", 4, 516, 4), v("eye"), AF.Copy, 0.5)
    units = [(v("eq", 128 * b, 128 * b + 128), v("es", 128 * b, 128 * b + 128)) for b in range(4)]
    for b in range(4):
        quant(units[b][0], units[b][1], v("et", 4 - b, 516 - b))
    for d in range(4):
        cp(v("kbr", 0, 128 - 32 * d, 1, 32 * d, 32 * d + 32), v("kb", 32 * d, 128, 1, 32 * d, 32 * d + 32), "VS")
        if d:
            cp(v("kbr", 128 - 32 * d, 128, 1, 32 * d, 32 * d + 32), v("kb", 0, 32 * d, 1, 32 * d, 32 * d + 32), "VS")
    act(v("sm"), v("n16"), AF.Sign)
    act(v("smb"), v("n16"), AF.Sign)
    ts(v("wm"), v("n16"), fc(2), OP.is_equal)
    act(v("wmh"), v("wm"), AF.Copy)
    act(v("wmb"), v("wm"), AF.Copy, 128.0)
    ts(ic(5), ic(0), 4, OP.arith_shift_right)
    ts(fc(15), ic(5), 0.125, OP.mult, 5, OP.add)
    act(v("wmc"), v("wm"), AF.Copy, fc(15))
    ts(fc(17), fc(2), -512, OP.add)
    ts(ic(6), ic(0), 5, OP.arith_shift_right)
    ts(fc(14), ic(6), -32, OP.mult, 128, OP.add)
    ts(fc(18), fc(0), 1.0 / 16384, OP.mult)
    ts(fc(7), fc(14), -1, OP.mult, 128, OP.add)
    ts(v("cw"), v("kb", 0, 32), fc(7), OP.add)
    ts(fc(32), ic(5), 0, OP.is_gt, 3, OP.mult)
    ts(v("gol", 0, 1), ic(5), fc(32), OP.add)
    ts(fc(35), ic(5), fc(32), OP.add)
    ts(v("gol", 4, 6), v("kb", 0, 2), 0, OP.mult, fc(35), OP.add)
    ts(fc(33), ic(5), 0, OP.is_gt, 7, OP.mult)
    ts(fc(34), ic(5), fc(33), OP.add)
    ts(v("gol", 2, 4), v("kb", 0, 2), 0, OP.mult, fc(34), OP.add)
    ts(fc(9), ic(5), 16, OP.mult)
    ts(v("idl"), v("kb", 0, 8), 16, OP.mult, fc(2), OP.add)
    ts(ic(4), ic(0), 4, OP.arith_shift_right, 1, OP.bitwise_and)
    cp(fc(8), ic(4))
    ts(v("fcol", 10, 12), v("kb", 0, 2), fc(8), OP.is_equal)
    ts(v("fcol", 12, 14), v("kb", 0, 256, 128), 2, OP.mult, 128, OP.add)

    ends = v("nl", 48, 72, 3, 0, 32)
    for q in range(4):
        ts(v("clq", 0, 8, 1, 32 * q, 32 * q + 32), ends, 1.0 / 128, OP.mult, -63.5 / 128, OP.add)
    for h in range(2):
        m, c = v("xm", 128 * h, 128 * h + 128), v("xs", 128 * h, 128 * h + 128)
        gather(m, v("fcol", 48 + 8 * h, 56 + 8 * h), v("clq"))
        run([c], [m], lambda e, m=m, c=c: g.vector.tensor_tensor_scan(c[0], m[0], m[0], 0.0, OP.add, OP.max), "V")
        act(v("sgs", 128 * h, 128 * h + 128), c, AF.Sign, -1.0, fc(6), v("kf", 64 + h, 65 + h))
    for a in range(4):
        for b in (a, a ^ 1):
            cp(v("kf", 72 + 2 * a, 74 + 2 * a, 1, 32 * b, 32 * b + 32), v("kf", 64, 66, 1, 32 * a, 32 * a + 32), "VS")
    cp(v("kf", 76, 80, 1, 0, 64), v("kf", 76, 80, 1, 64, 128), "VS")
    cp(v("kf", 72, 76, 1, 64, 128), v("kf", 72, 76, 1, 0, 64), "VS")
    ts(v("pl", 0, 8), v("kf", 72, 80), 128, OP.add, 0.5, OP.mult)
    quant(v("q0"), v("q0s"), v("xt", 0, 512))
    pick("w0", "ws0", 128, 256, "q0", "q0s", 0, 128, v("pl", 0, 8))
    pick("ll", "lls", 0, 16, "q0", "q0s", 0, 128, v("pl", 0, 1))
    run([v("posn")], [v("kb", 0, 128), v("pl", 0, 8)],
        lambda e: g.vector.tensor_copy(T.posn[:, 0:128].indirect(T.pl[:, 0:8]), T.kb[:, 0:128]), "V")
    gather(v("inv"), v("kb", 0, 128), v("pl", 0, 8))
    choose(v("invm"), v("posn"), v("idl"), v("wmh", 0, 128))
    scan(v("invs"), v("invm"))
    cp(v("pol"), v("invs", 15, 128, 16))

    def post(srcs, tr, leave, land=None):
        def emit(e):
            order("G", [], srcs)
            g.remote_dma_fused(tr, local_sem=T.sem.sent)
            total["sent"] = total.get("sent", 0) + leave
        i = add([], srcs, emit, "G")
        if land is not None:
            add([land], [], None, "R", (i,))

    def send_col(name, c0, dst, d0, sem):
        tr = []
        for who, es in ((far, lanes), (near, inside)):
            tr.append(RemoteDMATransfer(dst_ids=[dest(c) for d, c in who], dma_engine_mask=bits(es), remote_sem=T.sem[sem],
                                        srcs=[T[name][:, c0:c0 + 1]], dsts=[T[dst][:, d0 + d:d0 + d + 1] for d, c in who]))
        post([v(name, c0, c0 + 1)], tr, len(lanes) + len(inside), v(dst, d0 + 1, d0 + 8))

    def send_merged():
        a, b = 16 * plane[0][0], 16 * plane[-1][0] + 16
        tr = [RemoteDMATransfer(dst_ids=[dest(first[core]), dest(third[core])], dma_engine_mask=bits(others[:half]), remote_sem=T.sem.hop,
                                srcs=[T.ws0[:, 256:256 + 4 * (b - a)]], dsts=[T.hls[:, 0:4 * (b - a)]] * 2),
              RemoteDMATransfer(dst_ids=[dest(second[core])], dma_engine_mask=bits(others[half:]), remote_sem=T.sem.hop,
                                src=T.w0[:, 256 + a:256 + b].bitcast(dt.uint8), dst=T.hlc[:, a:b].bitcast(dt.uint8))]
        post([v("ws0", 256, 384), v("w0", 256, 384)], tr, len(others), v("lls", 144, 256))
        post([v("w0", 256, 384)], blocks(even(rest, True), "w0", 256, "ll", 128, "arr1"), engines(even(rest, True)), v("ll", 144, 256))

    few = len(far) * len(lanes) + len(near) * len(inside)
    total["arr0"] = engines(ways[0]) + engines(ways[1])
    total["arr1"] = 2 * engines(even(rest, True)) + 2 * engines(even(plane, False))
    total["thr0"] = total["thr1"] = total["thd"] = few
    for t in range(2):
        note("R", [v("ll", 128 * t + 16, 128 * t + 128), v("lls", 128 * t + 16, 128 * t + 128)], [], ("arr%d" % t, total["arr%d" % t]))
        note("R", [v("lt%d" % t, 4, 11)], [], ("thr%d" % t, few))
    note("R", [v("dt1", 8, 15)], [], ("thd", few))

    def bank(k, n=128):
        return v("pn" if k < 4 else "pm", 512 * (k % 4), 512 * (k % 4) + n)

    def score(t, k, b, m, bias=None):
        x, out = v("ex" + t, 128 * k, 128 * k + 128), v("sc" + t, k, k + 1)
        tt(x, bank(b), v(m, 0, 128), OP.mult)
        if bias is None:
            act(x, x, AF.Copy, acc=out)
        else:
            act(x, x, AF.Identity, bias=bias, acc=out)

    def spread(row, col):
        turn(v(row, 0, 32), v(col))
        for d in range(4):
            x = (d + 1) % 4
            cp(v(row, 32, 64, 1, 32 * d, 32 * d + 32), v(row, 0, 32, 1, 32 * x, 32 * x + 32), "VS")
        cp(v(row, 64, 128, 1, 0, 64), v(row, 0, 64, 1, 64, 128), "VS")
        cp(v(row, 64, 128, 1, 64, 128), v(row, 0, 64, 1, 0, 64), "VS")

    def across(out, a, b):
        ts(v("mq", 64, 96), v("mx0"), a, OP.max, b, OP.max)
        turn(v("mq", 96, 128), v("mq", 64, 96))
        red(out, v("mq", 96, 128), OP.min)

    def halves(m, s, banks, start):
        for b in range(4):
            mm(bank(banks[b]), units[b][0], units[b][1], m, s, start, not start)

    def drain(t, k, banks):
        for b in range(4):
            cp(v("nt" + t, 512 * k + b, 512 * k + 512, 4), bank(banks[b]), "VS")

    def requant(t, k):
        quant(v("w" + t, 256 * k, 256 * k + 128), v("ws" + t, 256 * k, 256 * k + 128), v("nt" + t, 512 * k, 512 * k + 512))

    def with_w(k, a):
        mm(bank(k), v("wq"), v("wqs"), v("w1", a, a + 128), v("ws1", a, a + 128))
        cp(v("ya", a, a + 128), bank(k), "VS")

    n0, n1 = v("ns", 15, 16), v("ns", 31, 32)
    low4, mixed = (0, 1, 2, 3), (7, 6, 4, 5)
    for t in "01":
        W, WS = v("w" + t, 128, 256), v("ws" + t, 128, 256)
        G, GS = v("g" + t), v("gs" + t)
        L, LS = (v("la"), v("las")) if t == "0" else (v("l1"), v("l1s"))

        def s_(a):
            return v("sc" + t, a, a + 1)

        def pen(a):
            return v("pen" + t, a, a + 1)

        best = v("mq", 32 * int(t), 32 * int(t) + 1)
        if t == "0":
            post([W], blocks(ways[0], "w0", 128, "ll", 0, "arr0"), engines(ways[0]), v("ll", 16, 128))
            post([WS], blocks(ways[1], "ws0", 128, "lls", 0, "arr0"), engines(ways[1]), v("lls", 16, 128))
            ts(v("lf", 0, 24, 1, 0, 32), v("nl", 0, 72, 3, 0, 32), 0, OP.add)
            ts(km(2), ends, 127, OP.bitwise_and)
            ts(v("lf", 24, 32, 1, 0, 32), km(2), 128 * r, OP.add)
            cp(v("lf", 0, 32, 1, 32, 64), v("lf", 0, 32, 1, 0, 32), "S")
            cp(v("lf", 0, 32, 1, 64, 128), v("lf", 0, 32, 1, 0, 64), "S")
            ts(v("nlu"), v("lf"), -128 * r, OP.add)
            gather(v("npos"), v("kb", 0, 128), v("nlu", 0, 16))
            gather(v("rk"), v("kb", 0, 128), v("nlu", 24, 32))
            tt(v("kf", 66, 68), v("kf", 64, 66), v("fcol", 10, 12), OP.mult)
            red(fc(40), v("kf", 66, 68), OP.add)
            ts(v("il", 0, 2), v("fcol", 12, 14), fc(40), OP.add, 0.5, OP.mult)
            ts(fc(1), fc(40), 0.5, OP.mult, 65, OP.add)
            gather(v("mq", 40, 56), v("rk"), v("il", 0, 1))
            choose(v("iv", 16, 32), v("rk"), v("il", 0, 1), v("wmh", 0, 16))
            red(fc(46), v("iv", 16, 32), OP.add)
            ts(v("iv", 0, 16), v("mq", 40, 56), fc(46), OP.is_lt)
            red(fc(47), v("iv", 0, 16), OP.add)
            wrap("s", "wmb", fc(47), fc(9), OP.add, v("swl"), -128, OP.add)
            ts(fc(45), fc(47), fc(9), OP.add)
            ts(v("em"), v("kbh"), fc(45), OP.is_equal)
            ts(v("mx1"), v("cw"), fc(9), OP.subtract, fc(47), OP.not_equal)
            ts(v("mx0"), v("mx1"), 2 * BIG, OP.mult, -BIG, OP.add)
            choose(v("n32"), v("npos"), v("il", 0, 2), v("wmh", 0, 32))
        else:
            cp(v("il", 2, 4), v("ns", 15, 32, 16))
            choose(v("n32"), v("posn"), v("il", 2, 4), v("wmh", 0, 32))
        scan(v("ns"), v("n32"))
        ts(v("e0"), v("kbh", 0, 128), n0, OP.is_equal)
        if t == "0":
            ts(v("e1"), v("kbh", 0, 128), n1, OP.is_equal)
        ts(fc(41), n1, n0, OP.subtract)
        own = ("q0", "q0s", 0, 128) if t == "0" else ("w1", "ws1", 128, 256)
        mm(bank(4), W, WS, v(own[0], *own[2:]), v(own[1], *own[2:]))
        if t == "0":
            score(t, 0, 4, "e0")
            score(t, 1, 4, "e1")
            across(v("lt0", 0, 1), s_(0), s_(1))
            tt(best, s_(0), s_(1), OP.max)
        else:
            ts(fc(42), n0, n1, OP.add, -0.5, OP.mult)
            act(fc(43), fc(41), AF.Abs, 0.5)
            ts(fc(44), v("sc0", 10, 11), -0.5, OP.add, fc(41), OP.mult)
            ts(fc(36), v("sc0", 11, 12), fc(44), OP.mult, fc(42), OP.add)
            ts(fc(37), v("sc0", 11, 12), 0.5, OP.is_lt, fc(43), OP.mult)
            act(v("fs"), v("kb", 0, 128), AF.Abs, 1.0, fc(36))
            ts(v("rk"), v("fs"), fc(37), OP.not_equal, -BIG, OP.mult)
            tt(v("ex1", 128, 256), bank(4), v("rk"), OP.add)
            red(best, v("ex1", 128, 256), OP.max)
            across(v("lt1", 0, 1), best, best)
            score(t, 0, 4, "e0", pen(0))
        send_col("lt" + t, 0, "lt" + t, 3, "thr" + t)
        ts(s_(8), best if t == "1" else s_(1), s_(0), OP.is_gt, fc(41), OP.mult)
        wrap("b" + t, "wmb", s_(8), n0, OP.add, v("bl" + t), -128, OP.add)
        pick("g" + t, "gs" + t, 0, 128, *own, v("bl" + t))
        if t == "0":
            pick("la", "las", 0, 128, "ll", "lls", 0, 128, v("swl"))
            halves(W, WS, low4, True)
            halves(G, GS, low4, False)
            drain(t, 1, low4)
            requant(t, 1)
            send_merged()
            halves(W, WS, low4, True)
        else:
            pick("ll", "lls", 128, 144, "w1", "ws1", 128, 256, v("idl", 0, 1))
            mm(bank(5), W, WS, v("ll", 0, 128), v("lls", 0, 128))
            mm(bank(6), W, WS, v("ll", 128, 256), v("lls", 128, 256))
            pick("l1", "l1s", 0, 128, "ll", "lls", 0, 256, v("dl"))
            with_w(7, 128)
            halves(W, WS, low4, True)
        ts(s_(10), best if t == "1" else s_(1), s_(0), OP.is_gt)
        if t == "0":
            ts(s_(9), s_(8), n0, OP.add)
            ts(v("mp"), v("inv"), s_(9), OP.is_equal, fc(1), OP.mult)
            choose(v("mu"), v("kb1"), v("bl0"), v("mp"), OP.is_equal)
            act(v("sel"), v("mu"), AF.Identity, -BIG, BIG / 128, pen(3))
            run([v("ry")], [v("mu"), v("swl")], lambda e: g.vector.tensor_copy(T.ry[:, 0:128].indirect(T.swl[:, 0:8]), T.mu[:, 0:128]), "V")
        else:
            score(t, 2, 5, "em", pen(2))
            score(t, 3, 6, "em", pen(2))
            ts(v("sc1", 12, 14), v("kb", 1, 3), s_(10), OP.add)
            ts(s_(15), s_(2), best, OP.is_le, s_(12), OP.mult)
            ts(s_(16), s_(3), best, OP.is_le, s_(12), OP.mult)
            ts(s_(17), s_(16), s_(15), OP.subtract)
            listed(v("zy"), v("dt1", 0, 15), v("gol", 2, 4), s_(17), s_(15))
            ts(s_(18), v("mq", 8, 9), 128, OP.is_lt, s_(2), OP.mult)
            ts(s_(19), v("mq", 8, 9), 128, OP.is_ge, s_(3), OP.mult)
            ts(s_(20), s_(18), s_(19), OP.add)
            ts(v("ma"), v("kbr"), n0, OP.subtract, s_(8), OP.is_equal)
            ts(s_(14), v("zy", 0, 1), 0, OP.is_gt, s_(13), OP.mult)
            ts(v("mb"), v("ma"), s_(14), OP.mult, -1, OP.add)
            spread("ry", "zy")
            choose(v("mp"), v("ry"), v("idl"), v("mb"), OP.is_equal)
            act(v("sel"), v("mp"), AF.Identity, 1.0, fc(18), s_(11))
            ts(s_(21), s_(20), best, OP.is_le, -4 * BIG, OP.mult)
            ts(s_(22), s_(21), s_(20), OP.add)
        if t == "0":
            turn(v("lft", 0, 32, 1, 0, 32), v("lf", 0, 32, 1, 0, 32))
            dma("Y", "d_nbp", (v("nbp", 0, 128, 1, 0, 1), v("lft", 0, 16, 1, 16, 24)))
            gather(v("pa", 0, 128), v("nbp"), v("pl", 0, 8))
            act(v("gid"), v("inv"), AF.Identity, 1.0, float(128 * r))
            ts(v("sc0", 12, 14), v("kb", 0, 2), s_(10), OP.is_equal, -BIG, OP.mult)
            quant(v("wq"), v("wqs"), v("wt", 0, 512))
            ts(v("km", 0, 8), v("pol"), fc(14), OP.add)
            ts(v("km", 8, 16), v("km", 0, 8), 127, OP.bitwise_and)
            cp(v("ofl"), v("km", 8, 16))
            run([v("pa", 256, 384)], [v("kb1"), v("bl0")], lambda e: g.scalar.activation(
                T.pa[:, 256:384], T.kb1[:, 0:128].indirect(T.bl0[:, 0:8]), AF.Identity, bias=float(128 * r - 1)), "S")
        else:
            gather(v("pa", 256, 384), v("gid"), v("bl1"))
        if t == "0":
            mm(bank(5), W, WS, v("ll", 0, 128), v("lls", 0, 128))
            mm(bank(6), G, GS, v("ll", 0, 128), v("lls", 0, 128))
            halves(L, LS, low4, False)
            score(t, 2, 5, "em")
            score(t, 3, 6, "ry", pen(3))
            ts(s_(11), s_(2), s_(3), OP.max, best, OP.is_le)
            across(v("dsr", 0, 1), s_(11), s_(11))
            send_col("dsr", 0, "dt1", 7, "thd")
        else:
            halves(L, LS, low4, False)
        if t == "0":
            under(v("cq0"), v("lt0", 0, 11), v("gol", 0, 1), best, s_(2))
        else:
            halves(W, WS, mixed, True)
            halves(G, GS, mixed, False)
        drain(t, 0, low4)
        requant(t, 0)
        if t == "0":
            wrap("v0", "wmc", s_(11), v("cq0", 0, 1), OP.subtract, v("vl0"), 128, OP.mult, fc(17), OP.add)
            pick("w1", "ws1", 128, 256, "w0", "ws0", 0, 384, v("vl0"))
            ts(v("pen1", 0, 2), v("sc0", 12, 14), s_(11), OP.mult)
            ts(v("pen1", 2, 3), v("cq0", 0, 1), -BIG, OP.mult)
            listed(v("mq", 8, 24), v("dt1", 0, 15), v("gol", 2, 3), 128.0, fc(45))
            wrap("d", "wmh", v("mq", 8, 9), None, None, v("dl"), 0, OP.add)
            gather(v("prs0"), v("pa"), v("vl0"))
            gather(v("pro0"), v("prs0"), v("pol"))
            dma("Y", "d_p0", (T.pr[0:1, :], v("pro0", 0, 128, 1, 0, 1)))

    with_w(0, 0)
    drain("1", 1, mixed)
    requant("1", 1)
    with_w(7, 256)
    run([v("zx")], [v("lt1", 0, 11), v("gol", 4, 6), v("sc1", 22, 23), v("sc1", 11, 12)], lambda e: g.vector.tensor_scalar(
        T.zx[:, :], T.lt1[:, 0:11].indirect(T.gol[:, 4:6]), T.sc1[:, 22:23], T.sc1[:, 11:12], OP.is_ge, OP.add), "V")
    spread("rx", "zx")
    choose(v("rk"), v("rx"), v("ofl"), v("wm"))
    scan(v("fs"), v("rk"))
    ts(v("vl1"), v("fs", 15, 128, 16), 128, OP.mult)
    f1, last = v("f1"), v("vl1")
    codes(f1, v("w1"), last)
    gather(v("sel"), v("ya"), last, "VS")
    gather(v("f1s"), v("ws1"), last, "VS")
    gather(v("pro1"), v("pa"), last, "VS")
    dma("Y", "d_oc", (T.oc[:, :], (T.f1[:, :].bitcast(dt.uint8),) + f1[1:]))
    dma("YS", "d_y", (T.y[:, :], v("sel")))
    for k in range(4):
        dma("YS", "d_os%d" % k, (T.osc[4 * k:4 * k + 4, :], v("f1s", 0, 128, 1, 32 * k, 32 * k + 4)))
    dma("YS", "d_p1", (T.pr[1:2, :], v("pro1", 0, 128, 1, 0, 1)))
    schedule()
    for sem, n in total.items():
        if waited.get(sem, 0) < n:
            (g if sem == "sent" else g.sync).wait_ge(T.sem[sem], n)
